import numpy as np, ml_dtypes
CORES = [35,38,43,46]
N = 4
BF = ml_dtypes.bfloat16
def gentries(a):
    return np.ascontiguousarray(a.reshape(8, 16, -1).transpose(0, 2, 1)).reshape(8, -1)
def gtable(e):
    e = np.asarray(e); return np.ascontiguousarray(e.reshape(8, -1, 16).transpose(0, 2, 1)).reshape(128, -1).astype(np.int32)
W, L, B, VI, PS, ST = 4096, 16, 256, 4, 1, 16
KAP = 241 * np.arange(L) + 37
def tables_of(rng):
    lv = rng.random((N, 8, 16, W), dtype=np.float32); x = rng.integers(0, 16, (N, 8, 16, W))
    h = rng.choice(np.array([0.15, 0.22, 0.3]), (N, 8, 1, 1)); w = rng.choice(np.array([0.12, 0.18]), (N, 8, 1, 1))
    e = np.where(lv < h, 12 + (x & 3), np.where(lv < h + w, x & 3, 4 + (x & 7)))
    nd = rng.choice(np.array([0.0, 0.05, 0.1, 0.2]), (N, 8, 1, W)); x = rng.integers(0, 12, (N, 8, 16, W))
    return e, np.where(rng.random((N, 8, 16, W), dtype=np.float32) < nd, 12 + (x & 3), x)
def own_steps(rng, s):
    return np.take_along_axis(s, rng.integers(0, L, (N, 8, L, B)), axis=2)
def pack(e, p, s, q, st, th):
    return {"eff": e.reshape(N, 128, W).astype(np.float32).astype(BF), "req": p.reshape(N, 128, W).astype(np.float32).astype(BF),
            "act": np.stack([gtable(a.reshape(8, L * B)) for a in s]), "why": np.stack([gtable(a.reshape(8, L * B)) for a in q]),
            "st0": np.ascontiguousarray(st).reshape(N, 128, B).astype(np.float32).astype(BF), "bar": np.stack([gtable(a) for a in th])}
def setup_inputs(rng):
    e, p = tables_of(rng); s = rng.integers(0, W, (N, 8, L, B)); w = rng.integers(0, 5, (N, 8, L, B))
    q = np.where(w < 2, -1, np.where(w < 4, own_steps(rng, s), rng.integers(0, W, (N, 8, L, B))))
    return pack(e, p, s, q, rng.integers(0, 16, (N, 8, 16, B)), rng.choice(np.array([0, 1, 2, 2, 3, 3, 4]), (N, 8, B)))
def setup_inputs_alike(rng):
    e, p = tables_of(rng)
    fw = np.concatenate([np.argsort(rng.random((N, 8, W - 2)), axis=-1)[..., :4] + 1, np.zeros((N, 8, 1), np.int64), np.full((N, 8, 1), W - 1)], axis=2)
    ix = np.broadcast_to(fw[:, :, None, :], (N, 8, 16, 6))
    np.put_along_axis(e, ix, rng.choice(np.array([0, 3, 4, 8, 11, 12, 15]), (N, 8, 16, 6)), axis=3)
    np.put_along_axis(p, ix, np.where(rng.random((N, 8, 16, 6)) < 0.2, 12, 11), axis=3)
    n = rng.integers(0, 6, (N, 8, L, B)); n[:, 1::2] = n[:, 1::2, :, :1]
    n = np.where(rng.random((N, 8, 1, B)) < 0.15, n[:, :, :1], n)
    s = np.take_along_axis(fw, n.reshape(N, 8, L * B), axis=2).reshape(N, 8, L, B)
    q = np.take_along_axis(fw, rng.integers(0, 6, (N, 8, L * B)), axis=2).reshape(N, 8, L, B)
    q = np.where(rng.random((N, 8, L, B)) < 0.4, -1, q)
    return pack(e, p, s, q, rng.integers(0, 16, (N, 8, 16, B)), rng.integers(0, 5, (N, 8, B)))
def setup_inputs_corners(rng):
    o = np.argsort(rng.random((N, 8, W)), axis=-1); kc = np.zeros((N, 8, W), np.int64)
    np.put_along_axis(kc, o, np.broadcast_to(np.arange(W) & 7, (N, 8, W)), axis=2)
    k4 = kc[:, :, None, :]; bit = rng.integers(0, 2, (N, 8, 16, W)) == 1
    e = np.where(bit, np.array([4, 0, 12, 4, 4, 4, 4, 4])[k4], np.array([11, 3, 15, 11, 11, 11, 11, 11])[k4])
    e = np.where(k4 == 7, np.array([3, 4, 11, 12])[rng.integers(0, 4, (N, 8, 16, W))], e)
    rk = ((2 * rng.integers(0, 8, (N, 8, 1, W)) + 1) * np.arange(16)[None, None, :, None] + rng.integers(0, 16, (N, 8, 1, W))) & 15
    nd = np.where(k4 == 7, rng.integers(0, 4, (N, 8, 1, W)), np.array([0, 0, 0, 1, 2, 3, 16, 0])[k4]); bit = rng.integers(0, 2, (N, 8, 16, W)) == 1
    p = np.where(rk < nd, np.where(bit, 12, 15), np.where(bit, 11, 0))
    tp = rng.integers(0, 8, (N, 8, 1, B)); y = rng.integers(4, 7, (N, 8, 1, B)); v = rng.integers(1, L, (N, 8, 1, B)); kk = np.arange(L)[None, None, :, None]
    j = rng.choice(np.array([0, L // 2, L - 2]), (N, 8, 1, B)); cp = np.zeros((N, 8, L, B), np.int64)
    cp = np.where((tp == 1) & (kk == 0), y, cp)
    cp = np.where((tp == 2) & (kk == j), 1, cp); cp = np.where((tp == 2) & (kk == L - 1), y, cp)
    cp = np.where(tp == 3, 3, cp)
    for a, b in ((L // 3, 4), (L // 2, 5), (L - 1, 6)): cp = np.where((tp == 4) & (kk == a), b, cp)
    cp = np.where(tp == 5, np.where(kk == v, y, 1), cp)
    cp = np.where((tp == 6) & (kk == 0), 2, cp); cp = np.where((tp == 6) & (kk == L - 1), 1, cp)
    cp = np.where(tp == 7, rng.integers(0, 8, (N, 8, L, B)), cp)
    s = np.take_along_axis(o, (8 * rng.integers(0, W // 8, (N, 8, L, B)) + cp).reshape(N, 8, L * B), axis=2).reshape(N, 8, L, B)
    st = np.array([7, 8, 0, 15])[rng.integers(0, 4, (N, 8, 16, B))]
    st = np.where((tp == 1) | (tp == 3) | (tp == 4), 7, np.where(tp == 2, 8, st))
    h = np.where(tp == 2, j, np.where(tp == 5, v - 1, np.where(tp == 4, L // 3, 0))); own = np.take_along_axis(s, h, axis=2)
    qm = rng.integers(0, 4, (N, 8, 1, B))
    q = np.where(qm == 0, -1, np.where(qm == 1, own, np.where(qm == 2, np.where(rng.random((N, 8, L, B)) < 0.5, own, -1), own_steps(rng, s))))
    return pack(e, p, s, q, st, rng.choice(np.array([0, 1, 2, 3, 16]), (N, 8, B)))
def setup_inputs_ends(rng):
    t = W - 1
    e = 15 * (rng.random((N, 8, 16, W), dtype=np.float32) < rng.choice(np.array([0.0, 0.1, 0.5, 0.9, 1.0]), (N, 8, 1, W))).astype(np.int64)
    p = 15 * (rng.random((N, 8, 16, W), dtype=np.float32) < rng.choice(np.array([0.0, 0.0, 0.1, 0.3, 1.0]), (N, 8, 1, W))).astype(np.int64)
    kk = np.arange(L)[None, None, :, None]; x = rng.choice(np.array([0, 1, L // 2, L - 2, L - 1, L]), (N, 8, 1, B)); x[..., B - 1] = L - 2; x[..., B - 2] = L - 1
    m = rng.random((N, 8, 1, B)) < 0.6; m[..., B - 2:] = True
    s = t * np.where(m, (kk >= x).astype(np.int64), rng.integers(0, 2, (N, 8, L, B)))
    q = np.where(rng.random((N, 8, L, B)) < rng.choice(np.array([0.0, 0.2, 0.5, 1.0]), (N, 8, 1, B)), t, -1)
    st = 15 * (rng.random((N, 8, 16, B)) < rng.choice(np.array([0.0, 0.5, 1.0]), (N, 8, 1, B))).astype(np.int64)
    th = 16 * rng.integers(0, 2, (N, 8, B)); th[..., B - 1] = 16; th[..., B - 2] = 0
    c0 = (KAP * t) & t; c1 = ((t * t >> 5) + KAP * t) & t
    for r in range(N):
        for g in range(8):
            k = (N + 7 - r - g) & 3; u = e[r, g]
            if k == 3: continue
            if k == 0:
                u[0, c0] = 0; u[:, c0[L - 1]] = 15; u[:, 0] = 0; u[:, t] = 15 * rng.integers(0, 2, 16)
            elif k == 1:
                u[:, c1[[1, 2, L - 1]]] = 15; u[5, c1[0]] = 0; u[:, 0] = 15; u[:, t] = 0
            else:
                u[:, c1] = 0; u[:, 0] = 15; u[:, t] = 15; u[rng.permutation(16)[:2], t] = 0
            p[r, g, :, 0] = 0; p[r, g, :, t] = 15
    return pack(e, p, s, q, st, th)
def setup_inputs_full(rng):
    e, p = tables_of(rng); s = rng.integers(0, W, (N, 8, L, B)); st = rng.integers(0, 16, (N, 8, 16, B)); th = rng.choice(np.array([0, 1, 2, 2, 3, 3, 4]), (N, 8, B)); kk = np.arange(L)[:, None]
    for r in range(N):
        for g in range(8):
            m = (g + r + 2 - N) & 7
            if m > 4: continue
            o = rng.permutation(W).reshape(32, W // 32); kc = np.zeros(W, np.int64); kc[o] = np.arange(32)[:, None]
            y = rng.integers(0, 4, (16, W)); e[r, g] = np.where(kc < 17, rng.integers(4, 12, (16, W)), np.where(kc < 20, y, 12 + y))
            rk = ((2 * rng.integers(0, 8, W) + 1) * np.arange(16)[:, None] + rng.integers(0, 16, W)) & 15
            p[r, g] = np.where((rk < kc) & (kc < 17), rng.integers(12, 16, (16, W)), rng.integers(0, 12, (16, W)))
            n = rng.integers(2, 16, B) if m == 0 else rng.integers(4, 17, B)
            x = rng.choice(np.array([0, L // 2, L - 1, L - 1]), B); j = rng.integers(0, L, B); low = (j < x) & (rng.random(B) < 0.5)
            calm = rng.random(B) < (0.1 if m else 0.0)
            if m: calm[B // 2] = True
            kd = np.where(kk == x, n, np.where(kk > x, rng.integers(0, 32, (L, B)), 0)); kd = np.where((kk == j) & low, rng.integers(17, 20, B), kd); kd = np.where(calm, 0, kd)
            s[r, g] = o[kd, rng.integers(0, W // 32, (L, B))]
            st[r, g] = rng.integers(0, 8, (16, B)) + 8 * (low | calm).astype(np.int64)
            up = np.ones(B, np.int64) if m == 0 else rng.integers(0, 2, B)
            th[r, g] = np.minimum(n + up, 16)
    w = rng.integers(0, 5, (N, 8, L, B))
    q = np.where(w < 2, -1, np.where(w < 4, own_steps(rng, s), rng.integers(0, W, (N, 8, L, B))))
    return pack(e, p, s, q, st, th)
def setup_inputs_spread(rng):
    def power(hi, pw, shape): return np.minimum((hi * rng.random(shape, dtype=np.float32) ** pw.astype(np.float32)).astype(np.int64), hi - 1)
    e = power(16, rng.choice(np.array([0.5, 1.0, 2.0]), (N, 8, 16, 1)), (N, 8, 16, W))
    p = power(16, rng.choice(np.array([1.0, 3.0, 8.0, 20.0, 20.0]), (N, 8, 1, W)), (N, 8, 16, W))
    s = power(W, rng.choice(np.array([0.25, 1.0, 4.0]), (N, 8, L, 1)), (N, 8, L, B))
    q = np.where(rng.random((N, 8, L, B)) < 0.5, own_steps(rng, s), rng.integers(-1, W, (N, 8, L, B)))
    return pack(e, p, s, q, power(16, rng.choice(np.array([0.3, 1.0, 3.0]), (N, 8, 1, B)), (N, 8, 16, B)), power(17, rng.choice(np.array([1.0, 3.0, 6.0]), (N, 8, 1)), (N, 8, B)))
def check_inputs(d):
    bad = []
    for k, lo, hi in (("eff", 0, 15), ("req", 0, 15), ("act", 0, W - 1), ("why", -1, W - 1), ("st0", 0, 15), ("bar", 0, 16)):
        v = np.asarray(d[k]).astype(np.float64)
        if not (np.min(v) >= lo and np.max(v) <= hi): bad.append("range of " + k)
        elif np.any(v != np.floor(v)): bad.append("whole numbers in " + k)
    return bad
def pick(tab, ix):
    return np.stack([tab[g][:, ix[g]] for g in range(8)])
def visit(E, P, S, Q, s, th, R, t):
    kk = np.arange(L)[None, :, None]
    es = pick(E, S.reshape(8, L * B)).reshape(8, 16, L, B); ps = pick(P, S.reshape(8, L * B)).reshape(8, 16, L, B)
    flaw = np.zeros((8, 16, L, B), bool)
    for k in range(L):
        flaw[:, :, k] = (ps[:, :, k] >= 12) & (s < 8)
        s = np.where((es[:, :, k] >= 12) | (es[:, :, k] <= 3), es[:, :, k], s)
    over = np.add.reduce(flaw.astype(np.int16), axis=1) >= 2 + (R & 1)
    found = np.any(over, axis=1); ks = np.argmax(over, axis=1)
    fl = np.take_along_axis(flaw, ks[:, None, None, :], 2); need = np.take_along_axis(ps, ks[:, None, None, :], 2) >= 12
    low = np.any((es <= 3) & fl, axis=1) & (kk < ks[:, None, :])
    d = np.where(np.any(low, axis=1), L - 1 - np.argmax(low[:, ::-1], axis=1), ks)
    a = np.take_along_axis(S, ks[:, None, :], 1); z = np.take_along_axis(S, d[:, None, :], 1)
    c = ((a * z >> 5) + KAP[None, :, None] * a + 97 * t) & (W - 1)
    ec = pick(E, c.reshape(8, L * B)).reshape(8, 16, L, B)
    score = np.add.reduce(((ec >= 12) & fl).astype(np.int64), axis=1) - np.add.reduce(((ec <= 3) & need & ~fl).astype(np.int64), axis=1)
    m = np.argmax(score, axis=1); best = np.max(score, axis=1); cm = np.take_along_axis(c, m[:, None, :], 1)
    put = (found & (best >= th))[:, None, :]; ret = (found & (best < th))[:, None, :]
    kb = ks[:, None, :]
    si = np.where(kk < kb, S, np.where(kk == kb, cm, np.concatenate([S[:, :1], S[:, :-1]], axis=1)))
    qi = np.where(kk < kb, Q, np.where(kk == kb, z, np.concatenate([Q[:, :1], Q[:, :-1]], axis=1)))
    go = (kk == d[:, None, :]) | (Q == z)
    order = np.argsort(go, axis=1, kind="stable"); kept = kk < L - np.add.reduce(go.astype(np.int64), axis=1)[:, None, :]
    sr = np.where(kept, np.take_along_axis(S, order, 1), c); qr = np.where(kept, np.take_along_axis(Q, order, 1), -1)
    at = ST * np.arange(B)[None, :] + (np.add.reduce(s.astype(np.int64), axis=1) & (ST - 1))
    e2 = np.array(E); np.put_along_axis(e2, np.broadcast_to(at[:, None, :], (8, 16, B)), (pick(E, at) + s) >> 1, axis=2)
    return np.where(put, si, np.where(ret, sr, S)), np.where(put, qi, np.where(ret, qr, Q)), s, e2, int(np.count_nonzero(ret))
def reference(eff, req, act, why, st0, bar):
    E = [x.astype(np.float32).astype(np.int16).reshape(8, 16, W) for x in eff]; P = [x.astype(np.float32).astype(np.int16).reshape(8, 16, W) for x in req]
    S = [gentries(x).astype(np.int64).reshape(8, L, B) for x in act]; Q = [gentries(x).astype(np.int64).reshape(8, L, B) for x in why]
    s = [x.astype(np.float32).astype(np.int16).reshape(8, 16, B) for x in st0]; th = [gentries(x).astype(np.int64) for x in bar]; R = [0] * N
    for t in range(VI):
        v = [visit(E[r], P[r], S[r], Q[r], s[r], th[r], R[r], t) for r in range(N)]
        E = [x[3] for x in v]; R = [x[4] for x in v]; go = PS if t < VI - 1 else 0
        S = [v[(r - go) % N][0] for r in range(N)]; Q = [v[(r - go) % N][1] for r in range(N)]; s = [v[(r - 1) % N][2] for r in range(N)]
    return {"ys": np.stack([gtable(x.reshape(8, L * B)) for x in S]).astype(np.float32), "yw": np.stack([gtable(x.reshape(8, L * B)) for x in Q]).astype(np.float32),
            "ye": np.stack([x.reshape(128, W) for x in E]).astype(np.float32).astype(BF)}

@@ -1,0 +1,646 @@
+import numpy as np
+import math
+import comms_topo
+from concourse.mybir import AluOpType as A, ActivationFunctionType as F
+
+NCH, W, L, VI = 2, 4096, 16, 4
+LC = 256 // NCH
+CA = LC * L
+NJ = LC // 16
+NP = 2
+LN2 = math.log(2.0)
+BIG = 1024.0
+NDMA = 80
+NB = 8 // NCH
+BIAS = {"run0": -2.3, "end0": -1.5, "head0": 5.7, "net0": 6.6, "score0": 7.1, "fin0": 6.9, "fin1": -8.9, "run1": -8.5,
+        "net1": -4.1, "head1": 2.0, "score1": -2.5, "end1": -1.2, "tab": -3.6}
+ND = 2
+
+SCRATCH = {}
+SEMAPHORES = ["qv", "qa", "qt", "qg"] + ["d%d" % i for i in range(NDMA)]
+for _t in range(VI - 1):
+    for _c in range(NCH):
+        SEMAPHORES += ["ap%d_%d" % (_t, _c), "as%d_%d" % (_t, _c), "lp%d_%d" % (_t, _c), "ls%d_%d" % (_t, _c)]
+LOG = {}
+_SHORT = {"bfloat16": "bf", "float16": "hf", "float32": "ff", "int32": "nn", "uint16": "uu"}
+
+
+def _buf(name, cols, dtype, where="sbuf"):
+    if where == "psum":
+        SCRATCH[name] = (where, [128, cols], dtype)
+        LOG[name] = (where, cols, dtype, name, 0)
+        return
+    t = "pk" + _SHORT[dtype]
+    o = SCRATCH[t][1][1] if t in SCRATCH else 0
+    SCRATCH[t] = ("sbuf", [128, o + -(-cols // 64) * 64], dtype)
+    LOG[name] = (where, cols, dtype, t, o)
+
+
+for _n in ("er", "gt", "nt", "tq"):
+    _buf(_n, W, "bfloat16")
+for _n in ("ip", "ic", "gp", "gc", "kp", "kc"):
+    _buf(_n, 128, "int32")
+for _n in ("dd", "cc", "pp", "ns", "eye", "blk", "str", "tri", "first", "half", "shd", "sh1", "sh2", "sh4", "sh8", "neg",
+           "i4", "im85", "i512", "i71", "i72", "i2048", "mt", "mth", "mr", "blkz", "ones", "nblk", "blk4", "e0"):
+    _buf(_n, 128, "bfloat16")
+_buf("wk", 16 * 128, "bfloat16")
+_buf("thf", 128, "float32")
+_buf("allo", 128, "float32")
+for _n in ("kcol", "kap", "cq", "k16", "thr", "m1c"):
+    _buf(_n, 8, "float32")
+_buf("rci", 8, "int32")
+_buf("xbase", 2 * NJ, "bfloat16")
+_buf("xbi", NJ, "int32")
+_buf("bari", 256, "int32")
+_buf("barb", 256, "bfloat16")
+for _n in ("bark", "sti", "sth", "stc"):
+    _buf(_n, 256, "bfloat16")
+_buf("actk", 256, "int32")
+_buf("whyk", 256, "int32")
+_buf("ysk", 256, "float32")
+_buf("ywk", 256, "float32")
+for _c in range(NCH):
+    for _t in range(VI):
+        _buf("w%d_%d" % (_t, _c), 2 * LC, "float16")
+        _buf("wo%d_%d" % (_t, _c), 2 * LC, "float16")
+        _buf("s%d_%d" % (_t, _c), LC, "bfloat16")
+        _buf("so%d_%d" % (_t, _c), LC, "bfloat16")
+        _buf("ac%d_%d" % (_t, _c), 8, "float32")
+    _buf("gb%d" % _c, CA + 16, "bfloat16")
+    for _n in ("kb", "zb", "fl", "cg", "hb"):
+        _buf("%s%d" % (_n, _c), CA, "bfloat16")
+    for _n in ("e15", "k15", "t15", "val", "h8", "ov", "X", "zx", "nx", "hx", "w8", "f1", "T", "D", "pw", "pv", "eq", "M",
+               "insi", "nin", "xi", "ret", "qe", "go", "fm", "rb", "ar", "eo", "ne", "cl", "hh", "ng"):
+        _buf("%s_%d" % (_n, _c), LC, "bfloat16")
+    for _n in ("ds", "cf", "mc", "iv", "iq"):
+        _buf("%s_%d" % (_n, _c), LC, "float16")
+    for _n in ("a1", "a2", "m0", "m1", "m2", "m3", "wb", "fi", "xq"):
+        _buf("%s_%d" % (_n, _c), 2 * LC, "float16")
+    for _n in ("f4", "y7", "pr", "sh", "sm", "ci", "ri", "mk", "eh"):
+        _buf("%s_%d" % (_n, _c), LC, "int32")
+    for _n in ("tj", "sx", "tb"):
+        _buf("%s_%d" % (_n, _c), LC, "float32")
+    for _n in ("off", "c16"):
+        _buf("%s_%d" % (_n, _c), LC, "uint16")
+    _buf("xl_%d" % _c, 2 * NJ, "uint16")
+    _buf("vl_%d" % _c, NJ, "uint16")
+    for _n in ("ui", "uj", "uk", "vb"):
+        _buf("%s_%d" % (_n, _c), NJ, "int32")
+for _i in range(8):
+    _buf("p%d" % _i, 512, "float32", "psum")
+
+
+def overlap(a, b):
+    if a[0] != b[0] or a[1] >= b[2] or b[1] >= a[2]:
+        return False
+    if a[3] == b[3] and a[3] > 1 and (a[1] - b[1]) % a[3]:
+        return False
+    if a[4] is not None and b[4] is not None and a[4] != b[4]:
+        return False
+    return True
+
+
+def rank_program(g, core, T, topo):
+    rank = T.rank_of(core)
+    if rank is None:
+        return
+    nxt = T.cores[(rank + 1) % len(T.cores)]
+    ops = []
+    acc = {}
+    Q = {"v": g.vector, "a": g.scalar, "t": g.tensor, "g": g, "s": g.sync}
+    QS = {"v": "qv", "a": "qa", "t": "qt", "g": "qg"}
+    dn = [0]
+    PH = ["set"]
+    PS = set("p%d" % i for i in range(8))
+
+    def R(name, a=None, b=None, st=1, p=None):
+        n = LOG[name][1] if name in LOG else T[name].shape[1]
+        return (name, 0 if a is None else a, n if b is None else b, st, p)
+
+    def ap(r):
+        t, o = (LOG[r[0]][3], LOG[r[0]][4]) if r[0] in LOG else (r[0], 0)
+        if r[4] is not None:
+            return T[t][r[4][0]:r[4][1]:r[4][2], o + r[1]:o + r[2]]
+        if r[3] > 1:
+            return T[t][:, o + r[1]:o + r[2]:r[3]]
+        return T[t][:, o + r[1]:o + r[2]]
+
+    def ind(win, off):
+        return ("IND", win, off)
+
+    def x(r):
+        if isinstance(r, tuple):
+            if r[0] == "IND":
+                return ap(r[1]).indirect(ap(r[2]))
+            return ap(r)
+        return r
+
+    def n_of(r):
+        return -(-(r[2] - r[1]) // r[3])
+
+    def add(q, fns, reads, writes, cost, kind="c", lat=0.0, sem=None, inc=0, extra=()):
+        i = len(ops)
+        rd = []
+        for r in reads:
+            if isinstance(r, tuple):
+                rd += [r[1], r[2]] if r[0] == "IND" else [r]
+        wr = []
+        for r in writes:
+            if r[0] == "IND":
+                wr.append(r[1])
+                rd.append(r[2])
+            else:
+                wr.append(r)
+        deps = set(extra)
+        for lst, isw in ((rd, False), (wr, True)):
+            for r in lst:
+                ps = r[0] in PS
+                for (j, r2, w2) in acc.get(r[0], ()):
+                    if ps and ops[j]["q"] != q:
+                        deps.add(j)
+                    elif (isw or w2) and overlap(r, r2):
+                        deps.add(j)
+        for lst, isw in ((rd, False), (wr, True)):
+            for r in lst:
+                cur = acc.setdefault(r[0], [])
+                if isw and r[3] == 1 and r[4] is None and r[0] not in PS:
+                    cur[:] = [e for e in cur if not (e[1][1] >= r[1] and e[1][2] <= r[2])]
+                cur.append((i, r, isw))
+        ops.append({"ph": PH[0], "q": q, "fns": fns, "deps": deps, "cost": cost, "kind": kind, "lat": lat, "sem": sem, "inc": inc})
+        return i
+
+    def two(*rs):
+        return all(isinstance(r, tuple) and r[0] in LOG and LOG[r[0]][2] in ("bfloat16", "float16", "uint16") and r[0] not in PS for r in rs)
+
+    CY = 0.00083
+
+    def vc(n, rate):
+        return 0.02 + max(64, n * rate) * CY
+
+    def tt(out, a, b, op):
+        rate = 1.6 if a[0] == "IND" else (1.0 if a[0] in PS or b[0] in PS else 2.0)
+        return add("v", [lambda: g.vector.tensor_tensor(x(out), x(a), x(b), op)], [a, b], [out], vc(n_of(out), rate))
+
+    def ts(out, a, s1, op0, s2=None, op1=None):
+        rate = 0.5 if two(out, a) else 1.0
+        if op1 is None:
+            f = lambda: g.vector.tensor_scalar(x(out), x(a), x(s1), None, op0)
+        else:
+            f = lambda: g.vector.tensor_scalar(x(out), x(a), x(s1), x(s2), op0, op1)
+        return add("v", [f], [a, s1, s2], [out], vc(n_of(out), rate))
+
+    def cp(out, a):
+        rate = 4.0 if out[0] == "IND" else (0.5 if two(out, a) else 1.0)
+        return add("v", [lambda: g.vector.tensor_copy(x(out), x(a))], [a], [out], vc(n_of(a), rate))
+
+    def fill(out, v):
+        add("v", [lambda: g.vector.memset(x(out), v)], [], [out], 0.1)
+
+    def scan(out, d0, d1):
+        add("v", [lambda: g.vector.tensor_tensor_scan(x(out), x(d0), x(d1), 0.0, A.mult, A.add)], [d0, d1], [out], vc(n_of(out), 0.5))
+
+    def act(out, a, func, bias=None, scale=None, accum=None):
+        kw = {}
+        if func == F.Copy and (bias is not None or scale is not None):
+            func = F.Identity
+        if bias is not None:
+            kw["bias"] = bias
+        if scale is not None:
+            kw["scale"] = scale
+        if accum is not None:
+            kw["accum_out"] = accum
+        rate = 1.6 if a[0] == "IND" else 1.0
+        return add("a", [lambda: g.scalar.activation(x(out), x(a), func, **{k: x(v) for k, v in kw.items()})], [a, bias, scale],
+                   [out] + ([accum] if accum is not None else []), 0.04 + max(64, n_of(out) * rate) * CY)
+
+    def mm(items):
+        fns, rd, wr, cost = [], [], [], 0.02
+        for (o, l, r, s, e) in items:
+            fns.append(lambda o=o, l=l, r=r, s=s, e=e: g.tensor.matmul(x(o), x(l), x(r), s, e))
+            rd += [l, r]
+            wr.append(o)
+            cost += max(64, n_of(r)) * CY * (4 if LOG[r[0]][2] == "float32" else 1)
+        return add("t", fns, list(dict.fromkeys(rd)), list(dict.fromkeys(wr)), cost)
+
+    def dma(q, out, a):
+        s = "d%d" % dn[0]
+        dn[0] += 1
+        return add(q, [lambda: Q[q].dma_start(x(out), x(a))], [a], [out], 0.1, "d", 2.2, s, 16)
+
+    def remote(tag, out, a):
+        m, ne = 0, 8
+        for e in topo.engines(core, nxt)[:ne]:
+            m |= 1 << e
+        rid, pid = topo.addr(nxt)[0], topo.addr(nxt)[1]
+        ra, la = T.sem["a" + tag], T.sem["l" + tag]
+        i = add("g", [lambda: g.remote_dma(ap(out), ap(a), ra, la, pid, rid, m)], [a], [], 1.2, "r", 2.5, "l" + tag, ne)
+        return add("x", [], [], [out], 0.0, "x", 0.0, "a" + tag, ne, (i,))
+
+    ring = [[0] for _ in range(NCH)]
+
+    def bank(c):
+        i = ring[c][0]
+        ring[c][0] = (i + 1) % (NB - 2)
+        return "p%d" % (c * NB + i)
+
+    def nbank(c):
+        return "p%d" % (c * NB + NB - 2)
+
+    def wbank(c):
+        return "p%d" % (c * NB + NB - 1)
+
+    def lanes(q, buf, name, r0, r1):
+        for r in range(r0, r1):
+            dma(q, R(buf, 16 * r, 16 * r + 16), R(name, None, None, 1, (r, 128, 16)))
+    for j in range(4):
+        dma("s", R("er", 1024 * j, 1024 * j + 1024), R("eff", 1024 * j, 1024 * j + 1024))
+    lanes("a", "actk", "act", 0, 16 // NCH)
+    dma("a", R("sti"), R("st0"))
+    for j in range(4):
+        dma("s", R("tq", 1024 * j, 1024 * j + 1024), R("req", 1024 * j, 1024 * j + 1024))
+    lanes("s", "actk", "act", 16 // NCH, 16)
+    fill(R("bari"), 0)
+    dma("s", R("bari", None, None, 1, (0, 128, 16)), R("bar"))
+    lanes("s", "whyk", "why", 0, 16)
+
+    def iota(out, pattern, base, cm):
+        add("g", [lambda: g.iota(x(out), pattern, base, cm)], [], [out], 0.13 + 2 * n_of(out) * CY)
+    iota(R("ip"), [[0, 128]], 0, 1)
+    iota(R("ic"), [[1, 128]], 0, 0)
+    iota(R("xbi"), [[256, NJ]], 0, 0)
+    for c in range(NCH):
+        iota(R("vb_%d" % c), [[16, NJ]], LC * c, 0)
+    ts(R("gp"), R("ip"), 4, A.arith_shift_right)
+    ts(R("gc"), R("ic"), 4, A.arith_shift_right)
+    ts(R("kp"), R("ip"), 15, A.bitwise_and)
+    ts(R("kc"), R("ic"), 15, A.bitwise_and)
+    tt(R("blk"), R("gp"), R("gc"), A.is_equal)
+    ts(R("ns"), R("blk"), -64.0, A.mult, 64.0, A.add)
+    tt(R("cc"), R("kc"), R("ns"), A.add)
+    tt(R("pp"), R("kp"), R("ns"), A.add)
+    tt(R("dd"), R("kc"), R("pp"), A.subtract)
+    ts(R("eye"), R("dd"), 0.0, A.is_equal)
+    ts(R("str"), R("dd"), 1.0, A.is_ge)
+    ts(R("tri"), R("dd"), 0.0, A.is_ge)
+    for nm, de in (("shd", 1.0), ("sh1", -1.0), ("sh2", -2.0), ("sh4", -4.0), ("sh8", -8.0)):
+        ts(R("hb0", 0, 128), R("dd"), de, A.is_equal)
+        tt(R(nm), R("hb0", 0, 128), R("eye"), A.subtract)
+    for nm, f in (("neg", -1.0), ("i4", 4.0), ("im85", -8.5), ("i512", -512.0), ("i71", 71.5), ("i72", 72.0), ("i2048", 2048.0)):
+        act(R(nm), R("eye"), F.Copy, None, f)
+    ts(R("mt"), R("str"), -32.0, A.mult)
+    tt(R("first"), R("mt"), R("eye"), A.add)
+    ts(R("half"), R("first"), 0.5, A.mult)
+    ts(R("mr"), R("eye"), -64.0, A.mult)
+    tt(R("mr"), R("mr"), R("str"), A.add)
+    ts(R("e0"), R("pp"), 0.0, A.is_equal)
+    ts(R("mt"), R("sh1"), -2.0, A.mult)
+    tt(R("mt"), R("mt"), R("e0"), A.subtract)
+    ts(R("thf"), R("dd"), 5.0, A.min, 8.0 * LN2, A.mult)
+    ts(R("kcol", 0, 1), R("kp", 0, 1), 1.0, A.mult)
+    BC = {}
+    for q, (nm, v) in enumerate((("thj", 56.0 * LN2 + math.log(0.7)), ("w8", 60.0 * LN2), ("tb", 40.0 * LN2 + math.log(0.7 / 24.0)),
+                                 ("f4", -3.5), ("one", -1.0), ("hi", -11.5), ("pv", -40.0 * LN2))):
+        BC[nm] = R("m1c", q, q + 1)
+        fill(BC[nm], v)
+    act(R("mth"), R("thf"), F.Exp, BC["thj"])
+    ts(R("blkz"), R("blk"), 1.0 / 24.0, A.mult)
+    ts(R("blk4"), R("blk"), 4.0, A.mult)
+    ts(R("nblk"), R("blk"), -1.0, A.mult)
+    for k in range(16):
+        ts(R("wk", 128 * k, 128 * k + 128), R("cc"), float(k), A.is_equal)
+    ts(R("kap", 0, 1), R("kcol", 0, 1), 241.0, A.mult, 101.0, A.add)
+    for t in range(VI):
+        ts(R("kap", 4 + t, 5 + t), R("kap", 0, 1), 2048.0, A.mult, float(97 * t), A.add)
+    ts(R("cq", 0, 1), R("kcol", 0, 1), -16.0, A.mult, 0.5, A.add)
+    ts(R("k16", 0, 1), R("kcol", 0, 1), -1.0, A.mult, 16.0, A.add)
+    fill(R("thr", 0, 1), -1.5)
+    fill(R("ones"), 1.0)
+    fill(R("allo"), 1.0 / 16.0)
+    ts(R("kcol", 2, 3), R("kcol", 0, 1), 16.0, A.mult)
+    ts(R("xbase", 0, NJ), R("xbi"), R("kcol", 2, 3), A.add)
+    fill(R("xbase", NJ, 2 * NJ), 2048.0)
+    ts(R("kcol", 4, 5), R("kcol", 0, 1), 256.0, A.mult)
+    for c in range(NCH):
+        ts(R("vb_%d" % c), R("vb_%d" % c), R("kcol", 4, 5), A.add)
+    cp(R("barb"), R("bari"))
+    b = bank(0)
+    mm([(R(b, 0, 256), R("e0"), R("barb"), True, True)])
+    cp(R("bark"), R(b, 0, 256))
+    for c in range(NCH):
+        a0, a1 = c * LC, (c + 1) * LC
+        ts(R("w0_%d" % c, 0, LC), R("actk", a0, a1), -2048.0, A.add)
+        ts(R("w0_%d" % c, LC, 2 * LC), R("whyk", a0, a1), -2047.0, A.add)
+    ts(R("sth"), R("sti"), 8.0, A.is_ge, 144.0, A.mult)
+    tt(R("stc"), R("sti"), R("sth"), A.add)
+    for r in range(16):
+        c, o = divmod(16 * r, LC)
+        act(R("s0_%d" % c, o, o + 16), R("stc", r, 256, 16), F.Copy, -20.0)
+
+    def code(dst, src, cl, hh, b, n):
+        ts(cl, src, 4.0, A.max, 11.0, A.min)
+        act(hh, src, F.Sign, BC["hi"])
+        mm([(R(b, 0, n), R("eye"), src, True, False), (R(b, 0, n), R("neg"), cl, False, False), (R(b, 0, n), R("i71"), hh, False, True)])
+        act(dst, R(b, 0, n), F.Copy, 63.5)
+    for j in range(8):
+        c0, c1 = 512 * j, 512 * j + 512
+        d = 512 * (j % 4)
+        if j >= 8 - ND:
+            n1, n2 = R("fl%d" % (j % 2), d, d + 512), R("cg%d" % (j % 2), d, d + 512)
+            ts(n1, R("er", c0, c1), 4.0, A.max, 11.0, A.min)
+            tt(n2, R("er", c0, c1), n1, A.subtract)
+            ts(n1, R("er", c0, c1), 12.0, A.is_ge, 143.0, A.mult)
+            tt(n2, n2, n1, A.add)
+            ts(R("gt", c0, c1), n2, -8.0, A.add)
+            continue
+        code(R("gt", c0, c1), R("er", c0, c1), R("kb%d" % (j // 4), d, d + 512), R("zb%d" % (j // 4), d, d + 512), bank(j % 2), 512)
+    for j in range(4):
+        c0, c1 = 1024 * j, 1024 * j + 1024
+        ts(R("nt", c0, c1), R("tq", c0, c1), 12.0, A.is_lt, -BIG, A.mult)
+
+    def run(t, c):
+        def K(n, *a):
+            return R("%s_%d" % (n, c), *a)
+        PH[0] = "run%d" % c
+        gb, kb, zb, fl = "gb%d" % c, "kb%d" % c, "zb%d" % c, "fl%d" % c
+        w, s = "w%d_%d" % (t, c), "s%d_%d" % (t, c)
+        ts(K("off"), R(w, 0, LC), 2048.0, A.add)
+        b = bank(c)
+        for p in range(NP):
+            l0, l1 = p * LC // NP, (p + 1) * LC // NP
+            e0, e1 = 16 * l0, 16 * l1
+            act(R(gb, e0 + 1, e1 + 1), ind(R("gt"), K("off", l0, l1)), F.Copy)
+            act(K("e15", l0, l1), R(gb, e0 + 16, e1 + 1, 16), F.Copy, 4.0)
+            act(R(gb, e0, e1, 16), R(s, l0, l1), F.Copy)
+            ts(R(kb, e0, e1), R(gb, e0, e1), -8.0, A.is_equal)
+            scan(R(zb, e0, e1), R(kb, e0, e1), R(gb, e0, e1))
+            tt(R(fl, e0, e1), ind(R("nt"), K("off", l0, l1)), R(zb, e0, e1), A.is_gt)
+            mm([(R(b, l0, l1), R("wk", 128 * k, 128 * k + 128), R(fl, e0 + k, e1, 16), k == 0, k == 15) for k in range(16)])
+        act(K("ov"), R(b, 0, LC), F.Sign, R("thr", 0, 1))
+        PH[0] = "end%d" % c
+        nb = nbank(c)
+        o = R(nb, 0, LC)
+        ts(K("k15"), K("e15"), -4.0, A.is_equal)
+        tt(K("t15"), K("k15"), R(zb, 15, CA, 16), A.mult)
+        mm([(o, R("eye"), K("t15"), True, False), (o, R("eye"), K("e15"), False, True)])
+        cp(K("f4"), o)
+        act(K("h8"), o, F.Sign, BC["f4"])
+        ts(K("y7"), K("f4"), 7, A.bitwise_and)
+        mm([(o, R("i4"), K("h8"), True, False), (o, R("i4"), R("ones", 0, LC), False, True)])
+        tt(K("val"), K("y7"), o, A.add)
+        if t < VI - 1:
+            mm([(o, R("eye"), K("val"), True, False), (o, R("i72"), K("h8"), False, True)])
+            act(R("so%d_%d" % (t, c)), o, F.Copy, 52.0)
+            remote("s%d_%d" % (t, c), R("s%d_%d" % (t + 1, c)), R("so%d_%d" % (t, c)))
+        o = R(nb, 0, NJ)
+        mm([(o, R("wk", 128 * r, 128 * r + 128), R("val_%d" % c, r, LC, 16), r == 0, r == 15) for r in range(16)])
+        cp(K("ui"), o)
+        ts(K("uj"), K("ui"), 15, A.bitwise_and)
+        tt(K("uk"), K("uj"), K("vb"), A.add)
+        cp(K("vl"), K("uk"))
+        act(K("eo"), ind(R("er"), K("vl")), F.Copy)
+        o = R(nb, 0, LC)
+        mm([(o, R("eye"), K("eo"), True, False), (o, R("eye"), K("val"), False, True)])
+        ts(K("eh"), o, 0.5, A.mult, -0.25, A.add)
+        cp(K("ne"), K("eh"))
+        if t < VI - 1:
+            code(K("ng"), K("ne"), K("cl"), K("hh"), nb, LC)
+        cp(ind(R("er"), K("vl")), K("ne"))
+
+    def table(t, c):
+        PH[0] = "tab"
+        if t < VI - 1:
+            cp(ind(R("gt"), R("vl_%d" % c)), R("ng_%d" % c))
+
+    def cand(t, c):
+        def K(n, *a):
+            return R("%s_%d" % (n, c), *a)
+        PH[0] = "head%d" % c
+        w = "w%d_%d" % (t, c)
+        S_, Q_ = R(w, 0, LC), R(w, LC, 2 * LC)
+        pw, nb = wbank(c), nbank(c)
+        wp, n2 = R(pw, 0, 2 * LC), R(nb, 0, 2 * LC)
+        mm([(wp, R("eye"), R(w, 0, 2 * LC), True, True)])
+        wS = R(pw, 0, LC)
+        b = bank(c)
+        mm([(R(b, 0, LC), R("half"), K("ov"), True, True)])
+        act(K("X"), R(b, 0, LC), F.Relu, R("cq", 0, 1))
+        ts(K("xq", 0, LC), K("X"), R("kcol", 0, 1), A.mult)
+        tt(K("xq", LC, 2 * LC), K("X"), wS, A.mult)
+        b = bank(c)
+        mm([(R(b, 0, 2 * NJ), R("wk", 128 * r, 128 * r + 128), R("xq_%d" % c, r, 2 * LC, 16), r == 0, False) for r in range(16)]
+           + [(R(b, 0, 2 * NJ), R("eye"), R("xbase"), False, True)])
+        cp(K("xl"), R(b, 0, 2 * NJ))
+        b = bank(c)
+        mm([(R(b, 0, LC), R("mth"), K("X"), True, True)])
+        act(K("tj"), R(b, 0, LC), F.Copy)
+        act(K("zx"), ind(R("zb%d" % c), K("xl", 0, NJ)), F.Copy)
+        act(K("nx"), ind(R("nt"), K("xl", NJ, 2 * NJ)), F.Copy)
+        ts(K("hx"), K("zx"), 0.0, A.is_ge)
+        b = bank(c)
+        mm([(R(b, 0, LC), R("eye"), K("zx"), True, False), (R(b, 0, LC), R("i512"), K("hx"), False, False), (R(b, 0, LC), R("eye"), K("nx"), False, True)])
+        act(K("w8"), R(b, 0, LC), F.Exp, BC["w8"], LN2)
+        ts(K("f1"), K("w8"), 0.0, A.is_gt)
+        b = bank(c)
+        mm([(R(b, 0, LC), R("blk"), K("w8"), True, True)])
+        tt(K("T"), R(b, 0, LC), K("tj"), A.is_ge)
+        b = bank(c)
+        mm([(R(b, 0, LC), R("mt"), K("T"), True, False), (R(b, 0, LC), R("eye"), K("X"), False, True)])
+        act(K("D"), R(b, 0, LC), F.Relu)
+        tt(K("ds"), K("D"), wS, A.mult)
+        b = bank(c)
+        mm([(R(b, 0, LC), R("blk"), K("xq", LC, 2 * LC), True, True)])
+        mm([(R(b, LC, 2 * LC), R("blk"), K("ds"), True, True)])
+        mm([(R(pw, 2 * LC, 3 * LC), R("blk"), K("ds"), True, False), (R(pw, 2 * LC, 3 * LC), R("eye"), R("ones", 0, LC), False, True)])
+        act(K("sx"), R(b, 0, LC), F.Copy, 2048.0)
+        act(R(b, 2 * LC, 3 * LC), R(b, 0, LC), F.Copy, R("kap", 4 + t, 5 + t), R("kap", 0, 1))
+        tt(K("pr"), R(b, LC, 2 * LC), K("sx"), A.mult)
+        ts(K("sh"), K("pr"), 5, A.arith_shift_right)
+        tt(K("sm"), K("sh"), R(b, 2 * LC, 3 * LC), A.add)
+        ts(K("ci"), K("sm"), 4095, A.bitwise_and)
+        cp(K("c16"), K("ci"))
+        PH[0] = "net%d" % c
+
+        def prod(n, wd, mask):
+            tt(K(n, 0, LC), R(wd[0], wd[1], wd[1] + LC), mask, A.mult)
+            tt(K(n, LC, 2 * LC), R(wd[0], wd[1] + LC, wd[1] + 2 * LC), mask, A.mult)
+        ts(K("cf"), K("ci"), -2048.0, A.add)
+        tt(K("qe"), Q_, R(pw, 2 * LC, 3 * LC), A.is_equal)
+        o = R(nb, 0, LC)
+        mm([(o, R("eye"), K("D"), True, False), (o, R("eye"), K("qe"), False, False), (o, R("blk4"), K("X"), False, True)])
+        ts(K("go"), o, 4.5, A.is_ge)
+        pr = R(nb, LC, 2 * LC)
+        mm([(o, R("blk"), K("go"), True, True), (pr, R("mr"), K("go"), True, True)])
+        act(K("rb"), pr, F.Relu)
+        ts(K("fm"), o, R("k16", 0, 1), A.is_ge)
+        o2 = R(nb, 2 * LC, 3 * LC)
+        mm([(o2, R("tri"), K("X"), True, True)])
+        tt(K("a1", 0, LC), S_, o2, A.mult)
+        tt(K("a1", LC, 2 * LC), Q_, o2, A.mult)
+        tt(K("iq"), K("X"), R(pw, 2 * LC, 3 * LC), A.mult)
+        prod("a2", wp, K("go"))
+        tt(K("fi", 0, LC), K("fm"), K("cf"), A.mult)
+        ts(K("fi", LC, 2 * LC), K("fm"), -2048.0, A.mult)
+        base, moves = R(w, 0, 2 * LC), [("neg", "a2")]
+        for s in range(4):
+            ts(K("ri"), pr, 0.0, A.max)
+            ts(K("mk"), K("ri"), s, A.arith_shift_right, 1, A.bitwise_and)
+            prod("m%d" % s, wp, K("mk"))
+            moves.append(("sh%d" % (1 << s), "m%d" % s))
+            if s < 3:
+                tt(K("ar"), pr, K("mk"), A.mult)
+                pr = R(nb, ((s + 2) % 4) * LC, ((s + 2) % 4 + 1) * LC)
+                mm([(pr, R("eye"), K("rb"), True, False), (pr, R("sh%d" % (1 << s)), K("ar"), False, True)])
+                if s < 2:
+                    act(K("rb"), pr, F.Copy)
+            if s == 3:
+                moves += [("eye", "fi")]
+            mm([(wp, R("eye"), base, True, False)] + [(wp, R(m), K(a), False, q == len(moves) - 1) for q, (m, a) in enumerate(moves)])
+            if s == 1:
+                cp(K("wb"), wp)
+                base, moves = K("wb"), []
+        mm([(n2, R("eye"), R(w, 0, 2 * LC), True, False), (n2, R("shd"), K("a1"), False, False),
+            (R(nb, LC, 2 * LC), R("eye"), K("iq"), False, True)])
+        PH[0] = "score%d" % c
+        hb, cg = "hb%d" % c, "cg%d" % c
+        rb_ = bank(c)
+        rr = R(rb_, 0, LC)
+        mm([(rr, R("im85"), K("hx"), True, False), (rr, R("eye"), K("nx"), False, True)])
+        b = bank(c)
+        mm([(R(b, 0, LC), R("nblk"), K("f1"), True, False), (R(b, 0, LC), R("eye"), R("bark", c * LC, (c + 1) * LC), False, True)])
+        act(K("tb"), R(b, 0, LC), F.Exp, BC["tb"], 5.0 * LN2)
+        act(R(cg), ind(R("gt"), K("c16")), F.Copy)
+        for m in range(16):
+            tt(R(hb, m * LC, (m + 1) * LC), R(cg, m, CA, 16), rr, A.is_gt)
+        mm([(R(b, m, 128, 16), R(hb, m * LC, (m + 1) * LC), R("blk", 0, 128, 16), True, True) for m in range(16)])
+        act(K("pv"), R(b, 0, LC), F.Exp, BC["pv"], 5.0 * LN2)
+        mm([(R(b, LC, 2 * LC), K("pv"), R("eye"), True, True)])
+        act(K("pw"), R(b, LC, 2 * LC), F.Copy)
+        mm([(rr, R("blkz"), K("pw"), True, True)])
+        tt(K("eq"), rr, K("pw"), A.is_le)
+        tt(K("insi"), rr, K("tb"), A.is_ge)
+        tt(K("nin"), rr, K("tb"), A.is_lt)
+        b = bank(c)
+        mm([(R(b, 0, LC), R("first"), K("eq"), True, True)])
+        act(K("M"), R(b, 0, LC), F.Relu)
+        mm([(R(b, 2 * LC, 3 * LC), R("eye"), K("X"), True, False), (R(b, 2 * LC, 3 * LC), R("eye"), K("insi"), False, True),
+            (R(b, 3 * LC, 4 * LC), R("blk"), K("X"), True, False), (R(b, 3 * LC, 4 * LC), R("neg"), K("insi"), False, True)])
+        act(K("xi"), R(b, 2 * LC, 3 * LC), F.Relu, BC["one"])
+        if t < VI - 1:
+            act(K("ret"), R(b, 3 * LC, 4 * LC), F.Relu, accum=R("ac%d_%d" % (t, c), 0, 1))
+        tt(K("mc"), K("M"), K("cf"), A.mult)
+        mm([(rr, R("blk"), K("mc"), True, True)])
+        PH[0] = "fin%d" % c
+        prod("m0", n2, K("insi"))
+        prod("m1", wp, K("nin"))
+        tt(K("iv"), K("xi"), rr, A.mult)
+        b = bank(c)
+        fp = R(b, 0, 2 * LC)
+        mm([(fp, R("eye"), K("m1"), True, False), (fp, R("eye"), K("m0"), False, False), (R(b, 0, LC), R("eye"), K("iv"), False, True)])
+        if t < VI - 1:
+            wo = "wo%d_%d" % (t, c)
+            cp(R(wo), fp)
+            remote("p%d_%d" % (t, c), R("w%d_%d" % (t + 1, c)), R(wo))
+        else:
+            act(R("ysk", c * LC, (c + 1) * LC), R(b, 0, LC), F.Copy, 2048.0)
+            act(R("ywk", c * LC, (c + 1) * LC), R(b, LC, 2 * LC), F.Copy, 2047.0)
+            for r in range(c * NJ, (c + 1) * NJ):
+                dma("s", R("ys", None, None, 1, (r, 128, 16)), R("ysk", 16 * r, 16 * r + 16))
+                dma("a" if c == NCH - 1 else "s", R("yw", None, None, 1, (r, 128, 16)), R("ywk", 16 * r, 16 * r + 16))
+
+    def count(t):
+        b = bank(0)
+        mm([(R(b, 0, 1), R("allo"), R("ac%d_%d" % (t, c), 0, 1), c == 0, c == NCH - 1) for c in range(NCH)])
+        cp(R("rci", 0, 1), R(b, 0, 1))
+        ts(R("rci", 4, 5), R("rci", 0, 1), 1, A.bitwise_and)
+        ts(R("thr", 0, 1), R("rci", 4, 5), -1.0, A.mult, -1.5, A.add)
+
+    for t in range(VI):
+        for c in range(NCH):
+            run(t, c)
+        for c in range(NCH):
+            cand(t, c)
+        for c in range(NCH):
+            table(t, c)
+        if t < VI - 1:
+            count(t)
+    for j in range(2):
+        dma("s" if j else "a", R("ye", 2048 * j, 2048 * j + 2048), R("er", 2048 * j, 2048 * j + 2048))
+
+    n = len(ops)
+    HOP = 0.07
+    tail = [0.0] * n
+    succ = [[] for _ in range(n)]
+    for i, o in enumerate(ops):
+        for d in o["deps"]:
+            succ[d].append(i)
+    for i in range(n - 1, -1, -1):
+        o = ops[i]
+        m = 0.0
+        for j in succ[i]:
+            m = max(m, tail[j])
+        tail[i] = m + o["cost"] + o["lat"] + HOP
+    prio = [tail[i] + BIAS.get(ops[i]["ph"], 0.0) for i in range(n)]
+    ndep = [len(o["deps"]) for o in ops]
+    ready = [0.0] * n
+    avail = [i for i in range(n) if ndep[i] == 0]
+    free = {q: 0.0 for q in "vatgsx"}
+    order = []
+    while avail:
+        best = None
+        for i in avail:
+            q = ops[i]["q"]
+            st = ready[i] if q == "x" else max(ready[i], free[q])
+            key = (round(st, 2), -prio[i], i)
+            if best is None or key < best[0]:
+                best = (key, i, st)
+        _, i, st = best
+        avail.remove(i)
+        o = ops[i]
+        if o["q"] != "x":
+            free[o["q"]] = st + o["cost"]
+        fin = st + o["cost"] + o["lat"]
+        order.append(i)
+        for j in succ[i]:
+            ready[j] = max(ready[j], fin + (HOP if ops[j]["q"] != o["q"] else 0.03))
+            ndep[j] -= 1
+            if ndep[j] == 0:
+                avail.append(j)
+
+    cnt = {"qv": 0, "qa": 0, "qt": 0, "qg": 0}
+    known = {q: {} for q in "vatgs"}
+    done = {}
+    tot = {}
+
+    def wait(q, sem, v):
+        if known[q].get(sem, 0) < v:
+            Q[q].wait_ge(T.sem[sem], v)
+            known[q][sem] = v
+
+    for i in order:
+        o = ops[i]
+        q = o["q"]
+        if q == "x":
+            done[i] = (o["sem"], o["inc"], {o["sem"]: o["inc"]})
+            tot[o["sem"]] = o["inc"]
+            continue
+        for d in sorted(o["deps"], reverse=True):
+            sem, v, clk = done[d]
+            if known[q].get(sem, 0) < v:
+                wait(q, sem, v)
+                for s2, v2 in clk.items():
+                    if known[q].get(s2, 0) < v2:
+                        known[q][s2] = v2
+        for f in o["fns"]:
+            r = f()
+            if o["kind"] == "c":
+                cnt[QS[q]] += 1
+                r.then_inc(T.sem[QS[q]], 1)
+            elif o["kind"] == "d":
+                r.then_inc(T.sem[o["sem"]], 16)
+        clk = dict(known[q])
+        s, v = (QS[q], cnt[QS[q]]) if o["kind"] == "c" else (o["sem"], o["inc"])
+        clk[s] = v
+        done[i] = (s, v, clk)
+        tot[s] = v
+    for s, v in tot.items():
+        wait("g", s, v)

@@ -8,13 +8,22 @@ LC = 256 // NCH
 CA = LC * L
 NJ = LC // 16
 NP = 2
+NPC = 1
+NG = 2
+NF = 2
+NC = 4
 LN2 = math.log(2.0)
-BIG = 1024.0
+AGE = 7
+LA = 80.0 / AGE
 NDMA = 80
-NB = 8 // NCH
-BIAS = {"run0": -2.3, "end0": -1.5, "head0": 5.7, "net0": 6.6, "score0": 7.1, "fin0": 6.9, "fin1": -8.9, "run1": -8.5,
-        "net1": -4.1, "head1": 2.0, "score1": -2.5, "end1": -1.2, "tab": -3.6}
-ND = 2
+LEAD = 6.0
+SLACK = 3.0
+PASSES = 4
+BIAS = {"end1": 2.1, "score0": -2.5, "set": 3.4, "fin1": 1.2, "fin0": 2.6, "run0": 2.3, "nt": 0.7, "pre0": 0.5, "pre1": 0.5,
+        "count": 0.3, "gt": -0.4, "end0": 0.3, "head1": -0.2, "tab": -0.4, "net0": 0.3}
+ENG = {"off": "v", "e15": "a", "slot": "a", "yi": "a", "ui": "a", "vl": "v", "ne": "v", "xl": "a", "sh": "v", "c16": "a",
+       "cf": "a", "wb": "a", "wo": "a", "sx": "a", "ci": "a", "ret": "a", "nret": "a", "so": "v", "ng": "v", "eh": "a", "sg": "v"}
+NTV = 2
 
 SCRATCH = {}
 SEMAPHORES = ["qv", "qa", "qt", "qg"] + ["d%d" % i for i in range(NDMA)]
@@ -36,24 +45,27 @@ def _buf(name, cols, dtype, where="sbuf"):
     LOG[name] = (where, cols, dtype, t, o)
 
 
-for _n in ("er", "gt", "nt", "tq"):
+for _n in ("er", "gt", "nt", "tq", "tcl", "tsg"):
     _buf(_n, W, "bfloat16")
 for _n in ("ip", "ic", "gp", "gc", "kp", "kc"):
     _buf(_n, 128, "int32")
-for _n in ("dd", "cc", "pp", "ns", "eye", "blk", "str", "tri", "first", "half", "shd", "sh1", "sh2", "sh4", "sh8", "neg",
-           "i4", "im85", "i512", "i71", "i72", "i2048", "mt", "mth", "mr", "blkz", "ones", "nblk", "blk4", "e0"):
+for _n in ("dd", "pp", "ns", "eye", "blk", "tri", "shd", "sh1", "sh2", "sh4", "sh8", "neg", "e16", "n16", "ial", "hneg", "i13",
+           "n2048", "mt", "mth", "nblk", "hblk", "blk32", "blkk", "e0", "e1", "r1", "r2", "tmp"):
     _buf(_n, 128, "bfloat16")
-_buf("wk", 16 * 128, "bfloat16")
-_buf("thf", 128, "float32")
-_buf("allo", 128, "float32")
-for _n in ("kcol", "kap", "cq", "k16", "thr", "m1c"):
+_buf("msk", 256, "bfloat16")
+_buf("al", CA // NP, "bfloat16")
+_buf("cb", 128, "float16")
+_buf("cb2", 128, "float16")
+for _n in ("thf", "all1", "all16"):
+    _buf(_n, 128, "float32")
+for _n in ("kcol", "kap", "thr", "m1c", "m2c"):
     _buf(_n, 8, "float32")
 _buf("rci", 8, "int32")
 _buf("xbase", 2 * NJ, "bfloat16")
 _buf("xbi", NJ, "int32")
+_buf("stl", 16, "uint16")
 _buf("bari", 256, "int32")
-_buf("barb", 256, "bfloat16")
-for _n in ("bark", "sti", "sth", "stc"):
+for _n in ("barb", "sti", "sth", "stc", "stn"):
     _buf(_n, 256, "bfloat16")
 _buf("actk", 256, "int32")
 _buf("whyk", 256, "int32")
@@ -67,18 +79,18 @@ for _c in range(NCH):
         _buf("so%d_%d" % (_t, _c), LC, "bfloat16")
         _buf("ac%d_%d" % (_t, _c), 8, "float32")
     _buf("gb%d" % _c, CA + 16, "bfloat16")
-    for _n in ("kb", "zb", "fl", "cg", "hb"):
+    for _n in ("zb", "fl", "cg", "hb"):
         _buf("%s%d" % (_n, _c), CA, "bfloat16")
-    for _n in ("e15", "k15", "t15", "val", "h8", "ov", "X", "zx", "nx", "hx", "w8", "f1", "T", "D", "pw", "pv", "eq", "M",
-               "insi", "nin", "xi", "ret", "qe", "go", "fm", "rb", "ar", "eo", "ne", "cl", "hh", "ng"):
+    for _n in ("e15", "h", "q", "um", "ov", "st", "XL", "X", "zx", "nx", "w8", "f1", "T", "M", "ins", "ret", "nret", "ne", "keep", "fm",
+               "eo", "eh", "nw", "cl", "sg", "ng"):
         _buf("%s_%d" % (_n, _c), LC, "bfloat16")
-    for _n in ("ds", "cf", "mc", "iv", "iq"):
+    for _n in ("xs", "ds", "cf", "mc", "iqe", "fi", "fw", "mx", "iv"):
         _buf("%s_%d" % (_n, _c), LC, "float16")
-    for _n in ("a1", "a2", "m0", "m1", "m2", "m3", "wb", "fi", "xq"):
+    for _n in ("a1", "a2", "m0", "m1", "m2", "m3", "wb", "xm"):
         _buf("%s_%d" % (_n, _c), 2 * LC, "float16")
-    for _n in ("f4", "y7", "pr", "sh", "sm", "ci", "ri", "mk", "eh"):
+    for _n in ("yi", "y7", "pr", "sh", "sm", "ci", "cn", "k0", "k1", "k2", "k3"):
         _buf("%s_%d" % (_n, _c), LC, "int32")
-    for _n in ("tj", "sx", "tb"):
+    for _n in ("ab", "ln", "sx"):
         _buf("%s_%d" % (_n, _c), LC, "float32")
     for _n in ("off", "c16"):
         _buf("%s_%d" % (_n, _c), LC, "uint16")
@@ -117,12 +129,17 @@ def rank_program(g, core, T, topo):
         n = LOG[name][1] if name in LOG else T[name].shape[1]
         return (name, 0 if a is None else a, n if b is None else b, st, p)
 
+    def rev(r):
+        return (r[0], r[1], r[2], -1, None)
+
     def ap(r):
         t, o = (LOG[r[0]][3], LOG[r[0]][4]) if r[0] in LOG else (r[0], 0)
         if r[4] is not None:
             return T[t][r[4][0]:r[4][1]:r[4][2], o + r[1]:o + r[2]]
         if r[3] > 1:
             return T[t][:, o + r[1]:o + r[2]:r[3]]
+        if r[3] < 0:
+            return T[t][:, o + r[2] - 1:o + r[1] - 1:-1]
         return T[t][:, o + r[1]:o + r[2]]
 
     def ind(win, off):
@@ -136,9 +153,9 @@ def rank_program(g, core, T, topo):
         return r
 
     def n_of(r):
-        return -(-(r[2] - r[1]) // r[3])
+        return -(-(r[2] - r[1]) // abs(r[3]))
 
-    def add(q, fns, reads, writes, cost, kind="c", lat=0.0, sem=None, inc=0, extra=()):
+    def add(q, fns, reads, writes, cost, kind="c", lat=0.0, sem=None, inc=0, extra=(), soft=()):
         i = len(ops)
         rd = []
         for r in reads:
@@ -166,8 +183,16 @@ def rank_program(g, core, T, topo):
                 if isw and r[3] == 1 and r[4] is None and r[0] not in PS:
                     cur[:] = [e for e in cur if not (e[1][1] >= r[1] and e[1][2] <= r[2])]
                 cur.append((i, r, isw))
-        ops.append({"ph": PH[0], "q": q, "fns": fns, "deps": deps, "cost": cost, "kind": kind, "lat": lat, "sem": sem, "inc": inc})
+        deps |= set(soft)
+        ops.append({"ph": PH[0], "nm": wr[0][0] if wr else "", "q": q, "fns": fns, "deps": deps, "cost": cost, "kind": kind,
+                    "lat": lat, "sem": sem, "inc": inc, "soft": set(soft)})
         return i
+
+    def chain(row):
+        for a, b in zip(row, row[1:]):
+            if a not in ops[b]["deps"]:
+                ops[b]["deps"].add(a)
+                ops[b]["soft"].add(a)
 
     def two(*rs):
         return all(isinstance(r, tuple) and r[0] in LOG and LOG[r[0]][2] in ("bfloat16", "float16", "uint16") and r[0] not in PS for r in rs)
@@ -194,14 +219,15 @@ def rank_program(g, core, T, topo):
         return add("v", [lambda: g.vector.tensor_copy(x(out), x(a))], [a], [out], vc(n_of(a), rate))
 
     def fill(out, v):
-        add("v", [lambda: g.vector.memset(x(out), v)], [], [out], 0.1)
+        add("v", [lambda: g.vector.memset(x(out), v)], [], [out], vc(n_of(out), 0.5 if two(out) else 1.0))
 
-    def scan(out, d0, d1):
-        add("v", [lambda: g.vector.tensor_tensor_scan(x(out), x(d0), x(d1), 0.0, A.mult, A.add)], [d0, d1], [out], vc(n_of(out), 0.5))
+    def scan(out, d0, d1, op1):
+        return add("v", [lambda: g.vector.tensor_tensor_scan(x(out), x(d0), x(d1), 0.0, A.mult, op1)], [d0, d1], [out],
+                   vc(n_of(out), 0.5 if two(out, d0, d1) else 1.0))
 
     def act(out, a, func, bias=None, scale=None, accum=None):
         kw = {}
-        if func == F.Copy and (bias is not None or scale is not None):
+        if func == F.Copy and (bias is not None or scale is not None or accum is not None):
             func = F.Identity
         if bias is not None:
             kw["bias"] = bias
@@ -213,14 +239,24 @@ def rank_program(g, core, T, topo):
         return add("a", [lambda: g.scalar.activation(x(out), x(a), func, **{k: x(v) for k, v in kw.items()})], [a, bias, scale],
                    [out] + ([accum] if accum is not None else []), 0.04 + max(64, n_of(out) * rate) * CY)
 
-    def mm(items):
+    def aff(nm, out, a, scale=None, bias=None):
+        if ENG[nm] == "a":
+            return act(out, a, F.Copy, bias, scale)
+        if scale is None:
+            return cp(out, a) if bias is None else ts(out, a, bias, A.add)
+        return ts(out, a, scale, A.mult) if bias is None else ts(out, a, scale, A.mult, bias, A.add)
+
+    def mm(items, soft=()):
         fns, rd, wr, cost = [], [], [], 0.02
         for (o, l, r, s, e) in items:
             fns.append(lambda o=o, l=l, r=r, s=s, e=e: g.tensor.matmul(x(o), x(l), x(r), s, e))
             rd += [l, r]
             wr.append(o)
             cost += max(64, n_of(r)) * CY * (4 if LOG[r[0]][2] == "float32" else 1)
-        return add("t", fns, list(dict.fromkeys(rd)), list(dict.fromkeys(wr)), cost)
+        return add("t", fns, list(dict.fromkeys(rd)), list(dict.fromkeys(wr)), cost, soft=soft)
+
+    def msum(o, terms):
+        return mm([(t[2] if len(t) > 2 else o, t[0], t[1], q == 0, q == len(terms) - 1) for q, t in enumerate(terms)])
 
     def dma(q, out, a):
         s = "d%d" % dn[0]
@@ -236,18 +272,8 @@ def rank_program(g, core, T, topo):
         i = add("g", [lambda: g.remote_dma(ap(out), ap(a), ra, la, pid, rid, m)], [a], [], 1.2, "r", 2.5, "l" + tag, ne)
         return add("x", [], [], [out], 0.0, "x", 0.0, "a" + tag, ne, (i,))
 
-    ring = [[0] for _ in range(NCH)]
-
-    def bank(c):
-        i = ring[c][0]
-        ring[c][0] = (i + 1) % (NB - 2)
-        return "p%d" % (c * NB + i)
-
-    def nbank(c):
-        return "p%d" % (c * NB + NB - 2)
-
-    def wbank(c):
-        return "p%d" % (c * NB + NB - 1)
+    def P(c, i, a=0, n=LC, st=1):
+        return R("p%d" % (4 * c + i), a, a + n, st)
 
     def lanes(q, buf, name, r0, r1):
         for r in range(r0, r1):
@@ -259,7 +285,7 @@ def rank_program(g, core, T, topo):
     for j in range(4):
         dma("s", R("tq", 1024 * j, 1024 * j + 1024), R("req", 1024 * j, 1024 * j + 1024))
     lanes("s", "actk", "act", 16 // NCH, 16)
-    fill(R("bari"), 0)
+    fill(R("bari"), 1)
     dma("s", R("bari", None, None, 1, (0, 128, 16)), R("bar"))
     lanes("s", "whyk", "why", 0, 16)
 
@@ -270,287 +296,293 @@ def rank_program(g, core, T, topo):
     iota(R("xbi"), [[256, NJ]], 0, 0)
     for c in range(NCH):
         iota(R("vb_%d" % c), [[16, NJ]], LC * c, 0)
+    tt(R("eye"), R("ip"), R("ic"), A.is_equal)
+    for nm, f in (("e16", 1.0 / 16), ("n16", -1.0 / 16), ("neg", -1.0), ("ial", 2.0 ** -AGE), ("hneg", -0.5), ("i13", 13.0 / 16), ("n2048", -2048.0)):
+        act(R(nm), R("eye"), F.Copy, None, f)
     ts(R("gp"), R("ip"), 4, A.arith_shift_right)
     ts(R("gc"), R("ic"), 4, A.arith_shift_right)
     ts(R("kp"), R("ip"), 15, A.bitwise_and)
     ts(R("kc"), R("ic"), 15, A.bitwise_and)
     tt(R("blk"), R("gp"), R("gc"), A.is_equal)
     ts(R("ns"), R("blk"), -64.0, A.mult, 64.0, A.add)
-    tt(R("cc"), R("kc"), R("ns"), A.add)
     tt(R("pp"), R("kp"), R("ns"), A.add)
     tt(R("dd"), R("kc"), R("pp"), A.subtract)
-    ts(R("eye"), R("dd"), 0.0, A.is_equal)
-    ts(R("str"), R("dd"), 1.0, A.is_ge)
     ts(R("tri"), R("dd"), 0.0, A.is_ge)
     for nm, de in (("shd", 1.0), ("sh1", -1.0), ("sh2", -2.0), ("sh4", -4.0), ("sh8", -8.0)):
-        ts(R("hb0", 0, 128), R("dd"), de, A.is_equal)
-        tt(R(nm), R("hb0", 0, 128), R("eye"), A.subtract)
-    for nm, f in (("neg", -1.0), ("i4", 4.0), ("im85", -8.5), ("i512", -512.0), ("i71", 71.5), ("i72", 72.0), ("i2048", 2048.0)):
-        act(R(nm), R("eye"), F.Copy, None, f)
-    ts(R("mt"), R("str"), -32.0, A.mult)
-    tt(R("first"), R("mt"), R("eye"), A.add)
-    ts(R("half"), R("first"), 0.5, A.mult)
-    ts(R("mr"), R("eye"), -64.0, A.mult)
-    tt(R("mr"), R("mr"), R("str"), A.add)
+        ts(R("tmp"), R("dd"), de, A.is_equal)
+        tt(R(nm), R("tmp"), R("eye"), A.subtract)
     ts(R("e0"), R("pp"), 0.0, A.is_equal)
-    ts(R("mt"), R("sh1"), -2.0, A.mult)
-    tt(R("mt"), R("mt"), R("e0"), A.subtract)
-    ts(R("thf"), R("dd"), 5.0, A.min, 8.0 * LN2, A.mult)
+    ts(R("e1"), R("pp"), 1.0, A.is_equal)
+    ts(R("mt"), R("e0"), 0.5, A.mult)
+    tt(R("mt"), R("mt"), R("sh1"), A.add)
+    ts(R("thf"), R("dd"), 2.0, A.min, AGE * LN2, A.mult)
     ts(R("kcol", 0, 1), R("kp", 0, 1), 1.0, A.mult)
     BC = {}
-    for q, (nm, v) in enumerate((("thj", 56.0 * LN2 + math.log(0.7)), ("w8", 60.0 * LN2), ("tb", 40.0 * LN2 + math.log(0.7 / 24.0)),
-                                 ("f4", -3.5), ("one", -1.0), ("hi", -11.5), ("pv", -40.0 * LN2))):
+    for q, (nm, v) in enumerate((("thj", AGE * LN2 + math.log(0.375)), ("one", -1.0), ("need", 46.0))):
         BC[nm] = R("m1c", q, q + 1)
         fill(BC[nm], v)
     act(R("mth"), R("thf"), F.Exp, BC["thj"])
-    ts(R("blkz"), R("blk"), 1.0 / 24.0, A.mult)
-    ts(R("blk4"), R("blk"), 4.0, A.mult)
-    ts(R("nblk"), R("blk"), -1.0, A.mult)
-    for k in range(16):
-        ts(R("wk", 128 * k, 128 * k + 128), R("cc"), float(k), A.is_equal)
+    for nm, f in (("nblk", -1.0), ("hblk", 0.5), ("blk32", 32.0), ("blkk", R("kcol", 0, 1))):
+        ts(R(nm), R("blk"), f, A.mult)
+    for h in range(2):
+        tt(R("msk", 128 * h, 128 * h + 128), R("kp"), R("kc"), A.is_equal)
+    ts(R("r1"), R("kc"), 1.0, A.is_ge)
+    ts(R("r2"), R("r1"), 2.0, A.mult)
+    ts(R("cb2"), R("kc"), -1.0 / 32, A.mult, -39.5, A.add)
+    tt(R("cb"), R("cb2"), R("e1"), A.mult)
+    tt(R("cb"), R("cb"), R("e0"), A.subtract)
+    fill(R("al"), 2.0 ** -AGE)
+    fill(R("al", 0, CA // NP, 16), 0.0)
     ts(R("kap", 0, 1), R("kcol", 0, 1), 241.0, A.mult, 101.0, A.add)
     for t in range(VI):
         ts(R("kap", 4 + t, 5 + t), R("kap", 0, 1), 2048.0, A.mult, float(97 * t), A.add)
-    ts(R("cq", 0, 1), R("kcol", 0, 1), -16.0, A.mult, 0.5, A.add)
-    ts(R("k16", 0, 1), R("kcol", 0, 1), -1.0, A.mult, 16.0, A.add)
+    ts(R("m2c", 0, 1), R("kcol", 0, 1), 15.0, A.is_equal, -0.5, A.add)
+    ts(R("m2c", 1, 2), R("kcol", 0, 1), 1.0, A.add)
     fill(R("thr", 0, 1), -1.5)
-    fill(R("ones"), 1.0)
-    fill(R("allo"), 1.0 / 16.0)
+    fill(R("all1"), 1.0)
+    fill(R("all16"), 1.0 / 16.0)
+    fill(R("tmp"), 1.0)
     ts(R("kcol", 2, 3), R("kcol", 0, 1), 16.0, A.mult)
     ts(R("xbase", 0, NJ), R("xbi"), R("kcol", 2, 3), A.add)
     fill(R("xbase", NJ, 2 * NJ), 2048.0)
+    ts(R("stl"), R("ic", 0, 16), R("kcol", 2, 3), A.add)
     ts(R("kcol", 4, 5), R("kcol", 0, 1), 256.0, A.mult)
     for c in range(NCH):
         ts(R("vb_%d" % c), R("vb_%d" % c), R("kcol", 4, 5), A.add)
     cp(R("barb"), R("bari"))
-    b = bank(0)
-    mm([(R(b, 0, 256), R("e0"), R("barb"), True, True)])
-    cp(R("bark"), R(b, 0, 256))
     for c in range(NCH):
         a0, a1 = c * LC, (c + 1) * LC
         ts(R("w0_%d" % c, 0, LC), R("actk", a0, a1), -2048.0, A.add)
         ts(R("w0_%d" % c, LC, 2 * LC), R("whyk", a0, a1), -2047.0, A.add)
-    ts(R("sth"), R("sti"), 8.0, A.is_ge, 144.0, A.mult)
-    tt(R("stc"), R("sti"), R("sth"), A.add)
-    for r in range(16):
-        c, o = divmod(16 * r, LC)
-        act(R("s0_%d" % c, o, o + 16), R("stc", r, 256, 16), F.Copy, -20.0)
+    ts(R("sth"), R("sti"), 8.0, A.is_lt, 25.0 / 16, A.mult)
+    ts(R("stn"), R("sti"), -1.0 / 16, A.mult, -5.0 / 16, A.add)
+    tt(R("stc"), R("stn"), R("sth"), A.add)
+    for c in range(NCH):
+        act(R("s0_%d" % c), ind(R("stc"), R("stl", c * NJ, (c + 1) * NJ)), F.Copy)
 
-    def code(dst, src, cl, hh, b, n):
-        ts(cl, src, 4.0, A.max, 11.0, A.min)
-        act(hh, src, F.Sign, BC["hi"])
-        mm([(R(b, 0, n), R("eye"), src, True, False), (R(b, 0, n), R("neg"), cl, False, False), (R(b, 0, n), R("i71"), hh, False, True)])
-        act(dst, R(b, 0, n), F.Copy, 63.5)
+    PH[0] = "gt"
     for j in range(8):
         c0, c1 = 512 * j, 512 * j + 512
-        d = 512 * (j % 4)
-        if j >= 8 - ND:
-            n1, n2 = R("fl%d" % (j % 2), d, d + 512), R("cg%d" % (j % 2), d, d + 512)
-            ts(n1, R("er", c0, c1), 4.0, A.max, 11.0, A.min)
-            tt(n2, R("er", c0, c1), n1, A.subtract)
-            ts(n1, R("er", c0, c1), 12.0, A.is_ge, 143.0, A.mult)
-            tt(n2, n2, n1, A.add)
-            ts(R("gt", c0, c1), n2, -8.0, A.add)
-            continue
-        code(R("gt", c0, c1), R("er", c0, c1), R("kb%d" % (j // 4), d, d + 512), R("zb%d" % (j // 4), d, d + 512), bank(j % 2), 512)
+        b = R("p%d" % j)
+        ts(R("tcl", c0, c1), R("er", c0, c1), 4.0, A.max, 11.0, A.min)
+        msum(b, [(R("n16"), R("er", c0, c1)), (R("e16"), R("tcl", c0, c1))])
+        act(R("tsg", c0, c1), b, F.Sign)
+        tt(R("gt", c0, c1), R("tsg", c0, c1), b, A.add)
+    PH[0] = "nt"
     for j in range(4):
         c0, c1 = 1024 * j, 1024 * j + 1024
-        ts(R("nt", c0, c1), R("tq", c0, c1), 12.0, A.is_lt, -BIG, A.mult)
+        if j < NTV:
+            ts(R("nt", c0, c1), R("tq", c0, c1), 12.0, A.is_lt, 4.0, A.mult)
+        else:
+            act(R("nt", c0, c1), R("tq", c0, c1), F.Relu, BC["need"], -4.0)
+
+    def pick(o, xm, n):
+        return [(R(xm, q * LC, (q + 1) * LC), R("blk", 0, 128, 16), R(o[0], o[1] + q * NJ, o[1] + (q + 1) * NJ)) for q in range(n)]
+
+    def cut(a, b, n):
+        return [(a + (b - a) * i // n, a + (b - a) * (i + 1) // n) for i in range(n)]
 
     def run(t, c):
         def K(n, *a):
             return R("%s_%d" % (n, c), *a)
         PH[0] = "run%d" % c
-        gb, kb, zb, fl = "gb%d" % c, "kb%d" % c, "zb%d" % c, "fl%d" % c
+        gb, zb, fl = "gb%d" % c, "zb%d" % c, "fl%d" % c
         w, s = "w%d_%d" % (t, c), "s%d_%d" % (t, c)
-        ts(K("off"), R(w, 0, LC), 2048.0, A.add)
-        b = bank(c)
+        aff("off", K("off"), R(w, 0, LC), None, 2048.0)
+        ra, rv = [], []
         for p in range(NP):
             l0, l1 = p * LC // NP, (p + 1) * LC // NP
             e0, e1 = 16 * l0, 16 * l1
-            act(R(gb, e0 + 1, e1 + 1), ind(R("gt"), K("off", l0, l1)), F.Copy)
-            act(K("e15", l0, l1), R(gb, e0 + 16, e1 + 1, 16), F.Copy, 4.0)
-            act(R(gb, e0, e1, 16), R(s, l0, l1), F.Copy)
-            ts(R(kb, e0, e1), R(gb, e0, e1), -8.0, A.is_equal)
-            scan(R(zb, e0, e1), R(kb, e0, e1), R(gb, e0, e1))
-            tt(R(fl, e0, e1), ind(R("nt"), K("off", l0, l1)), R(zb, e0, e1), A.is_gt)
-            mm([(R(b, l0, l1), R("wk", 128 * k, 128 * k + 128), R(fl, e0 + k, e1, 16), k == 0, k == 15) for k in range(16)])
-        act(K("ov"), R(b, 0, LC), F.Sign, R("thr", 0, 1))
+            for (a0, a1) in cut(l0, l1, NG):
+                ra.append(act(R(gb, 16 * a0 + 1, 16 * a1 + 1), ind(R("gt"), K("off", a0, a1)), F.Copy))
+            aff("e15", K("e15", l0, l1), R(gb, e0 + 16, e1 + 1, 16))
+            aff("slot", R(gb, e0, e1, 16), R(s, l0, l1))
+            rv.append(scan(R(zb, e0, e1), R("al"), R(gb, e0, e1), A.add))
+            for (a0, a1) in cut(l0, l1, NF):
+                rv.append(tt(R(fl, 16 * a0, 16 * a1), ind(R("nt"), K("off", a0, a1)), R(zb, 16 * a0, 16 * a1), A.is_lt))
+        chain(ra)
+        chain(rv)
+        mm([(P(c, 1, k, 128 - k, 16), R(fl, k, CA, 16), R("blk", 0, 128, 16), True, True) for k in range(16)])
+        act(K("ov"), P(c, 1), F.Sign, R("thr", 0, 1))
         PH[0] = "end%d" % c
-        nb = nbank(c)
-        o = R(nb, 0, LC)
-        ts(K("k15"), K("e15"), -4.0, A.is_equal)
-        tt(K("t15"), K("k15"), R(zb, 15, CA, 16), A.mult)
-        mm([(o, R("eye"), K("t15"), True, False), (o, R("eye"), K("e15"), False, True)])
-        cp(K("f4"), o)
-        act(K("h8"), o, F.Sign, BC["f4"])
-        ts(K("y7"), K("f4"), 7, A.bitwise_and)
-        mm([(o, R("i4"), K("h8"), True, False), (o, R("i4"), R("ones", 0, LC), False, True)])
-        tt(K("val"), K("y7"), o, A.add)
+        o = P(c, 2)
+        msum(o, [(R("ial"), R(zb, 15, CA, 16)), (R("eye"), K("e15"))])
+        act(K("ab"), o, F.Abs)
+        act(K("h"), o, F.Sign)
+        act(K("ln"), K("ab"), F.Ln, None, 2.0 ** (8 * AGE))
+        aff("yi", K("yi"), K("ln"), LA / LN2, -LA * math.log2(13.0 / 16) - 0.21)
+        ts(K("y7"), K("yi"), 7, A.bitwise_and)
+        tt(K("q"), K("y7"), K("h"), A.mult)
         if t < VI - 1:
-            mm([(o, R("eye"), K("val"), True, False), (o, R("i72"), K("h8"), False, True)])
-            act(R("so%d_%d" % (t, c)), o, F.Copy, 52.0)
+            o = P(c, 2, LC)
+            msum(o, [(R("e16"), K("q")), (R("i13"), K("h"))])
+            aff("so", R("so%d_%d" % (t, c)), o)
             remote("s%d_%d" % (t, c), R("s%d_%d" % (t + 1, c)), R("so%d_%d" % (t, c)))
-        o = R(nb, 0, NJ)
-        mm([(o, R("wk", 128 * r, 128 * r + 128), R("val_%d" % c, r, LC, 16), r == 0, r == 15) for r in range(16)])
-        cp(K("ui"), o)
+        o = P(c, 2, 2 * LC)
+        msum(o, [(K("q"), R("blk")), (K("h"), R("hblk"))])
+        tt(K("um"), o, R("msk", 0, LC), A.mult)
+        o = P(c, 2, 3 * LC, NJ)
+        msum(o, pick(o, "um_%d" % c, 1))
+        aff("ui", K("ui"), o, -1.0, 120.0)
         ts(K("uj"), K("ui"), 15, A.bitwise_and)
         tt(K("uk"), K("uj"), K("vb"), A.add)
-        cp(K("vl"), K("uk"))
+        aff("vl", K("vl"), K("uk"))
         act(K("eo"), ind(R("er"), K("vl")), F.Copy)
-        o = R(nb, 0, LC)
-        mm([(o, R("eye"), K("eo"), True, False), (o, R("eye"), K("val"), False, True)])
-        ts(K("eh"), o, 0.5, A.mult, -0.25, A.add)
-        cp(K("ne"), K("eh"))
+        o = P(c, 2)
+        msum(o, [(R("eye"), K("eo")), (R("neg"), K("q")), (R("hneg"), K("h"))])
+        aff("eh", K("eh"), o, 0.5, 195.5)
+        aff("ne", K("nw"), K("eh"), None, -192.0)
         if t < VI - 1:
-            code(K("ng"), K("ne"), K("cl"), K("hh"), nb, LC)
-        cp(ind(R("er"), K("vl")), K("ne"))
+            ts(K("cl"), K("eh"), 196.0, A.max, 203.0, A.min)
+            aff("sg", K("sg"), K("eh"), 0.125, 167.0625)
+            o = P(c, 2, LC)
+            msum(o, [(R("n16"), K("eh")), (R("e16"), K("cl")), (R("neg"), K("sg"))])
+            aff("ng", K("ng"), o, None, 192.0)
+        else:
+            cp(ind(R("er"), K("vl")), K("nw"))
 
-    def table(t, c):
+    def table(t, c, tab, new):
         PH[0] = "tab"
         if t < VI - 1:
-            cp(ind(R("gt"), R("vl_%d" % c)), R("ng_%d" % c))
+            cp(ind(R(tab), R("vl_%d" % c)), R("%s_%d" % (new, c)))
 
     def cand(t, c):
         def K(n, *a):
             return R("%s_%d" % (n, c), *a)
         PH[0] = "head%d" % c
         w = "w%d_%d" % (t, c)
-        S_, Q_ = R(w, 0, LC), R(w, LC, 2 * LC)
-        pw, nb = wbank(c), nbank(c)
-        wp, n2 = R(pw, 0, 2 * LC), R(nb, 0, 2 * LC)
-        mm([(wp, R("eye"), R(w, 0, 2 * LC), True, True)])
-        wS = R(pw, 0, LC)
-        b = bank(c)
-        mm([(R(b, 0, LC), R("half"), K("ov"), True, True)])
-        act(K("X"), R(b, 0, LC), F.Relu, R("cq", 0, 1))
-        ts(K("xq", 0, LC), K("X"), R("kcol", 0, 1), A.mult)
-        tt(K("xq", LC, 2 * LC), K("X"), wS, A.mult)
-        b = bank(c)
-        mm([(R(b, 0, 2 * NJ), R("wk", 128 * r, 128 * r + 128), R("xq_%d" % c, r, 2 * LC, 16), r == 0, False) for r in range(16)]
-           + [(R(b, 0, 2 * NJ), R("eye"), R("xbase"), False, True)])
-        cp(K("xl"), R(b, 0, 2 * NJ))
-        b = bank(c)
-        mm([(R(b, 0, LC), R("mth"), K("X"), True, True)])
-        act(K("tj"), R(b, 0, LC), F.Copy)
+        W_, S_, Q_ = R(w), R(w, 0, LC), R(w, LC, 2 * LC)
+        ac = "ac%d_%d" % (t, c)
+        scan(K("st"), R("r2"), K("ov"), A.max)
+        ts(K("XL"), K("st"), 1.0, A.is_equal)
+        o = P(c, 0)
+        msum(o, [(K("XL"), R("eye"))])
+        act(K("X"), o, F.Copy, accum=R(ac, 0, 1) if t < VI - 1 else None)
+        tt(K("xs"), S_, o, A.mult)
+        mm([(P(c, 1, LC), K("X"), R("blkk"), True, True), (P(c, 1, 2 * LC), K("xs"), R("blk"), True, True)])
+        tt(K("xm"), P(c, 1, LC, 2 * LC), R("msk"), A.mult)
+        o = P(c, 0, LC, 2 * NJ)
+        msum(o, [(R("eye"), R("xbase"))] + pick(o, "xm_%d" % c, 2))
+        aff("xl", K("xl"), o)
+        sx, kap = P(c, 3, 2 * LC), P(c, 3, 3 * LC)
+        msum(sx, [(R("blk"), K("xs"))])
+        aff("sx", K("sx"), sx, None, 2048.0)
+        act(kap, sx, F.Copy, R("kap", 4 + t, 5 + t), R("kap", 0, 1))
         act(K("zx"), ind(R("zb%d" % c), K("xl", 0, NJ)), F.Copy)
         act(K("nx"), ind(R("nt"), K("xl", NJ, 2 * NJ)), F.Copy)
-        ts(K("hx"), K("zx"), 0.0, A.is_ge)
-        b = bank(c)
-        mm([(R(b, 0, LC), R("eye"), K("zx"), True, False), (R(b, 0, LC), R("i512"), K("hx"), False, False), (R(b, 0, LC), R("eye"), K("nx"), False, True)])
-        act(K("w8"), R(b, 0, LC), F.Exp, BC["w8"], LN2)
-        ts(K("f1"), K("w8"), 0.0, A.is_gt)
-        b = bank(c)
-        mm([(R(b, 0, LC), R("blk"), K("w8"), True, True)])
-        tt(K("T"), R(b, 0, LC), K("tj"), A.is_ge)
-        b = bank(c)
-        mm([(R(b, 0, LC), R("mt"), K("T"), True, False), (R(b, 0, LC), R("eye"), K("X"), False, True)])
-        act(K("D"), R(b, 0, LC), F.Relu)
-        tt(K("ds"), K("D"), wS, A.mult)
-        b = bank(c)
-        mm([(R(b, 0, LC), R("blk"), K("xq", LC, 2 * LC), True, True)])
-        mm([(R(b, LC, 2 * LC), R("blk"), K("ds"), True, True)])
-        mm([(R(pw, 2 * LC, 3 * LC), R("blk"), K("ds"), True, False), (R(pw, 2 * LC, 3 * LC), R("eye"), R("ones", 0, LC), False, True)])
-        act(K("sx"), R(b, 0, LC), F.Copy, 2048.0)
-        act(R(b, 2 * LC, 3 * LC), R(b, 0, LC), F.Copy, R("kap", 4 + t, 5 + t), R("kap", 0, 1))
-        tt(K("pr"), R(b, LC, 2 * LC), K("sx"), A.mult)
-        ts(K("sh"), K("pr"), 5, A.arith_shift_right)
-        tt(K("sm"), K("sh"), R(b, 2 * LC, 3 * LC), A.add)
+        o = P(c, 1)
+        msum(o, [(R("eye"), K("zx")), (R("neg"), K("nx"))])
+        act(K("w8"), o, F.Relu)
+        act(K("f1"), o, F.Sign)
+        o = P(c, 0, 2 * LC)
+        msum(o, [(R("mth"), K("X")), (R("nblk"), K("w8"))])
+        act(K("T"), o, F.Sign)
+        D = P(c, 3)
+        msum(D, [(R("eye"), K("X")), (R("mt"), K("T"))])
+        act(D, D, F.Relu, R("m2c", 0, 1))
+        tt(K("ds"), S_, D, A.mult)
+        sda, sdp = P(c, 3, LC), P(c, 3, 2 * LC)
+        msum(sda, [(R("blk"), K("ds"))])
+        tt(K("pr"), sda, K("sx"), A.mult)
+        if ENG["sh"] == "a":
+            act(K("sh"), K("pr"), F.Copy, -31.0 / 64, 1.0 / 32)
+        else:
+            ts(K("sh"), K("pr"), 5, A.arith_shift_right)
+        tt(K("sm"), K("sh"), kap, A.add)
         ts(K("ci"), K("sm"), 4095, A.bitwise_and)
-        cp(K("c16"), K("ci"))
+        aff("c16", K("c16"), K("ci"))
         PH[0] = "net%d" % c
 
         def prod(n, wd, mask):
             tt(K(n, 0, LC), R(wd[0], wd[1], wd[1] + LC), mask, A.mult)
             tt(K(n, LC, 2 * LC), R(wd[0], wd[1] + LC, wd[1] + 2 * LC), mask, A.mult)
-        ts(K("cf"), K("ci"), -2048.0, A.add)
-        tt(K("qe"), Q_, R(pw, 2 * LC, 3 * LC), A.is_equal)
-        o = R(nb, 0, LC)
-        mm([(o, R("eye"), K("D"), True, False), (o, R("eye"), K("qe"), False, False), (o, R("blk4"), K("X"), False, True)])
-        ts(K("go"), o, 4.5, A.is_ge)
-        pr = R(nb, LC, 2 * LC)
-        mm([(o, R("blk"), K("go"), True, True), (pr, R("mr"), K("go"), True, True)])
-        act(K("rb"), pr, F.Relu)
-        ts(K("fm"), o, R("k16", 0, 1), A.is_ge)
-        o2 = R(nb, 2 * LC, 3 * LC)
-        mm([(o2, R("tri"), K("X"), True, True)])
-        tt(K("a1", 0, LC), S_, o2, A.mult)
-        tt(K("a1", LC, 2 * LC), Q_, o2, A.mult)
-        tt(K("iq"), K("X"), R(pw, 2 * LC, 3 * LC), A.mult)
-        prod("a2", wp, K("go"))
-        tt(K("fi", 0, LC), K("fm"), K("cf"), A.mult)
-        ts(K("fi", LC, 2 * LC), K("fm"), -2048.0, A.mult)
-        base, moves = R(w, 0, 2 * LC), [("neg", "a2")]
+        wp = [P(c, 2, 0, 2 * LC), P(c, 2, 2 * LC, 2 * LC)]
+        aff("cf", K("cf"), K("ci"), None, -2048.0)
+        msum(sdp, [(R("eye"), R("tmp")), (R("blk"), K("ds"))])
+        msum(wp[0], [(R("eye"), W_)])
+        tt(K("ne"), Q_, sdp, A.not_equal)
+        tt(K("keep"), K("ne"), D, A.is_gt)
+        tt(K("iqe"), K("X"), sdp, A.mult)
+        mm([(P(c, 2, 2 * LC), R("tri"), K("keep"), True, True), (P(c, 2, 3 * LC), R("blk"), K("keep"), True, True)])
+        aff("ci", K("cn"), P(c, 2, 2 * LC), -1.0, R("m2c", 1, 2))
+        ts(K("fm"), P(c, 2, 3 * LC), R("kcol", 0, 1), A.is_le)
+        prod("a2", wp[0], K("keep"))
         for s in range(4):
-            ts(K("ri"), pr, 0.0, A.max)
-            ts(K("mk"), K("ri"), s, A.arith_shift_right, 1, A.bitwise_and)
-            prod("m%d" % s, wp, K("mk"))
-            moves.append(("sh%d" % (1 << s), "m%d" % s))
-            if s < 3:
-                tt(K("ar"), pr, K("mk"), A.mult)
-                pr = R(nb, ((s + 2) % 4) * LC, ((s + 2) % 4 + 1) * LC)
-                mm([(pr, R("eye"), K("rb"), True, False), (pr, R("sh%d" % (1 << s)), K("ar"), False, True)])
-                if s < 2:
-                    act(K("rb"), pr, F.Copy)
-            if s == 3:
-                moves += [("eye", "fi")]
-            mm([(wp, R("eye"), base, True, False)] + [(wp, R(m), K(a), False, q == len(moves) - 1) for q, (m, a) in enumerate(moves)])
-            if s == 1:
-                cp(K("wb"), wp)
-                base, moves = K("wb"), []
-        mm([(n2, R("eye"), R(w, 0, 2 * LC), True, False), (n2, R("shd"), K("a1"), False, False),
-            (R(nb, LC, 2 * LC), R("eye"), K("iq"), False, True)])
+            ts(K("k%d" % s), K("cn"), s, A.arith_shift_right, 1, A.bitwise_and)
+        tt(K("fi"), K("fm"), K("cf"), A.mult)
+        terms = [(R("eye"), K("a2"))]
+        for s in range(4):
+            cur = wp[(s + 1) % 2]
+            msum(cur, terms)
+            if s == 2:
+                aff("wb", K("wb"), cur)
+                terms = [(R("eye"), K("wb"))]
+            prod("m%d" % s, cur, K("k%d" % s))
+            terms.append((R("sh%d" % (1 << s)), K("m%d" % s)))
+        rw = wp[1]
+        msum(rw, terms + [(R("eye"), K("fi"), P(c, 2, 2 * LC)), (R("n2048"), K("fm"), P(c, 2, 3 * LC))])
+        PH[0] = "pre%d" % c
+        msum(sda, [(R("tri"), K("X"))])
+        tt(K("a1", 0, LC), S_, sda, A.mult)
+        tt(K("a1", LC, 2 * LC), Q_, sda, A.mult)
+        iw = P(c, 3, 0, 2 * LC)
+        msum(iw, [(R("eye"), W_), (R("shd"), K("a1")), (R("eye"), K("iqe"), P(c, 3, LC))])
         PH[0] = "score%d" % c
         hb, cg = "hb%d" % c, "cg%d" % c
-        rb_ = bank(c)
-        rr = R(rb_, 0, LC)
-        mm([(rr, R("im85"), K("hx"), True, False), (rr, R("eye"), K("nx"), False, True)])
-        b = bank(c)
-        mm([(R(b, 0, LC), R("nblk"), K("f1"), True, False), (R(b, 0, LC), R("eye"), R("bark", c * LC, (c + 1) * LC), False, True)])
-        act(K("tb"), R(b, 0, LC), F.Exp, BC["tb"], 5.0 * LN2)
-        act(R(cg), ind(R("gt"), K("c16")), F.Copy)
-        for m in range(16):
-            tt(R(hb, m * LC, (m + 1) * LC), R(cg, m, CA, 16), rr, A.is_gt)
-        mm([(R(b, m, 128, 16), R(hb, m * LC, (m + 1) * LC), R("blk", 0, 128, 16), True, True) for m in range(16)])
-        act(K("pv"), R(b, 0, LC), F.Exp, BC["pv"], 5.0 * LN2)
-        mm([(R(b, LC, 2 * LC), K("pv"), R("eye"), True, True)])
-        act(K("pw"), R(b, LC, 2 * LC), F.Copy)
-        mm([(rr, R("blkz"), K("pw"), True, True)])
-        tt(K("eq"), rr, K("pw"), A.is_le)
-        tt(K("insi"), rr, K("tb"), A.is_ge)
-        tt(K("nin"), rr, K("tb"), A.is_lt)
-        b = bank(c)
-        mm([(R(b, 0, LC), R("first"), K("eq"), True, True)])
-        act(K("M"), R(b, 0, LC), F.Relu)
-        mm([(R(b, 2 * LC, 3 * LC), R("eye"), K("X"), True, False), (R(b, 2 * LC, 3 * LC), R("eye"), K("insi"), False, True),
-            (R(b, 3 * LC, 4 * LC), R("blk"), K("X"), True, False), (R(b, 3 * LC, 4 * LC), R("neg"), K("insi"), False, True)])
-        act(K("xi"), R(b, 2 * LC, 3 * LC), F.Relu, BC["one"])
-        if t < VI - 1:
-            act(K("ret"), R(b, 3 * LC, 4 * LC), F.Relu, accum=R("ac%d_%d" % (t, c), 0, 1))
-        tt(K("mc"), K("M"), K("cf"), A.mult)
-        mm([(rr, R("blk"), K("mc"), True, True)])
+        rr, V = P(c, 0), P(c, 1)
+        msum(rr, [(R("eye"), K("f1")), (R("neg"), K("nx"))])
+        opened = [mm([(V, R("barb", c * LC, (c + 1) * LC), R("cb"), True, False), (V, K("X"), R("blk32"), False, False),
+                      (V, K("f1"), R("hblk"), False, False)])]
+        ra, rv = [], []
+        for p in range(NPC):
+            l0, l1 = p * LC // NPC, (p + 1) * LC // NPC
+            for (a0, a1) in cut(l0, l1, NC):
+                if t < VI - 1:
+                    ra.append(act(R(cg, 16 * a0, 16 * a1), ind(R("er"), K("c16", a0, a1)), F.Copy, -1.875, 0.25))
+                else:
+                    ra.append(act(R(cg, 16 * a0, 16 * a1), ind(R("gt"), K("c16", a0, a1)), F.Copy, None, -2.0))
+            for m in range(16):
+                rv.append(tt(R(hb, m * LC + l0, m * LC + l1), R(cg, 16 * l0 + m, 16 * l1, 16), P(c, 0, l0, l1 - l0), A.is_gt))
+        chain(ra)
+        chain(rv)
+        for m0 in range(0, 16, 4):
+            opened.append(mm([(P(c, 1, m, 128 - m, 16), R(hb, m * LC, (m + 1) * LC), R("blk", 0, 128, 16), False, m == 15)
+                              for m in range(m0, m0 + 4)], opened))
+        scan(K("fw"), R("r1"), V, A.max)
+        scan(rev(K("mx")), R("r1"), rev(K("fw")), A.max)
+        tt(K("M"), V, K("mx"), A.is_equal)
+        act(K("ins"), K("mx"), F.Sign, accum=R(ac, 4, 5) if t < VI - 1 else None)
+        o = P(c, 0, LC)
+        msum(o, [(K("M"), R("eye"))])
+        tt(K("mc"), o, K("cf"), A.mult)
         PH[0] = "fin%d" % c
-        prod("m0", n2, K("insi"))
-        prod("m1", wp, K("nin"))
-        tt(K("iv"), K("xi"), rr, A.mult)
-        b = bank(c)
-        fp = R(b, 0, 2 * LC)
-        mm([(fp, R("eye"), K("m1"), True, False), (fp, R("eye"), K("m0"), False, False), (R(b, 0, LC), R("eye"), K("iv"), False, True)])
+        o = P(c, 1, LC)
+        msum(o, [(R("blk"), K("X")), (K("ins"), R("neg"))])
+        aff("ret", K("ret"), o)
+        aff("nret", K("nret"), o, -1.0, 1.0)
+        o = P(c, 0, 2 * LC)
+        msum(o, [(R("blk"), K("mc"))])
+        prod("m1", rw, K("ret"))
+        prod("m0", iw, K("nret"))
+        tt(K("iv"), K("X"), o, A.mult)
+        fp = P(c, 1, 2 * LC, 2 * LC)
+        msum(fp, [(R("eye"), K("m1")), (R("eye"), K("m0")), (R("eye"), K("iv"), P(c, 1, 2 * LC))])
         if t < VI - 1:
             wo = "wo%d_%d" % (t, c)
-            cp(R(wo), fp)
+            aff("wo", R(wo), fp)
             remote("p%d_%d" % (t, c), R("w%d_%d" % (t + 1, c)), R(wo))
         else:
-            act(R("ysk", c * LC, (c + 1) * LC), R(b, 0, LC), F.Copy, 2048.0)
-            act(R("ywk", c * LC, (c + 1) * LC), R(b, LC, 2 * LC), F.Copy, 2047.0)
+            act(R("ysk", c * LC, (c + 1) * LC), P(c, 1, 2 * LC), F.Copy, 2048.0)
+            act(R("ywk", c * LC, (c + 1) * LC), P(c, 1, 3 * LC), F.Copy, 2047.0)
             for r in range(c * NJ, (c + 1) * NJ):
                 dma("s", R("ys", None, None, 1, (r, 128, 16)), R("ysk", 16 * r, 16 * r + 16))
                 dma("a" if c == NCH - 1 else "s", R("yw", None, None, 1, (r, 128, 16)), R("ywk", 16 * r, 16 * r + 16))
 
     def count(t):
-        b = bank(0)
-        mm([(R(b, 0, 1), R("allo"), R("ac%d_%d" % (t, c), 0, 1), c == 0, c == NCH - 1) for c in range(NCH)])
-        cp(R("rci", 0, 1), R(b, 0, 1))
+        PH[0] = "count"
+        o = P(0, 3, 3 * LC, 1)
+        msum(o, [(R(m), R("ac%d_%d" % (t, c), q, q + 1)) for c in range(NCH) for m, q in (("all1", 0), ("all16", 4))])
+        cp(R("rci", 0, 1), o)
         ts(R("rci", 4, 5), R("rci", 0, 1), 1, A.bitwise_and)
         ts(R("thr", 0, 1), R("rci", 4, 5), -1.0, A.mult, -1.5, A.add)
 
@@ -558,9 +590,11 @@ def rank_program(g, core, T, topo):
         for c in range(NCH):
             run(t, c)
         for c in range(NCH):
+            table(t, c, "gt", "ng")
+        for c in range(NCH):
             cand(t, c)
         for c in range(NCH):
-            table(t, c)
+            table(t, c, "er", "nw")
         if t < VI - 1:
             count(t)
     for j in range(2):
@@ -575,36 +609,54 @@ def rank_program(g, core, T, topo):
             succ[d].append(i)
     for i in range(n - 1, -1, -1):
         o = ops[i]
-        m = 0.0
+        m = LEAD if o["ph"] == "fin0" else 0.0
         for j in succ[i]:
             m = max(m, tail[j])
-        tail[i] = m + o["cost"] + o["lat"] + HOP
+        tail[i] = m + o["cost"] + o["lat"] + HOP + (SLACK if o["kind"] == "r" else 0.0)
     prio = [tail[i] + BIAS.get(ops[i]["ph"], 0.0) for i in range(n)]
-    ndep = [len(o["deps"]) for o in ops]
-    ready = [0.0] * n
-    avail = [i for i in range(n) if ndep[i] == 0]
-    free = {q: 0.0 for q in "vatgsx"}
-    order = []
-    while avail:
-        best = None
-        for i in avail:
-            q = ops[i]["q"]
-            st = ready[i] if q == "x" else max(ready[i], free[q])
-            key = (round(st, 2), -prio[i], i)
-            if best is None or key < best[0]:
-                best = (key, i, st)
-        _, i, st = best
-        avail.remove(i)
-        o = ops[i]
-        if o["q"] != "x":
-            free[o["q"]] = st + o["cost"]
-        fin = st + o["cost"] + o["lat"]
-        order.append(i)
-        for j in succ[i]:
-            ready[j] = max(ready[j], fin + (HOP if ops[j]["q"] != o["q"] else 0.03))
-            ndep[j] -= 1
-            if ndep[j] == 0:
-                avail.append(j)
+    pred = [sorted(o["deps"]) for o in ops]
+
+    def place(prio, before, after, back):
+        left = [len(b) for b in before]
+        ready = [0.0] * n
+        start = [0.0] * n
+        busy = {q: [] for q in "vatgs"}
+        avail = [i for i in range(n) if left[i] == 0]
+        while avail:
+            i = max(avail, key=lambda k: (prio[k], -k))
+            avail.remove(i)
+            o = ops[i]
+            st = ready[i] + (o["lat"] if back else 0.0)
+            if o["q"] != "x":
+                row = busy[o["q"]]
+                lo, hi = 0, len(row)
+                while lo < hi:
+                    mid = (lo + hi) // 2
+                    if row[mid][1] <= st:
+                        lo = mid + 1
+                    else:
+                        hi = mid
+                while lo < len(row) and row[lo][0] < st + o["cost"]:
+                    st = max(st, row[lo][1])
+                    lo += 1
+                row.insert(lo, (st, st + o["cost"]))
+            start[i] = st
+            fin = st + o["cost"] + (0.0 if back else o["lat"])
+            for j in after[i]:
+                ready[j] = max(ready[j], fin + (HOP if ops[j]["q"] != o["q"] else 0.03))
+                left[j] -= 1
+                if left[j] == 0:
+                    avail.append(j)
+        return start, max(start[i] + ops[i]["cost"] + ops[i]["lat"] for i in range(n))
+
+    start, span = place(prio, pred, succ, False)
+    for _ in range(PASSES):
+        late, _x = place([start[i] + ops[i]["cost"] for i in range(n)], succ, pred, True)
+        again, span2 = place([late[i] + ops[i]["cost"] for i in range(n)], pred, succ, False)
+        if span2 >= span:
+            break
+        start, span = again, span2
+    order = sorted(range(n), key=lambda i: (start[i], i))
 
     cnt = {"qv": 0, "qa": 0, "qt": 0, "qg": 0}
     known = {q: {} for q in "vatgs"}
@@ -623,7 +675,7 @@ def rank_program(g, core, T, topo):
             done[i] = (o["sem"], o["inc"], {o["sem"]: o["inc"]})
             tot[o["sem"]] = o["inc"]
             continue
-        for d in sorted(o["deps"], reverse=True):
+        for d in sorted(o["deps"] - o["soft"], reverse=True):
             sem, v, clk = done[d]
             if known[q].get(sem, 0) < v:
                 wait(q, sem, v)

@@ -8,28 +8,40 @@ LC = 256 // NCH
 CA = LC * L
 NJ = LC // 16
 NP = 2
-NPC = 1
-NG = 2
-NF = 2
-NC = 4
+NPC = 2
+NG = 1
+NF = 1
+NC = 1
 LN2 = math.log(2.0)
 AGE = 7
 LA = 80.0 / AGE
-NDMA = 80
-LEAD = 6.0
-SLACK = 3.0
-PASSES = 4
-BIAS = {"end1": 2.1, "score0": -2.5, "set": 3.4, "fin1": 1.2, "fin0": 2.6, "run0": 2.3, "nt": 0.7, "pre0": 0.5, "pre1": 0.5,
-        "count": 0.3, "gt": -0.4, "end0": 0.3, "head1": -0.2, "tab": -0.4, "net0": 0.3}
-ENG = {"off": "v", "e15": "a", "slot": "a", "yi": "a", "ui": "a", "vl": "v", "ne": "v", "xl": "a", "sh": "v", "c16": "a",
-       "cf": "a", "wb": "a", "wo": "a", "sx": "a", "ci": "a", "ret": "a", "nret": "a", "so": "v", "ng": "v", "eh": "a", "sg": "v"}
-NTV = 2
+NDMA = 20
+VFIX = 0.01
+AFIX = 0.09
+MMC = 128
+FIP = 1
+WB = 1
+ULA = 0
+YV = 0
+SPLIT = 0
+RLAT = 3.0
+HOP = 0.15
+NER = 4
+AQ = "s"
+LEAD = 9.5
+SLACK = 4.0
+PASSES = 2
+BIAS = {'vsm0': -4.0, 'end1': 1.4, 'vgtb': 8.1, 'tfl1': 22.0, 'head1': 0.1, 'tblk0': -1.6, 'tw0': -1.2, 'acg1': -6.6, 'tf1': -2.1, 'run0': 7.2, 'axl0': -4.5, 'agb0': -8.9, 'vmx0': -3.2, 'vhb0': -1.9, 'end0': 3.0, 'fin0': 6.6, 'af1': -11.1, 'vk1': 1.0, 'te0': -4.7, 'pre1': -6.1, 'teye1': -1.6, 'txs1': -1.7, 'anw0': 3.5, 'tX1': -1.1, 'vc0': -1.1, 'te1': -4.5, 'tfm1': -7.8, 'ah0': 7.1, 'net0': -1.0, 'tzx1': -1.2, 'vfi0': -0.5, 'vrcit': -2.2, 'awb0': -8.0, 'agb1': -1.3, 'score0': 1.4, 'vkeep1': -2.0, 'vsg1': -2.9, 'set': -1.3, 'vsh1': -2.2, 'gt': -2.5, 'ains0': -0.6}
+ENG = {'off': 'a', 'e15': 'v', 'slot': 'v', 'yi': 'v', 'ui': 'a', 'vl': 'v', 'ne': 'a', 'xl': 'a', 'sh': 'v', 'c16': 'a', 'cf': 'a', 'wb': 'a', 'wo': 'a', 'sx': 'a', 'ci': 'v', 'ret': 'v', 'nret': 'v', 'w8': 'v', 'ov': 'v', 'y13': 'v', 'kap': 'a', 'D': 'v', 'c0': 'v', 'ng': 'a', 'eh': 'a', 'sg': 'v'}
+NTV = 4
 
 SCRATCH = {}
 SEMAPHORES = ["qv", "qa", "qt", "qg"] + ["d%d" % i for i in range(NDMA)]
 for _t in range(VI - 1):
     for _c in range(NCH):
         SEMAPHORES += ["ap%d_%d" % (_t, _c), "as%d_%d" % (_t, _c), "lp%d_%d" % (_t, _c), "ls%d_%d" % (_t, _c)]
+        if SPLIT:
+            SEMAPHORES += ["aq%d_%d" % (_t, _c), "lq%d_%d" % (_t, _c)]
 LOG = {}
 _SHORT = {"bfloat16": "bf", "float16": "hf", "float32": "ff", "int32": "nn", "uint16": "uu"}
 
@@ -47,23 +59,30 @@ def _buf(name, cols, dtype, where="sbuf"):
 
 for _n in ("er", "gt", "nt", "tq", "tcl", "tsg"):
     _buf(_n, W, "bfloat16")
-for _n in ("ip", "ic", "gp", "gc", "kp", "kc"):
-    _buf(_n, 128, "int32")
-for _n in ("dd", "pp", "ns", "eye", "blk", "tri", "shd", "sh1", "sh2", "sh4", "sh8", "neg", "e16", "n16", "ial", "hneg", "i13",
-           "n2048", "mt", "mth", "nblk", "hblk", "blk32", "blkk", "e0", "e1", "r1", "r2", "tmp"):
+for _n in ("ip", "kp"):
+    _buf(_n, 8, "int32")
+_buf("kc", 256, "int32")
+for _n in ("i48", "eye", "blk", "tri", "shd", "sh1", "sh2", "sh4", "sh8", "neg", "e16", "n16", "ial", "i125", "b125",
+           "i2048", "mt", "mth", "nblk", "hblk", "blk32", "blkk", "r1", "r2", "tmp", "mr", "m16"):
     _buf(_n, 128, "bfloat16")
 _buf("msk", 256, "bfloat16")
 _buf("al", CA // NP, "bfloat16")
 _buf("cb", 128, "float16")
-_buf("cb2", 128, "float16")
-for _n in ("thf", "all1", "all16"):
-    _buf(_n, 128, "float32")
+for _n in ("all1", "all16", "acb"):
+    _buf(_n, 128, "bfloat16")
 for _n in ("kcol", "kap", "thr", "m1c", "m2c"):
     _buf(_n, 8, "float32")
 _buf("rci", 8, "int32")
 _buf("xbase", 2 * NJ, "bfloat16")
 _buf("xbi", NJ, "int32")
-_buf("stl", 16, "uint16")
+for _n in ("stl", "bal"):
+    _buf(_n, 16, "uint16")
+for _n in ("lb", "lc", "kq"):
+    _buf(_n, 16, "int32")
+for _n in ("an", "at"):
+    _buf(_n, 512, "float16")
+for _n in ("in00", "in01", "in10", "in11", "out00", "out01", "out10", "out11"):
+    _buf(_n, 128, "bfloat16")
 _buf("bari", 256, "int32")
 for _n in ("barb", "sti", "sth", "stc", "stn"):
     _buf(_n, 256, "bfloat16")
@@ -88,7 +107,7 @@ for _c in range(NCH):
         _buf("%s_%d" % (_n, _c), LC, "float16")
     for _n in ("a1", "a2", "m0", "m1", "m2", "m3", "wb", "xm"):
         _buf("%s_%d" % (_n, _c), 2 * LC, "float16")
-    for _n in ("yi", "y7", "pr", "sh", "sm", "ci", "cn", "k0", "k1", "k2", "k3"):
+    for _n in ("yi", "y7", "pr", "sh", "sm", "ci", "cn", "c0", "k0", "k1", "k2", "k3"):
         _buf("%s_%d" % (_n, _c), LC, "int32")
     for _n in ("ab", "ln", "sx"):
         _buf("%s_%d" % (_n, _c), LC, "float32")
@@ -98,6 +117,8 @@ for _c in range(NCH):
     _buf("vl_%d" % _c, NJ, "uint16")
     for _n in ("ui", "uj", "uk", "vb"):
         _buf("%s_%d" % (_n, _c), NJ, "int32")
+    for _n in ("ub", "uf", "vc"):
+        _buf("%s_%d" % (_n, _c), NJ, "bfloat16")
 for _i in range(8):
     _buf("p%d" % _i, 512, "float32", "psum")
 
@@ -122,6 +143,7 @@ def rank_program(g, core, T, topo):
     Q = {"v": g.vector, "a": g.scalar, "t": g.tensor, "g": g, "s": g.sync}
     QS = {"v": "qv", "a": "qa", "t": "qt", "g": "qg"}
     dn = [0]
+    moved = [0.0]
     PH = ["set"]
     PS = set("p%d" % i for i in range(8))
 
@@ -184,7 +206,9 @@ def rank_program(g, core, T, topo):
                     cur[:] = [e for e in cur if not (e[1][1] >= r[1] and e[1][2] <= r[2])]
                 cur.append((i, r, isw))
         deps |= set(soft)
-        ops.append({"ph": PH[0], "nm": wr[0][0] if wr else "", "q": q, "fns": fns, "deps": deps, "cost": cost, "kind": kind,
+        nm = rd[-1][0] if q == "t" or not wr or wr[0][0] in PS else wr[0][0]
+        ops.append({"ph": PH[0], "nm": q + "".join(ch for ch in nm if ch.isalpha()) + PH[0][-1], "q": q,
+                    "ind": any(isinstance(r, tuple) and r[0] == "IND" for r in list(reads) + list(writes)), "fns": fns, "deps": deps, "cost": cost, "kind": kind,
                     "lat": lat, "sem": sem, "inc": inc, "soft": set(soft)})
         return i
 
@@ -200,7 +224,7 @@ def rank_program(g, core, T, topo):
     CY = 0.00083
 
     def vc(n, rate):
-        return 0.02 + max(64, n * rate) * CY
+        return VFIX + max(64, n * rate) * CY
 
     def tt(out, a, b, op):
         rate = 1.6 if a[0] == "IND" else (1.0 if a[0] in PS or b[0] in PS else 2.0)
@@ -217,6 +241,9 @@ def rank_program(g, core, T, topo):
     def cp(out, a):
         rate = 4.0 if out[0] == "IND" else (0.5 if two(out, a) else 1.0)
         return add("v", [lambda: g.vector.tensor_copy(x(out), x(a))], [a], [out], vc(n_of(a), rate))
+
+    def turn(out, a):
+        return add("v", [lambda: g.vector.transpose(x(out), x(a))], [a], [out], vc(n_of(a), 1.0))
 
     def fill(out, v):
         add("v", [lambda: g.vector.memset(x(out), v)], [], [out], vc(n_of(out), 0.5 if two(out) else 1.0))
@@ -236,8 +263,9 @@ def rank_program(g, core, T, topo):
         if accum is not None:
             kw["accum_out"] = accum
         rate = 1.6 if a[0] == "IND" else 1.0
+        first = 1.3 if func == F.Ln and PH[0] == "set" else 0.0
         return add("a", [lambda: g.scalar.activation(x(out), x(a), func, **{k: x(v) for k, v in kw.items()})], [a, bias, scale],
-                   [out] + ([accum] if accum is not None else []), 0.04 + max(64, n_of(out) * rate) * CY)
+                   [out] + ([accum] if accum is not None else []), AFIX + first + max(64, n_of(out) * rate) * CY)
 
     def aff(nm, out, a, scale=None, bias=None):
         if ENG[nm] == "a":
@@ -246,14 +274,35 @@ def rank_program(g, core, T, topo):
             return cp(out, a) if bias is None else ts(out, a, bias, A.add)
         return ts(out, a, scale, A.mult) if bias is None else ts(out, a, scale, A.mult, bias, A.add)
 
-    def mm(items, soft=()):
-        fns, rd, wr, cost = [], [], [], 0.02
-        for (o, l, r, s, e) in items:
-            fns.append(lambda o=o, l=l, r=r, s=s, e=e: g.tensor.matmul(x(o), x(l), x(r), s, e))
-            rd += [l, r]
-            wr.append(o)
-            cost += max(64, n_of(r)) * CY * (4 if LOG[r[0]][2] == "float32" else 1)
-        return add("t", fns, list(dict.fromkeys(rd)), list(dict.fromkeys(wr)), cost, soft=soft)
+    def relu(nm, out, a, bias=None):
+        if ENG[nm] == "a":
+            return act(out, a, F.Relu, bias)
+        return ts(out, a, 0.0, A.max) if bias is None else ts(out, a, bias, A.add, 0.0, A.max)
+
+    group = {}
+
+    def mm(items):
+        rows, cols = [[]], 0
+        for it in items:
+            n = max(64, n_of(it[2])) * (4 if LOG[it[2][0]][2] == "float32" else 1)
+            if cols + n > MMC and rows[-1] and PH[0] != "gt":
+                rows.append([])
+                cols = 0
+            rows[-1].append(it)
+            cols += n
+        for row in rows:
+            fns, rd, wr, cost = [], [], [], 0.01
+            for (o, l, r, s, e) in row:
+                fns.append(lambda o=o, l=l, r=r, s=s, e=e: g.tensor.matmul(x(o), x(l), x(r), s, e))
+                rd += [l, r]
+                wr.append(o)
+                cost += max(64, n_of(r)) * CY * (4 if LOG[r[0]][2] == "float32" else 1)
+            bank = row[0][0][0]
+            i = add("t", fns, list(dict.fromkeys(rd)), list(dict.fromkeys(wr)), cost, soft=[] if row[0][3] else group[bank])
+            if bank in group:
+                chain([group[bank][-1], i])
+            group[bank] = [i] if row[0][3] else group[bank] + [i]
+        return i
 
     def msum(o, terms):
         return mm([(t[2] if len(t) > 2 else o, t[0], t[1], q == 0, q == len(terms) - 1) for q, t in enumerate(terms)])
@@ -261,7 +310,8 @@ def rank_program(g, core, T, topo):
     def dma(q, out, a):
         s = "d%d" % dn[0]
         dn[0] += 1
-        return add(q, [lambda: Q[q].dma_start(x(out), x(a))], [a], [out], 0.1, "d", 2.2, s, 16)
+        moved[0] += n_of(out if out[0] in LOG else a) * 0.0008 - (0.3 if q == "s" else 0.0)
+        return add(q, [lambda: Q[q].dma_start(x(out), x(a))], [a], [out], 0.6, "d", 2.0 + moved[0], s, 16)
 
     def remote(tag, out, a):
         m, ne = 0, 8
@@ -269,93 +319,119 @@ def rank_program(g, core, T, topo):
             m |= 1 << e
         rid, pid = topo.addr(nxt)[0], topo.addr(nxt)[1]
         ra, la = T.sem["a" + tag], T.sem["l" + tag]
-        i = add("g", [lambda: g.remote_dma(ap(out), ap(a), ra, la, pid, rid, m)], [a], [], 1.2, "r", 2.5, "l" + tag, ne)
+        i = add("g", [lambda: g.remote_dma(ap(out), ap(a), ra, la, pid, rid, m)], [a], [], 1.0, "r", RLAT, "l" + tag, ne)
         return add("x", [], [], [out], 0.0, "x", 0.0, "a" + tag, ne, (i,))
 
     def P(c, i, a=0, n=LC, st=1):
         return R("p%d" % (4 * c + i), a, a + n, st)
 
-    def lanes(q, buf, name, r0, r1):
-        for r in range(r0, r1):
-            dma(q, R(buf, 16 * r, 16 * r + 16), R(name, None, None, 1, (r, 128, 16)))
-    for j in range(4):
-        dma("s", R("er", 1024 * j, 1024 * j + 1024), R("eff", 1024 * j, 1024 * j + 1024))
-    lanes("a", "actk", "act", 0, 16 // NCH)
-    dma("a", R("sti"), R("st0"))
-    for j in range(4):
-        dma("s", R("tq", 1024 * j, 1024 * j + 1024), R("req", 1024 * j, 1024 * j + 1024))
-    lanes("s", "actk", "act", 16 // NCH, 16)
+    BC = {}
+    for q, (nm, v) in enumerate((("need", 736.0), ("least", 13.0 / 16))):
+        BC[nm] = R("m1c", q, q + 1)
+        fill(BC[nm], v)
+    act(R("m1c", 2, 3), BC["least"], F.Ln, None, 2.0 ** (8 * AGE))
+    ts(R("m1c", 3, 4), R("m1c", 2, 3), -LA / LN2, A.mult, -0.21, A.add)
+    for j in range(NER):
+        dma("s", R("er", W // NER * j, W // NER * (j + 1)), R("eff", W // NER * j, W // NER * (j + 1)))
+        if j == NER - 1:
+            dma(AQ, R("actk"), R("act"))
+            dma(AQ, R("sti"), R("st0"))
+    chain([i for i, o in enumerate(ops) if o["q"] == "a"])
+    for j in range(2):
+        dma("s", R("tq", 2048 * j, 2048 * j + 2048), R("req", 2048 * j, 2048 * j + 2048))
+    dma("s", R("whyk"), R("why"))
     fill(R("bari"), 1)
     dma("s", R("bari", None, None, 1, (0, 128, 16)), R("bar"))
-    lanes("s", "whyk", "why", 0, 16)
+    chain([i for i, o in enumerate(ops) if o["q"] == "s"])
 
     def iota(out, pattern, base, cm):
         add("g", [lambda: g.iota(x(out), pattern, base, cm)], [], [out], 0.13 + 2 * n_of(out) * CY)
-    iota(R("ip"), [[0, 128]], 0, 1)
-    iota(R("ic"), [[1, 128]], 0, 0)
+    def keep(out, a, value, op, other):
+        add("g", [lambda: g.affine_select(x(out), x(a), value[0], op, other, value[1], value[2])], [a], [out], 0.17 + 2 * n_of(out) * CY)
+
+    def c_p(d):
+        return ([[1, 128]], -d, -1)
+
+    def row(k):
+        return ([[-16, 8], [0, 16]], -k, 1)
+    fill(R("all1"), 1.0)
+    keep(R("eye"), R("all1"), c_p(0), A.is_equal, 0.0)
+    iota(R("ip"), [[0, 8]], 0, 1)
+    iota(R("kc"), [[0, 16], [1, 16]], 0, 0)
+    keep(R("tmp"), R("all1"), row(0), A.is_ge, 0.0)
+    keep(R("blk"), R("tmp"), ([[16, 8], [0, 16]], 15, -1), A.is_ge, 0.0)
     iota(R("xbi"), [[256, NJ]], 0, 0)
-    for c in range(NCH):
-        iota(R("vb_%d" % c), [[16, NJ]], LC * c, 0)
-    tt(R("eye"), R("ip"), R("ic"), A.is_equal)
-    for nm, f in (("e16", 1.0 / 16), ("n16", -1.0 / 16), ("neg", -1.0), ("ial", 2.0 ** -AGE), ("hneg", -0.5), ("i13", 13.0 / 16), ("n2048", -2048.0)):
+    iota(R("lb"), [[64, 2], [128, 2], [4, 4]], 0, 0)
+    iota(R("lc"), [[4, 2], [8, 2], [64, 4]], 0, 0)
+    for g2 in range(2):
+        for h in range(2):
+            keep(R("in%d%d" % (g2, h)), R("all1"), ([[-32, 4], [200, 2], [-2, 16]], -h - 200 * g2, 1), A.is_equal, 0.0)
+            keep(R("out%d%d" % (g2, h)), R("all1"), ([[-32, 4], [-1, 16], [200, 2]], -16 * g2 - 200 * h, 1), A.is_equal, 0.0)
+    for nm, f in (("e16", 1.0 / 16), ("n16", -1.0 / 16)):
+        ts(R(nm), R("eye"), f, A.mult)
+    for nm, f in (("neg", -1.0), ("ial", 2.0 ** -AGE), ("i125", 12.5), ("i2048", 2048.0),
+                  ("m16", -16.0), ("i48", 48.0)):
         act(R(nm), R("eye"), F.Copy, None, f)
-    ts(R("gp"), R("ip"), 4, A.arith_shift_right)
-    ts(R("gc"), R("ic"), 4, A.arith_shift_right)
     ts(R("kp"), R("ip"), 15, A.bitwise_and)
-    ts(R("kc"), R("ic"), 15, A.bitwise_and)
-    tt(R("blk"), R("gp"), R("gc"), A.is_equal)
-    ts(R("ns"), R("blk"), -64.0, A.mult, 64.0, A.add)
-    tt(R("pp"), R("kp"), R("ns"), A.add)
-    tt(R("dd"), R("kc"), R("pp"), A.subtract)
-    ts(R("tri"), R("dd"), 0.0, A.is_ge)
-    for nm, de in (("shd", 1.0), ("sh1", -1.0), ("sh2", -2.0), ("sh4", -4.0), ("sh8", -8.0)):
-        ts(R("tmp"), R("dd"), de, A.is_equal)
-        tt(R(nm), R("tmp"), R("eye"), A.subtract)
-    ts(R("e0"), R("pp"), 0.0, A.is_equal)
-    ts(R("e1"), R("pp"), 1.0, A.is_equal)
-    ts(R("mt"), R("e0"), 0.5, A.mult)
-    tt(R("mt"), R("mt"), R("sh1"), A.add)
-    ts(R("thf"), R("dd"), 2.0, A.min, AGE * LN2, A.mult)
     ts(R("kcol", 0, 1), R("kp", 0, 1), 1.0, A.mult)
-    BC = {}
-    for q, (nm, v) in enumerate((("thj", AGE * LN2 + math.log(0.375)), ("one", -1.0), ("need", 46.0))):
-        BC[nm] = R("m1c", q, q + 1)
-        fill(BC[nm], v)
-    act(R("mth"), R("thf"), F.Exp, BC["thj"])
-    for nm, f in (("nblk", -1.0), ("hblk", 0.5), ("blk32", 32.0), ("blkk", R("kcol", 0, 1))):
-        ts(R(nm), R("blk"), f, A.mult)
-    for h in range(2):
-        tt(R("msk", 128 * h, 128 * h + 128), R("kp"), R("kc"), A.is_equal)
-    ts(R("r1"), R("kc"), 1.0, A.is_ge)
-    ts(R("r2"), R("r1"), 2.0, A.mult)
-    ts(R("cb2"), R("kc"), -1.0 / 32, A.mult, -39.5, A.add)
-    tt(R("cb"), R("cb2"), R("e1"), A.mult)
-    tt(R("cb"), R("cb"), R("e0"), A.subtract)
+    keep(R("tri"), R("blk"), c_p(0), A.is_ge, 0.0)
+    for nm, de in (("sh1", -1), ("shd", 1), ("sh2", -2), ("sh4", -4), ("sh8", -8)):
+        keep(R(nm), R("blk"), c_p(de), A.is_equal, 0.0)
+        keep(R(nm), R(nm), c_p(0), A.not_equal, -1.0)
+    keep(R("mt"), R("sh1"), row(0), A.not_equal, 0.5)
+    keep(R("mt"), R("mt"), ([[-16, 8], [128, 16]], 0, 1), A.not_equal, -0.5)
     fill(R("al"), 2.0 ** -AGE)
     fill(R("al", 0, CA // NP, 16), 0.0)
+    scan(rev(R("mth")), R("al", 0, 128), rev(R("i48")), A.add)
+    keep(R("mth"), R("mth"), ([[-1, 128]], 0, 1), A.is_ge, 48.0)
+    keep(R("mth"), R("mth"), row(0), A.is_ge, 0.0)
+    for nm, f in (("nblk", -1.0), ("hblk", 0.5), ("b125", -12.5), ("blk32", 32.0), ("blkk", R("kcol", 0, 1))):
+        ts(R(nm), R("blk"), f, A.mult)
+    ts(R("msk"), R("kc"), R("kcol", 0, 1), A.is_equal)
+    keep(R("r1"), R("all1"), ([[0, 8], [1, 16]], -1, 0), A.is_ge, 0.0)
+    ts(R("r2"), R("r1"), 2.0, A.mult)
+    ts(R("cb"), R("kc", 0, 128), -1.0 / 32, A.mult, -39.5, A.add)
+    keep(R("cb"), R("cb"), row(1), A.is_equal, 0.0)
+    keep(R("cb"), R("cb"), row(0), A.not_equal, -1.0)
+    keep(R("mr"), R("nblk"), c_p(0), A.is_ge, 0.0)
+    keep(R("mr"), R("mr"), c_p(0), A.not_equal, 63.0)
     ts(R("kap", 0, 1), R("kcol", 0, 1), 241.0, A.mult, 101.0, A.add)
     for t in range(VI):
         ts(R("kap", 4 + t, 5 + t), R("kap", 0, 1), 2048.0, A.mult, float(97 * t), A.add)
     ts(R("m2c", 0, 1), R("kcol", 0, 1), 15.0, A.is_equal, -0.5, A.add)
     ts(R("m2c", 1, 2), R("kcol", 0, 1), 1.0, A.add)
+    ts(R("m2c", 2, 3), R("kcol", 0, 1), -63.0, A.add)
     fill(R("thr", 0, 1), -1.5)
-    fill(R("all1"), 1.0)
     fill(R("all16"), 1.0 / 16.0)
-    fill(R("tmp"), 1.0)
     ts(R("kcol", 2, 3), R("kcol", 0, 1), 16.0, A.mult)
     ts(R("xbase", 0, NJ), R("xbi"), R("kcol", 2, 3), A.add)
     fill(R("xbase", NJ, 2 * NJ), 2048.0)
-    ts(R("stl"), R("ic", 0, 16), R("kcol", 2, 3), A.add)
-    ts(R("kcol", 4, 5), R("kcol", 0, 1), 256.0, A.mult)
+    ts(R("kq", 0, 1), R("kp", 0, 1), 3, A.bitwise_and)
+    ts(R("kq", 4, 5), R("kp", 0, 1), 2, A.arith_shift_right)
+    cp(R("kcol", 4, 5), R("kq", 0, 1))
+    cp(R("kcol", 5, 6), R("kq", 4, 5))
+    ts(R("kcol", 6, 7), R("kcol", 4, 5), 16.0, A.mult, R("kcol", 5, 6), A.add)
+    ts(R("kcol", 7, 8), R("kcol", 5, 6), 16.0, A.mult, R("kcol", 4, 5), A.add)
+    ts(R("stl"), R("lb"), R("kcol", 6, 7), A.add)
+    ts(R("bal"), R("lc"), R("kcol", 7, 8), A.add)
     for c in range(NCH):
-        ts(R("vb_%d" % c), R("vb_%d" % c), R("kcol", 4, 5), A.add)
-    cp(R("barb"), R("bari"))
-    for c in range(NCH):
-        a0, a1 = c * LC, (c + 1) * LC
-        ts(R("w0_%d" % c, 0, LC), R("actk", a0, a1), -2048.0, A.add)
-        ts(R("w0_%d" % c, LC, 2 * LC), R("whyk", a0, a1), -2047.0, A.add)
-    ts(R("sth"), R("sti"), 8.0, A.is_lt, 25.0 / 16, A.mult)
-    ts(R("stn"), R("sti"), -1.0 / 16, A.mult, -5.0 / 16, A.add)
+        ts(R(("vc_%d" if ULA else "vb_%d") % c), R("lb", c * NJ, (c + 1) * NJ), R("kcol", 6, 7), A.add, 16.0, A.mult)
+    act(R("barb"), ind(R("bari"), R("bal")), F.Copy)
+    ts(R("an", 0, 256), R("actk"), -2048.0, A.add)
+    ts(R("whyk"), R("whyk"), 8191, A.bitwise_and)
+    ts(R("an", 256, 512), R("whyk"), 4096.0, A.min, -2048.0, A.add)
+
+    def plans(f):
+        PH[0] = "set"
+        for c in range(NCH):
+            a0 = 256 * f + LC * c
+            for c4 in range(4):
+                turn(R("at", a0 + c4, a0 + LC, 4), R("an", 256 * f + 4 * c + c4, 256 * f + 256, 8))
+            for h in range(2):
+                msum(P(0, c + 2 * f, 64 * h, 64), [(R("in%d%d" % (g2, h)), R("at", a0 + 64 * g2, a0 + 64 * g2 + 64)) for g2 in range(2)])
+            act(R("w0_%d" % c, f * LC, (f + 1) * LC), P(0, c + 2 * f), F.Copy)
+    ts(R("sth"), R("sti"), 8.0, A.is_lt, 25.0, A.mult)
+    ts(R("stn"), R("sti"), -1.0, A.mult, -5.0, A.add)
     tt(R("stc"), R("stn"), R("sth"), A.add)
     for c in range(NCH):
         act(R("s0_%d" % c), ind(R("stc"), R("stl", c * NJ, (c + 1) * NJ)), F.Copy)
@@ -368,13 +444,17 @@ def rank_program(g, core, T, topo):
         msum(b, [(R("n16"), R("er", c0, c1)), (R("e16"), R("tcl", c0, c1))])
         act(R("tsg", c0, c1), b, F.Sign)
         tt(R("gt", c0, c1), R("tsg", c0, c1), b, A.add)
+        if j == 7:
+            plans(0)
+            PH[0] = "gt"
+    plans(1)
     PH[0] = "nt"
     for j in range(4):
         c0, c1 = 1024 * j, 1024 * j + 1024
         if j < NTV:
-            ts(R("nt", c0, c1), R("tq", c0, c1), 12.0, A.is_lt, 4.0, A.mult)
+            ts(R("nt", c0, c1), R("tq", c0, c1), 12.0, A.is_lt, 32.0, A.mult)
         else:
-            act(R("nt", c0, c1), R("tq", c0, c1), F.Relu, BC["need"], -4.0)
+            act(R("nt", c0, c1), R("tq", c0, c1), F.Relu, BC["need"], -64.0)
 
     def pick(o, xm, n):
         return [(R(xm, q * LC, (q + 1) * LC), R("blk", 0, 128, 16), R(o[0], o[1] + q * NJ, o[1] + (q + 1) * NJ)) for q in range(n)]
@@ -396,40 +476,48 @@ def rank_program(g, core, T, topo):
             for (a0, a1) in cut(l0, l1, NG):
                 ra.append(act(R(gb, 16 * a0 + 1, 16 * a1 + 1), ind(R("gt"), K("off", a0, a1)), F.Copy))
             aff("e15", K("e15", l0, l1), R(gb, e0 + 16, e1 + 1, 16))
-            aff("slot", R(gb, e0, e1, 16), R(s, l0, l1))
+            aff("slot", R(gb, e0, e1, 16), R(s, l0, l1), 1.0 / 16)
             rv.append(scan(R(zb, e0, e1), R("al"), R(gb, e0, e1), A.add))
             for (a0, a1) in cut(l0, l1, NF):
                 rv.append(tt(R(fl, 16 * a0, 16 * a1), ind(R("nt"), K("off", a0, a1)), R(zb, 16 * a0, 16 * a1), A.is_lt))
         chain(ra)
         chain(rv)
         mm([(P(c, 1, k, 128 - k, 16), R(fl, k, CA, 16), R("blk", 0, 128, 16), True, True) for k in range(16)])
-        act(K("ov"), P(c, 1), F.Sign, R("thr", 0, 1))
+        if ENG["ov"] == "a":
+            act(K("ov"), P(c, 1), F.Sign, R("thr", 0, 1))
+        else:
+            ts(K("ov"), P(c, 1), R("thr", 0, 1), A.add, 0.0, A.is_gt)
         PH[0] = "end%d" % c
         o = P(c, 2)
         msum(o, [(R("ial"), R(zb, 15, CA, 16)), (R("eye"), K("e15"))])
         act(K("ab"), o, F.Abs)
         act(K("h"), o, F.Sign)
         act(K("ln"), K("ab"), F.Ln, None, 2.0 ** (8 * AGE))
-        aff("yi", K("yi"), K("ln"), LA / LN2, -LA * math.log2(13.0 / 16) - 0.21)
+        aff("yi", K("yi"), K("ln"), LA / LN2, R("m1c", 3, 4))
         ts(K("y7"), K("yi"), 7, A.bitwise_and)
-        tt(K("q"), K("y7"), K("h"), A.mult)
+        sv = R("so%d_%d" % (t, c))
+        aff("y13", o, K("y7"), None, 13.0)
+        tt(sv, K("h"), o, A.mult)
         if t < VI - 1:
-            o = P(c, 2, LC)
-            msum(o, [(R("e16"), K("q")), (R("i13"), K("h"))])
-            aff("so", R("so%d_%d" % (t, c)), o)
-            remote("s%d_%d" % (t, c), R("s%d_%d" % (t + 1, c)), R("so%d_%d" % (t, c)))
+            remote("s%d_%d" % (t, c), R("s%d_%d" % (t + 1, c)), sv)
         o = P(c, 2, 2 * LC)
-        msum(o, [(K("q"), R("blk")), (K("h"), R("hblk"))])
+        msum(o, [(sv, R("blk")), (K("h"), R("b125"))])
         tt(K("um"), o, R("msk", 0, LC), A.mult)
         o = P(c, 2, 3 * LC, NJ)
         msum(o, pick(o, "um_%d" % c, 1))
-        aff("ui", K("ui"), o, -1.0, 120.0)
-        ts(K("uj"), K("ui"), 15, A.bitwise_and)
-        tt(K("uk"), K("uj"), K("vb"), A.add)
-        aff("vl", K("vl"), K("uk"))
+        if ULA:
+            act(K("ub"), o, F.Copy)
+            act(K("uf"), o, F.Copy, 192.0 + 112.5 / 16, -1.0 / 16)
+            msum(o, [(R("eye"), K("vc")), (R("neg"), K("ub")), (R("m16"), K("uf"))])
+            aff("vl", K("vl"), o, None, 3192.0)
+        else:
+            aff("ui", K("ui"), o, -1.0, 120.0)
+            ts(K("uj"), K("ui"), 15, A.bitwise_and)
+            tt(K("uk"), K("uj"), K("vb"), A.add)
+            aff("vl", K("vl"), K("uk"))
         act(K("eo"), ind(R("er"), K("vl")), F.Copy)
         o = P(c, 2)
-        msum(o, [(R("eye"), K("eo")), (R("neg"), K("q")), (R("hneg"), K("h"))])
+        msum(o, [(R("neg"), sv), (R("i125"), K("h")), (R("eye"), K("eo"))])
         aff("eh", K("eh"), o, 0.5, 195.5)
         aff("ne", K("nw"), K("eh"), None, -192.0)
         if t < VI - 1:
@@ -467,21 +555,29 @@ def rank_program(g, core, T, topo):
         sx, kap = P(c, 3, 2 * LC), P(c, 3, 3 * LC)
         msum(sx, [(R("blk"), K("xs"))])
         aff("sx", K("sx"), sx, None, 2048.0)
-        act(kap, sx, F.Copy, R("kap", 4 + t, 5 + t), R("kap", 0, 1))
+        aff("kap", kap, sx, R("kap", 0, 1), R("kap", 4 + t, 5 + t))
         act(K("zx"), ind(R("zb%d" % c), K("xl", 0, NJ)), F.Copy)
-        act(K("nx"), ind(R("nt"), K("xl", NJ, 2 * NJ)), F.Copy)
-        o = P(c, 1)
-        msum(o, [(R("eye"), K("zx")), (R("neg"), K("nx"))])
-        act(K("w8"), o, F.Relu)
-        act(K("f1"), o, F.Sign)
+        if YV:
+            tt(K("nx"), ind(R("nt"), K("xl", NJ, 2 * NJ)), K("zx"), A.subtract)
+            if ENG["w8"] == "a":
+                act(K("w8"), K("nx"), F.Relu, None, -1.0)
+            else:
+                ts(K("w8"), K("nx"), -1.0, A.mult, 0.0, A.max)
+            act(K("f1"), K("nx"), F.Sign, None, -1.0)
+        else:
+            act(K("nx"), ind(R("nt"), K("xl", NJ, 2 * NJ)), F.Copy)
+            o = P(c, 1)
+            msum(o, [(R("eye"), K("zx")), (R("neg"), K("nx"))])
+            relu("w8", K("w8"), o)
+            act(K("f1"), o, F.Sign)
         o = P(c, 0, 2 * LC)
         msum(o, [(R("mth"), K("X")), (R("nblk"), K("w8"))])
         act(K("T"), o, F.Sign)
         D = P(c, 3)
         msum(D, [(R("eye"), K("X")), (R("mt"), K("T"))])
-        act(D, D, F.Relu, R("m2c", 0, 1))
+        relu("D", D, D, R("m2c", 0, 1))
         tt(K("ds"), S_, D, A.mult)
-        sda, sdp = P(c, 3, LC), P(c, 3, 2 * LC)
+        sda = sdp = P(c, 3, LC)
         msum(sda, [(R("blk"), K("ds"))])
         tt(K("pr"), sda, K("sx"), A.mult)
         if ENG["sh"] == "a":
@@ -496,43 +592,55 @@ def rank_program(g, core, T, topo):
         def prod(n, wd, mask):
             tt(K(n, 0, LC), R(wd[0], wd[1], wd[1] + LC), mask, A.mult)
             tt(K(n, LC, 2 * LC), R(wd[0], wd[1] + LC, wd[1] + 2 * LC), mask, A.mult)
-        wp = [P(c, 2, 0, 2 * LC), P(c, 2, 2 * LC, 2 * LC)]
+        wp = P(c, 2, 0, 2 * LC)
         aff("cf", K("cf"), K("ci"), None, -2048.0)
-        msum(sdp, [(R("eye"), R("tmp")), (R("blk"), K("ds"))])
-        msum(wp[0], [(R("eye"), W_)])
+        msum(wp, [(R("eye"), W_)])
         tt(K("ne"), Q_, sdp, A.not_equal)
         tt(K("keep"), K("ne"), D, A.is_gt)
         tt(K("iqe"), K("X"), sdp, A.mult)
-        mm([(P(c, 2, 2 * LC), R("tri"), K("keep"), True, True), (P(c, 2, 3 * LC), R("blk"), K("keep"), True, True)])
-        aff("ci", K("cn"), P(c, 2, 2 * LC), -1.0, R("m2c", 1, 2))
-        ts(K("fm"), P(c, 2, 3 * LC), R("kcol", 0, 1), A.is_le)
-        prod("a2", wp[0], K("keep"))
-        for s in range(4):
+        mm([(P(c, 1, LC), R("mr"), K("keep"), True, True), (P(c, 1, 2 * LC), R("tri"), K("keep"), True, True),
+            (P(c, 1, 3 * LC), R("blk"), K("keep"), True, True)])
+        relu("c0", K("c0"), P(c, 1, LC), R("m2c", 2, 3))
+        aff("ci", K("cn"), P(c, 1, 2 * LC), -1.0, R("m2c", 1, 2))
+        ts(K("fm"), P(c, 1, 3 * LC), R("kcol", 0, 1), A.is_le)
+        prod("a2", wp, K("keep"))
+        ts(K("k0"), K("c0"), 1, A.bitwise_and)
+        prod("m0", wp, K("k0"))
+        for s in range(1, 4):
             ts(K("k%d" % s), K("cn"), s, A.arith_shift_right, 1, A.bitwise_and)
-        tt(K("fi"), K("fm"), K("cf"), A.mult)
-        terms = [(R("eye"), K("a2"))]
-        for s in range(4):
-            cur = wp[(s + 1) % 2]
-            msum(cur, terms)
-            if s == 2:
-                aff("wb", K("wb"), cur)
-                terms = [(R("eye"), K("wb"))]
-            prod("m%d" % s, cur, K("k%d" % s))
-            terms.append((R("sh%d" % (1 << s)), K("m%d" % s)))
-        rw = wp[1]
-        msum(rw, terms + [(R("eye"), K("fi"), P(c, 2, 2 * LC)), (R("n2048"), K("fm"), P(c, 2, 3 * LC))])
         PH[0] = "pre%d" % c
         msum(sda, [(R("tri"), K("X"))])
         tt(K("a1", 0, LC), S_, sda, A.mult)
         tt(K("a1", LC, 2 * LC), Q_, sda, A.mult)
         iw = P(c, 3, 0, 2 * LC)
         msum(iw, [(R("eye"), W_), (R("shd"), K("a1")), (R("eye"), K("iqe"), P(c, 3, LC))])
+        PH[0] = "net%d" % c
+        if FIP:
+            act(P(c, 1, LC), K("ci"), F.Copy, -2048.0)
+            tt(K("fi"), K("fm"), P(c, 1, LC), A.mult)
+        else:
+            tt(K("fi"), K("fm"), K("cf"), A.mult)
+        terms = [(R("eye"), K("a2"))]
+        for s in range(4):
+            cur = (P(c, 2, 2 * LC, 2 * LC), P(c, 3, 2 * LC, 2 * LC), wp, P(c, 3, 2 * LC, 2 * LC))[s]
+            move = (R("sh%d" % (1 << s)), K("m%d" % s))
+            if s == 3:
+                if WB:
+                    terms = [(R("eye"), K("wb")), terms[-1]]
+                terms += [(R("eye"), K("fi"), P(c, 3, 2 * LC)), (R("i2048"), K("fm"), P(c, 3, 3 * LC))]
+            terms.append(move)
+            msum(cur, terms)
+            if s < 3:
+                prod("m%d" % (s + 1), cur, K("k%d" % (s + 1)))
+            if s == 1 and WB:
+                aff("wb", K("wb"), cur)
+        rw = cur
         PH[0] = "score%d" % c
         hb, cg = "hb%d" % c, "cg%d" % c
         rr, V = P(c, 0), P(c, 1)
-        msum(rr, [(R("eye"), K("f1")), (R("neg"), K("nx"))])
-        opened = [mm([(V, R("barb", c * LC, (c + 1) * LC), R("cb"), True, False), (V, K("X"), R("blk32"), False, False),
-                      (V, K("f1"), R("hblk"), False, False)])]
+        msum(rr, [(R("n16"), K("nx")), (R("eye"), K("f1"))])
+        mm([(V, R("barb", c * LC, (c + 1) * LC), R("cb"), True, False), (V, K("X"), R("blk32"), False, False),
+            (V, K("f1"), R("hblk"), False, False)])
         ra, rv = [], []
         for p in range(NPC):
             l0, l1 = p * LC // NPC, (p + 1) * LC // NPC
@@ -545,13 +653,11 @@ def rank_program(g, core, T, topo):
                 rv.append(tt(R(hb, m * LC + l0, m * LC + l1), R(cg, 16 * l0 + m, 16 * l1, 16), P(c, 0, l0, l1 - l0), A.is_gt))
         chain(ra)
         chain(rv)
-        for m0 in range(0, 16, 4):
-            opened.append(mm([(P(c, 1, m, 128 - m, 16), R(hb, m * LC, (m + 1) * LC), R("blk", 0, 128, 16), False, m == 15)
-                              for m in range(m0, m0 + 4)], opened))
+        mm([(P(c, 1, m, 128 - m, 16), R(hb, m * LC, (m + 1) * LC), R("blk", 0, 128, 16), False, m == 15) for m in range(16)])
         scan(K("fw"), R("r1"), V, A.max)
         scan(rev(K("mx")), R("r1"), rev(K("fw")), A.max)
         tt(K("M"), V, K("mx"), A.is_equal)
-        act(K("ins"), K("mx"), F.Sign, accum=R(ac, 4, 5) if t < VI - 1 else None)
+        act(K("ins"), K("mx"), F.Sign, accum=R(ac, 1, 2) if t < VI - 1 else None)
         o = P(c, 0, LC)
         msum(o, [(K("M"), R("eye"))])
         tt(K("mc"), o, K("cf"), A.mult)
@@ -565,23 +671,44 @@ def rank_program(g, core, T, topo):
         prod("m1", rw, K("ret"))
         prod("m0", iw, K("nret"))
         tt(K("iv"), K("X"), o, A.mult)
-        fp = P(c, 1, 2 * LC, 2 * LC)
-        msum(fp, [(R("eye"), K("m1")), (R("eye"), K("m0")), (R("eye"), K("iv"), P(c, 1, 2 * LC))])
-        if t < VI - 1:
-            wo = "wo%d_%d" % (t, c)
-            aff("wo", R(wo), fp)
-            remote("p%d_%d" % (t, c), R("w%d_%d" % (t + 1, c)), R(wo))
+        wo, wn = "wo%d_%d" % (t, c), "w%d_%d" % (t + 1, c)
+        if SPLIT or t == VI - 1:
+            for h, tag, y in ((1, "q", "yw"), (0, "p", "ys")):
+                a0, a1 = h * LC, (h + 1) * LC
+                fp = P(c, 1, (2 + h) * LC)
+                parts = [("m1", a0), ("m0", a0)] + ([] if h else [("iv", 0)])
+                if t < VI - 1:
+                    msum(fp, [(R("eye"), K(nm, b0, b0 + LC)) for nm, b0 in parts])
+                    aff("wo", R(wo, a0, a1), fp)
+                    remote("%s%d_%d" % (tag, t, c), R(wn, a0, a1), R(wo, a0, a1))
+                    continue
+                for g2 in range(2):
+                    msum(P(c, 1, (2 + h) * LC + 64 * g2, 64), [(R("out%d%d" % (g2, u)), K(nm, b0 + 64 * u, b0 + 64 * u + 64))
+                                                               for nm, b0 in parts for u in range(2)])
+                yt = K("sx" if h else "ln")
+                if h:
+                    ts(K("ab"), fp, 2048.0, A.is_lt, 4097.0, A.mult)
+                    tt(K("ab"), K("ab"), fp, A.add)
+                    act(yt, K("ab"), F.Copy, -2049.0)
+                else:
+                    act(yt, fp, F.Copy, 2048.0)
+                for c4 in range(4):
+                    turn(R(y + "k", 4 * c + c4, 256, 8), R(yt[0], c4, LC, 4))
+                if c == NCH - 1:
+                    moved[0] = 0.3
+                    dma("a" if h else "s", R(y), R(y + "k"))
         else:
-            act(R("ysk", c * LC, (c + 1) * LC), P(c, 1, 2 * LC), F.Copy, 2048.0)
-            act(R("ywk", c * LC, (c + 1) * LC), P(c, 1, 3 * LC), F.Copy, 2047.0)
-            for r in range(c * NJ, (c + 1) * NJ):
-                dma("s", R("ys", None, None, 1, (r, 128, 16)), R("ysk", 16 * r, 16 * r + 16))
-                dma("a" if c == NCH - 1 else "s", R("yw", None, None, 1, (r, 128, 16)), R("ywk", 16 * r, 16 * r + 16))
+            fp = P(c, 1, 2 * LC, 2 * LC)
+            msum(fp, [(R("eye"), K("m1")), (R("eye"), K("m0")), (R("eye"), K("iv"), P(c, 1, 2 * LC))])
+            aff("wo", R(wo), fp)
+            remote("p%d_%d" % (t, c), R(wn), R(wo))
 
     def count(t):
         PH[0] = "count"
         o = P(0, 3, 3 * LC, 1)
-        msum(o, [(R(m), R("ac%d_%d" % (t, c), q, q + 1)) for c in range(NCH) for m, q in (("all1", 0), ("all16", 4))])
+        for c in range(NCH):
+            ts(R("acb", 2 * c, 2 * c + 2), R("ac%d_%d" % (t, c), 0, 2), 1.0, A.mult)
+        msum(o, [(R(("all1", "all16")[q % 2]), R("acb", q, q + 1)) for q in range(2 * NCH)])
         cp(R("rci", 0, 1), o)
         ts(R("rci", 4, 5), R("rci", 0, 1), 1, A.bitwise_and)
         ts(R("thr", 0, 1), R("rci", 4, 5), -1.0, A.mult, -1.5, A.add)
@@ -597,12 +724,17 @@ def rank_program(g, core, T, topo):
             table(t, c, "er", "nw")
         if t < VI - 1:
             count(t)
+    moved[0] = 4.0
     for j in range(2):
-        dma("s" if j else "a", R("ye", 2048 * j, 2048 * j + 2048), R("er", 2048 * j, 2048 * j + 2048))
+        dma("s", R("ye", 2048 * j, 2048 * j + 2048), R("er", 2048 * j, 2048 * j + 2048))
 
     n = len(ops)
-    HOP = 0.07
     tail = [0.0] * n
+
+    def gap(i, j):
+        if i in ops[j]["soft"]:
+            return 0.0
+        return ops[i]["lat"] + (HOP if ops[j]["q"] != ops[i]["q"] else 0.04)
     succ = [[] for _ in range(n)]
     for i, o in enumerate(ops):
         for d in o["deps"]:
@@ -610,15 +742,16 @@ def rank_program(g, core, T, topo):
     for i in range(n - 1, -1, -1):
         o = ops[i]
         m = LEAD if o["ph"] == "fin0" else 0.0
+        m += o["lat"]
         for j in succ[i]:
-            m = max(m, tail[j])
-        tail[i] = m + o["cost"] + o["lat"] + HOP + (SLACK if o["kind"] == "r" else 0.0)
-    prio = [tail[i] + BIAS.get(ops[i]["ph"], 0.0) for i in range(n)]
+            m = max(m, tail[j] + gap(i, j))
+        tail[i] = m + o["cost"] + (SLACK if o["kind"] == "r" else 0.0)
+    prio = [tail[i] + BIAS.get(ops[i]["ph"], 0.0) + BIAS.get(ops[i]["nm"], 0.0) for i in range(n)]
     pred = [sorted(o["deps"]) for o in ops]
 
     def place(prio, before, after, back):
         left = [len(b) for b in before]
-        ready = [0.0] * n
+        ready = [o["lat"] if back else 0.0 for o in ops]
         start = [0.0] * n
         busy = {q: [] for q in "vatgs"}
         avail = [i for i in range(n) if left[i] == 0]
@@ -626,7 +759,7 @@ def rank_program(g, core, T, topo):
             i = max(avail, key=lambda k: (prio[k], -k))
             avail.remove(i)
             o = ops[i]
-            st = ready[i] + (o["lat"] if back else 0.0)
+            st = ready[i]
             if o["q"] != "x":
                 row = busy[o["q"]]
                 lo, hi = 0, len(row)
@@ -641,9 +774,8 @@ def rank_program(g, core, T, topo):
                     lo += 1
                 row.insert(lo, (st, st + o["cost"]))
             start[i] = st
-            fin = st + o["cost"] + (0.0 if back else o["lat"])
             for j in after[i]:
-                ready[j] = max(ready[j], fin + (HOP if ops[j]["q"] != o["q"] else 0.03))
+                ready[j] = max(ready[j], st + o["cost"] + (gap(j, i) if back else gap(i, j)))
                 left[j] -= 1
                 if left[j] == 0:
                     avail.append(j)

@@ -9,30 +9,43 @@ CA = LC * L
 NJ = LC // 16
 NP = 2
 NPC = 2
-NG = 1
-NF = 1
-NC = 1
+NG = 2
+NF = 2
+NC = 2
 LN2 = math.log(2.0)
 AGE = 7
 LA = 80.0 / AGE
 NDMA = 20
-VFIX = 0.01
-AFIX = 0.09
+ROUNDS = 12000
+SEED = 2
+PM = 0.05
+TEMP = 1.0
+D3 = 0
+JE = 1
+QL = 0
+WQ = 6
+MP = 0
+WK = 0
+VFIX = 0.015
+AFIX = 0.03
+SELF = 0.1
+TFIX = 0.008
 MMC = 128
-FIP = 1
-WB = 1
+FIP = 0
+WB = 6
 ULA = 0
-YV = 0
-SPLIT = 0
+YV = 1
+SPLIT = 2
+RL2 = 4.0
+RHOLD = 1.0
 RLAT = 3.0
-HOP = 0.15
-NER = 4
+HOP = 0.19
+ERS = (0, 512, 1536, 2560, 4096)
+GP = ()
 AQ = "s"
-LEAD = 9.5
-SLACK = 4.0
-PASSES = 2
-BIAS = {'vsm0': -4.0, 'end1': 1.4, 'vgtb': 8.1, 'tfl1': 22.0, 'head1': 0.1, 'tblk0': -1.6, 'tw0': -1.2, 'acg1': -6.6, 'tf1': -2.1, 'run0': 7.2, 'axl0': -4.5, 'agb0': -8.9, 'vmx0': -3.2, 'vhb0': -1.9, 'end0': 3.0, 'fin0': 6.6, 'af1': -11.1, 'vk1': 1.0, 'te0': -4.7, 'pre1': -6.1, 'teye1': -1.6, 'txs1': -1.7, 'anw0': 3.5, 'tX1': -1.1, 'vc0': -1.1, 'te1': -4.5, 'tfm1': -7.8, 'ah0': 7.1, 'net0': -1.0, 'tzx1': -1.2, 'vfi0': -0.5, 'vrcit': -2.2, 'awb0': -8.0, 'agb1': -1.3, 'score0': 1.4, 'vkeep1': -2.0, 'vsg1': -2.9, 'set': -1.3, 'vsh1': -2.2, 'gt': -2.5, 'ains0': -0.6}
-ENG = {'off': 'a', 'e15': 'v', 'slot': 'v', 'yi': 'v', 'ui': 'a', 'vl': 'v', 'ne': 'a', 'xl': 'a', 'sh': 'v', 'c16': 'a', 'cf': 'a', 'wb': 'a', 'wo': 'a', 'sx': 'a', 'ci': 'v', 'ret': 'v', 'nret': 'v', 'w8': 'v', 'ov': 'v', 'y13': 'v', 'kap': 'a', 'D': 'v', 'c0': 'v', 'ng': 'a', 'eh': 'a', 'sg': 'v'}
+LEAD = 8.5
+SLACK = 3.0
+ENG = {'back': 'a', 'zx': 'a', 'X': 'v', 'T': 'v', 'ins': 'a', 'off': 'a', 'e15': 'a', 'slot': 'v', 'yi': 'a', 'ui': 'a', 'vl': 'a', 'ne': 'a', 'xl': 'a', 'sh': 'v', 'c16': 'a', 'cf': 'a', 'wb': 'a', 'wo': 'a', 'sx': 'a', 'ci': 'a', 'ret': 'v', 'nret': 'v', 'w8': 'v', 'ov': 'v', 'y13': 'a', 'kap': 'a', 'D': 'v', 'c0': 'a', 'ng': 'a', 'eh': 'a', 'sg': 'a'}
 NTV = 4
 
 SCRATCH = {}
@@ -66,14 +79,17 @@ for _n in ("i48", "eye", "blk", "tri", "shd", "sh1", "sh2", "sh4", "sh8", "neg",
            "i2048", "mt", "mth", "nblk", "hblk", "blk32", "blkk", "r1", "r2", "tmp", "mr", "m16"):
     _buf(_n, 128, "bfloat16")
 _buf("msk", 256, "bfloat16")
-_buf("al", CA // NP, "bfloat16")
+_buf("wk", 2048, "bfloat16")
+SL = 16
+_buf("al", SL * LC // NP, "bfloat16")
+_buf("a16", 128, "bfloat16")
 _buf("cb", 128, "float16")
 for _n in ("all1", "all16", "acb"):
     _buf(_n, 128, "bfloat16")
 for _n in ("kcol", "kap", "thr", "m1c", "m2c"):
     _buf(_n, 8, "float32")
 _buf("rci", 8, "int32")
-_buf("xbase", 2 * NJ, "bfloat16")
+_buf("xbase", 2 * NJ, "float16")
 _buf("xbi", NJ, "int32")
 for _n in ("stl", "bal"):
     _buf(_n, 16, "uint16")
@@ -86,6 +102,15 @@ for _n in ("in00", "in01", "in10", "in11", "out00", "out01", "out10", "out11"):
 _buf("bari", 256, "int32")
 for _n in ("barb", "sti", "sth", "stc", "stn"):
     _buf(_n, 256, "bfloat16")
+for _n in ("jh", "jum", "jeo", "jeh", "jnw", "jcl", "jsg", "jng", "jo0", "jo1", "jo2", "jo3", "js0", "js1", "js2", "js3"):
+    _buf(_n, 256, "bfloat16")
+for _n in ("jab", "jln"):
+    _buf(_n, 256, "float32")
+for _n in ("jyi", "jy7"):
+    _buf(_n, 256, "int32")
+for _n in ("jui", "juj", "juk", "jvb"):
+    _buf(_n, 16, "int32")
+_buf("jvl", 16, "uint16")
 _buf("actk", 256, "int32")
 _buf("whyk", 256, "int32")
 _buf("ysk", 256, "float32")
@@ -97,15 +122,22 @@ for _c in range(NCH):
         _buf("s%d_%d" % (_t, _c), LC, "bfloat16")
         _buf("so%d_%d" % (_t, _c), LC, "bfloat16")
         _buf("ac%d_%d" % (_t, _c), 8, "float32")
-    _buf("gb%d" % _c, CA + 16, "bfloat16")
-    for _n in ("zb", "fl", "cg", "hb"):
+        _buf("of%d_%d" % (_t, _c), LC, "uint16")
+        _buf("oo%d_%d" % (_t, _c), LC, "uint16")
+    for _n in ("gb%d" % _c, "zb%d" % _c):
+        if D3 and _n[0] == "g":
+            SCRATCH[_n] = ("sbuf", [128, LC, 17], "bfloat16")
+            LOG[_n] = ("sbuf", 17 * LC, "bfloat16", _n, 0)
+        else:
+            _buf(_n, CA + 16, "bfloat16")
+    for _n in ("fl", "cg", "hb"):
         _buf("%s%d" % (_n, _c), CA, "bfloat16")
     for _n in ("e15", "h", "q", "um", "ov", "st", "XL", "X", "zx", "nx", "w8", "f1", "T", "M", "ins", "ret", "nret", "ne", "keep", "fm",
                "eo", "eh", "nw", "cl", "sg", "ng"):
         _buf("%s_%d" % (_n, _c), LC, "bfloat16")
     for _n in ("xs", "ds", "cf", "mc", "iqe", "fi", "fw", "mx", "iv"):
         _buf("%s_%d" % (_n, _c), LC, "float16")
-    for _n in ("a1", "a2", "m0", "m1", "m2", "m3", "wb", "xm"):
+    for _n in ("a1", "a2", "m0", "m1", "m2", "m3", "wb", "xm", "wb0", "wb1", "wb2"):
         _buf("%s_%d" % (_n, _c), 2 * LC, "float16")
     for _n in ("yi", "y7", "pr", "sh", "sm", "ci", "cn", "c0", "k0", "k1", "k2", "k3"):
         _buf("%s_%d" % (_n, _c), LC, "int32")
@@ -133,6 +165,112 @@ def overlap(a, b):
     return True
 
 
+PLACED = []
+
+
+def arrange(ops, tail, gap):
+    n = len(ops)
+    qs, cost, lat = [o["q"] for o in ops], [o["cost"] for o in ops], [o["lat"] for o in ops]
+    before, above, same, seen, last = [], [0] * n, [], {}, None
+    for j, o in enumerate(ops):
+        near, far = [], 0
+        for i in sorted(o["deps"], reverse=True):
+            if not (far >> i & 1 and lat[i] == 0):
+                near.append((i, gap(i, j)))
+                far |= above[i]
+        above[j] = far | sum(1 << i for i in o["deps"])
+        before.append(near)
+        if o["ph"] == "run0" and last != "run0":
+            seen = {}
+        last = o["ph"]
+        seen[last, o["nm"]] = seen.get((last, o["nm"]), 0) + 1
+        same.append((last, o["nm"], seen[last, o["nm"]]))
+
+    def place(shift, was=None):
+        prio = [0.0] * n
+        for j in range(n):
+            p = tail[j] + shift.get(same[j], 0.0)
+            for i, _ in before[j]:
+                if prio[i] <= p:
+                    p = prio[i] - 1e-6
+            prio[j] = p
+        end = [0.0] * n
+        busy = {q: ([], []) for q in "vatgs"}
+        for _, j in sorted(zip(prio, range(n)), reverse=True):
+            st, c = 0.0, cost[j]
+            for i, d in before[j]:
+                if end[i] + d > st:
+                    st = end[i] + d
+            if qs[j] == "x":
+                if was and same[j][0][:3] == "fin" and st > was[j] + 1.5:
+                    return 1e9, end, prio
+            else:
+                a, b = busy[qs[j]]
+                lo = m = len(a)
+                while lo and b[lo - 1] > st:
+                    lo -= 1
+                while lo < m and a[lo] < st + c:
+                    st = b[lo] if b[lo] > st else st
+                    lo += 1
+                a.insert(lo, st)
+                b.insert(lo, st + c)
+            end[j] = st + c
+        return max(end[j] + lat[j] for j in range(n)), end, prio
+
+    def held(end):
+        ahead, cur, out = {}, {}, []
+        for j in sorted(range(n), key=lambda k: end[k]):
+            ahead[j] = cur.get(qs[j])
+            cur[qs[j]] = j
+        j = max(range(n), key=lambda k: end[k] + lat[k])
+        while j is not None:
+            ready, i = max([(end[i] + d, i) for i, d in before[j]] + [(0.0, None)], key=lambda u: u[0])
+            if end[j] - cost[j] - ready > 1e-6 and ahead[j] is not None:
+                i = ahead[j]
+                out.append((j, i))
+            j = i
+        return out
+
+    part = {}
+    for e in sorted(set(same)):
+        part.setdefault(e[0], []).append(e)
+    seed = [SEED]
+
+    def rnd():
+        seed[0] = (seed[0] * 1103515245 + 12345) % 2147483648
+        return seed[0] / 2147483648.0
+
+    shift = {}
+    span, end, prio = place(shift)
+    best, pairs = (span, end), held(end)
+    for r in range(ROUNDS):
+        new = dict(shift)
+        for _ in range(1 + (rnd() < 0.33)):
+            j, i = pairs[int(rnd() * len(pairs))]
+            d, k = prio[i] - prio[j], rnd()
+            if k < PM:
+                u, v = same[j if rnd() < 0.5 else i][0], 2.0 * (rnd() - 0.5)
+                for e in part[u]:
+                    new[e] = new.get(e, 0.0) + v
+            elif d < 0 or k < PM + 0.12:
+                u = same[j if rnd() < 0.5 else i]
+                new[u] = new.get(u, 0.0) + 3.0 * (rnd() - 0.5)
+            elif k < 0.6:
+                row, top = [j], prio[i] + 0.5 * rnd()
+                for u in row:
+                    new[same[u]] = top - tail[u] + 0.01 * len(row)
+                    row += [e for e, _ in before[u] if prio[e] < top and e not in row and len(row) < 12]
+            else:
+                new[same[i]] = prio[j] - tail[i] - 0.5 * rnd()
+        span2, end2, prio2 = place(new, end)
+        if span2 <= span + TEMP * (1.0 - r / ROUNDS) * rnd():
+            shift, span, end, prio = new, span2, end2, prio2
+            pairs = held(end)
+            if span < best[0]:
+                best = (span, end)
+    return [best[1][j] - cost[j] for j in range(n)], best[0]
+
+
 def rank_program(g, core, T, topo):
     rank = T.rank_of(core)
     if rank is None:
@@ -154,7 +292,13 @@ def rank_program(g, core, T, topo):
     def rev(r):
         return (r[0], r[1], r[2], -1, None)
 
+    def S3(name, l0, l1, k0, k1):
+        return (name, 17 * l0, 17 * l1, 0, None, (k0, k1))
+
     def ap(r):
+        if r[3] == 0:
+            k0, k1 = r[5]
+            return T[r[0]][:, r[1] // 17:r[2] // 17, k0] if k1 == k0 + 1 else T[r[0]][:, r[1] // 17:r[2] // 17, k0:k1]
         t, o = (LOG[r[0]][3], LOG[r[0]][4]) if r[0] in LOG else (r[0], 0)
         if r[4] is not None:
             return T[t][r[4][0]:r[4][1]:r[4][2], o + r[1]:o + r[2]]
@@ -175,6 +319,8 @@ def rank_program(g, core, T, topo):
         return r
 
     def n_of(r):
+        if r[3] == 0:
+            return (r[2] - r[1]) // 17 * (r[5][1] - r[5][0])
         return -(-(r[2] - r[1]) // abs(r[3]))
 
     def add(q, fns, reads, writes, cost, kind="c", lat=0.0, sem=None, inc=0, extra=(), soft=()):
@@ -239,8 +385,8 @@ def rank_program(g, core, T, topo):
         return add("v", [f], [a, s1, s2], [out], vc(n_of(out), rate))
 
     def cp(out, a):
-        rate = 4.0 if out[0] == "IND" else (0.5 if two(out, a) else 1.0)
-        return add("v", [lambda: g.vector.tensor_copy(x(out), x(a))], [a], [out], vc(n_of(a), rate))
+        rate = 4.0 if out[0] == "IND" else 1.8 if a[0] == "IND" else (0.5 if two(out, a) else 1.0)
+        return add("v", [lambda: g.vector.tensor_copy(x(out), x(a))], [a], [out], vc(n_of(out if a[0] == "IND" else a), rate))
 
     def turn(out, a):
         return add("v", [lambda: g.vector.transpose(x(out), x(a))], [a], [out], vc(n_of(a), 1.0))
@@ -291,7 +437,7 @@ def rank_program(g, core, T, topo):
             rows[-1].append(it)
             cols += n
         for row in rows:
-            fns, rd, wr, cost = [], [], [], 0.01
+            fns, rd, wr, cost = [], [], [], TFIX * len(row)
             for (o, l, r, s, e) in row:
                 fns.append(lambda o=o, l=l, r=r, s=s, e=e: g.tensor.matmul(x(o), x(l), x(r), s, e))
                 rd += [l, r]
@@ -319,7 +465,7 @@ def rank_program(g, core, T, topo):
             m |= 1 << e
         rid, pid = topo.addr(nxt)[0], topo.addr(nxt)[1]
         ra, la = T.sem["a" + tag], T.sem["l" + tag]
-        i = add("g", [lambda: g.remote_dma(ap(out), ap(a), ra, la, pid, rid, m)], [a], [], 1.0, "r", RLAT, "l" + tag, ne)
+        i = add("g", [lambda: g.remote_dma(ap(out), ap(a), ra, la, pid, rid, m)], [a], [], RHOLD, "r", RLAT if tag[0] == "p" else RL2, "l" + tag, ne)
         return add("x", [], [], [out], 0.0, "x", 0.0, "a" + tag, ne, (i,))
 
     def P(c, i, a=0, n=LC, st=1):
@@ -331,9 +477,9 @@ def rank_program(g, core, T, topo):
         fill(BC[nm], v)
     act(R("m1c", 2, 3), BC["least"], F.Ln, None, 2.0 ** (8 * AGE))
     ts(R("m1c", 3, 4), R("m1c", 2, 3), -LA / LN2, A.mult, -0.21, A.add)
-    for j in range(NER):
-        dma("s", R("er", W // NER * j, W // NER * (j + 1)), R("eff", W // NER * j, W // NER * (j + 1)))
-        if j == NER - 1:
+    for j, (c0, c1) in enumerate(zip(ERS, ERS[1:])):
+        dma("s", R("er", c0, c1), R("eff", c0, c1))
+        if c1 == W:
             dma(AQ, R("actk"), R("act"))
             dma(AQ, R("sti"), R("st0"))
     chain([i for i, o in enumerate(ops) if o["q"] == "a"])
@@ -360,7 +506,7 @@ def rank_program(g, core, T, topo):
     iota(R("kc"), [[0, 16], [1, 16]], 0, 0)
     keep(R("tmp"), R("all1"), row(0), A.is_ge, 0.0)
     keep(R("blk"), R("tmp"), ([[16, 8], [0, 16]], 15, -1), A.is_ge, 0.0)
-    iota(R("xbi"), [[256, NJ]], 0, 0)
+    iota(R("xbi"), [[16 * SL, NJ]], 0, 0)
     iota(R("lb"), [[64, 2], [128, 2], [4, 4]], 0, 0)
     iota(R("lc"), [[4, 2], [8, 2], [64, 4]], 0, 0)
     for g2 in range(2):
@@ -381,31 +527,36 @@ def rank_program(g, core, T, topo):
     keep(R("mt"), R("sh1"), row(0), A.not_equal, 0.5)
     keep(R("mt"), R("mt"), ([[-16, 8], [128, 16]], 0, 1), A.not_equal, -0.5)
     fill(R("al"), 2.0 ** -AGE)
-    fill(R("al", 0, CA // NP, 16), 0.0)
-    scan(rev(R("mth")), R("al", 0, 128), rev(R("i48")), A.add)
+    fill(R("al", 0, SL * LC // NP, SL), 0.0)
+    fill(R("a16"), 2.0 ** -AGE)
+    fill(R("a16", 0, 128, 16), 0.0)
+    scan(rev(R("mth")), R("a16"), rev(R("i48")), A.add)
     keep(R("mth"), R("mth"), ([[-1, 128]], 0, 1), A.is_ge, 48.0)
     keep(R("mth"), R("mth"), row(0), A.is_ge, 0.0)
-    for nm, f in (("nblk", -1.0), ("hblk", 0.5), ("b125", -12.5), ("blk32", 32.0), ("blkk", R("kcol", 0, 1))):
+    for nm, f in (("nblk", -1.0), ("hblk", 0.5), ("b125", -12.5), ("blk32", -33.0), ("blkk", R("kcol", 0, 1))):
         ts(R(nm), R("blk"), f, A.mult)
     ts(R("msk"), R("kc"), R("kcol", 0, 1), A.is_equal)
     keep(R("r1"), R("all1"), ([[0, 8], [1, 16]], -1, 0), A.is_ge, 0.0)
     ts(R("r2"), R("r1"), 2.0, A.mult)
-    ts(R("cb"), R("kc", 0, 128), -1.0 / 32, A.mult, -39.5, A.add)
+    ts(R("cb"), R("kc", 0, 128), -1.0 / 32, A.mult, 25.5, A.add)
     keep(R("cb"), R("cb"), row(1), A.is_equal, 0.0)
     keep(R("cb"), R("cb"), row(0), A.not_equal, -1.0)
+    for r in range(16 * WK):
+        keep(R("wk", 128 * r, 128 * r + 128), R("blk"), ([[0, 8], [1, 16]], -r, 0), A.is_equal, 0.0)
     keep(R("mr"), R("nblk"), c_p(0), A.is_ge, 0.0)
     keep(R("mr"), R("mr"), c_p(0), A.not_equal, 63.0)
     ts(R("kap", 0, 1), R("kcol", 0, 1), 241.0, A.mult, 101.0, A.add)
     for t in range(VI):
         ts(R("kap", 4 + t, 5 + t), R("kap", 0, 1), 2048.0, A.mult, float(97 * t), A.add)
     ts(R("m2c", 0, 1), R("kcol", 0, 1), 15.0, A.is_equal, -0.5, A.add)
+    if ENG["T"] == "v":
+        ts(R("m2c", 0, 1), R("m2c", 0, 1), 2.0, A.mult)
     ts(R("m2c", 1, 2), R("kcol", 0, 1), 1.0, A.add)
     ts(R("m2c", 2, 3), R("kcol", 0, 1), -63.0, A.add)
     fill(R("thr", 0, 1), -1.5)
-    fill(R("all16"), 1.0 / 16.0)
-    ts(R("kcol", 2, 3), R("kcol", 0, 1), 16.0, A.mult)
+    ts(R("kcol", 2, 3), R("kcol", 0, 1), float(SL), A.mult, -1024.0, A.add)
     ts(R("xbase", 0, NJ), R("xbi"), R("kcol", 2, 3), A.add)
-    fill(R("xbase", NJ, 2 * NJ), 2048.0)
+    fill(R("xbase", NJ, 2 * NJ), 1024.0)
     ts(R("kq", 0, 1), R("kp", 0, 1), 3, A.bitwise_and)
     ts(R("kq", 4, 5), R("kp", 0, 1), 2, A.arith_shift_right)
     cp(R("kcol", 4, 5), R("kq", 0, 1))
@@ -414,7 +565,7 @@ def rank_program(g, core, T, topo):
     ts(R("kcol", 7, 8), R("kcol", 5, 6), 16.0, A.mult, R("kcol", 4, 5), A.add)
     ts(R("stl"), R("lb"), R("kcol", 6, 7), A.add)
     ts(R("bal"), R("lc"), R("kcol", 7, 8), A.add)
-    for c in range(NCH):
+    for c in range(0 if JE else NCH):
         ts(R(("vc_%d" if ULA else "vb_%d") % c), R("lb", c * NJ, (c + 1) * NJ), R("kcol", 6, 7), A.add, 16.0, A.mult)
     act(R("barb"), ind(R("bari"), R("bal")), F.Copy)
     ts(R("an", 0, 256), R("actk"), -2048.0, A.add)
@@ -433,17 +584,27 @@ def rank_program(g, core, T, topo):
     ts(R("sth"), R("sti"), 8.0, A.is_lt, 25.0, A.mult)
     ts(R("stn"), R("sti"), -1.0, A.mult, -5.0, A.add)
     tt(R("stc"), R("stn"), R("sth"), A.add)
-    for c in range(NCH):
+    if JE:
+        act(R("js0"), ind(R("stc"), R("stl")), F.Copy)
+        ts(R("jvb"), R("lb"), R("kcol", 6, 7), A.add, 16.0, A.mult)
+    for c in range(0 if JE else NCH):
         act(R("s0_%d" % c), ind(R("stc"), R("stl", c * NJ, (c + 1) * NJ)), F.Copy)
 
     PH[0] = "gt"
     for j in range(8):
         c0, c1 = 512 * j, 512 * j + 512
         b = R("p%d" % j)
-        ts(R("tcl", c0, c1), R("er", c0, c1), 4.0, A.max, 11.0, A.min)
-        msum(b, [(R("n16"), R("er", c0, c1)), (R("e16"), R("tcl", c0, c1))])
-        act(R("tsg", c0, c1), b, F.Sign)
-        tt(R("gt", c0, c1), R("tsg", c0, c1), b, A.add)
+        if j in GP:
+            act(b, R("er", c0, c1), F.Copy, None, 1.0 / 16)
+            ts(R("tcl", c0, c1), b, 4.0 / 16, A.max, 11.0 / 16, A.min)
+            tt(R("tsg", c0, c1), R("tcl", c0, c1), b, A.subtract)
+            act(b, R("tsg", c0, c1), F.Sign)
+            tt(R("gt", c0, c1), R("tsg", c0, c1), b, A.add)
+        else:
+            ts(R("tcl", c0, c1), R("er", c0, c1), 4.0, A.max, 11.0, A.min)
+            msum(b, [(R("n16"), R("er", c0, c1)), (R("e16"), R("tcl", c0, c1))])
+            act(R("tsg", c0, c1), b, F.Sign)
+            tt(R("gt", c0, c1), R("tsg", c0, c1), b, A.add)
         if j == 7:
             plans(0)
             PH[0] = "gt"
@@ -468,18 +629,30 @@ def rank_program(g, core, T, topo):
         PH[0] = "run%d" % c
         gb, zb, fl = "gb%d" % c, "zb%d" % c, "fl%d" % c
         w, s = "w%d_%d" % (t, c), "s%d_%d" % (t, c)
-        aff("off", K("off"), R(w, 0, LC), None, 2048.0)
+        of = "of%d_%d" % (t, c)
+        if SPLIT < 2 or t == 0:
+            aff("off", R(of), R(w, 0, LC), None, 2048.0)
+        elif QL or MP:
+            aff("back", R(w, 0, LC), R(of), None, -2048.0)
         ra, rv = [], []
         for p in range(NP):
             l0, l1 = p * LC // NP, (p + 1) * LC // NP
             e0, e1 = 16 * l0, 16 * l1
+            if D3:
+                aff("slot", S3(gb, l0, l1, 0, 1), R(s, l0, l1), 1.0 / 16)
+                for (a0, a1) in cut(l0, l1, NG):
+                    ra.append(act(S3(gb, a0, a1, 1, 17), ind(R("gt"), R(of, a0, a1)), F.Copy))
+                rv.append(scan(R(zb, e0, e1), R("al"), S3(gb, l0, l1, 0, 16), A.add))
+                for (a0, a1) in cut(l0, l1, NF):
+                    rv.append(tt(R(fl, 16 * a0, 16 * a1), ind(R("nt"), R(of, a0, a1)), R(zb, 16 * a0, 16 * a1), A.is_lt))
+                continue
             for (a0, a1) in cut(l0, l1, NG):
-                ra.append(act(R(gb, 16 * a0 + 1, 16 * a1 + 1), ind(R("gt"), K("off", a0, a1)), F.Copy))
+                ra.append(act(R(gb, 16 * a0 + 1, 16 * a1 + 1), ind(R("gt"), R(of, a0, a1)), F.Copy))
             aff("e15", K("e15", l0, l1), R(gb, e0 + 16, e1 + 1, 16))
-            aff("slot", R(gb, e0, e1, 16), R(s, l0, l1), 1.0 / 16)
+            aff("slot", R(gb, e0, e1, 16), R("js%d" % t, c * LC + l0, c * LC + l1) if JE else R(s, l0, l1), 1.0 / 16)
             rv.append(scan(R(zb, e0, e1), R("al"), R(gb, e0, e1), A.add))
             for (a0, a1) in cut(l0, l1, NF):
-                rv.append(tt(R(fl, 16 * a0, 16 * a1), ind(R("nt"), K("off", a0, a1)), R(zb, 16 * a0, 16 * a1), A.is_lt))
+                rv.append(tt(R(fl, 16 * a0, 16 * a1), ind(R("nt"), R(of, a0, a1)), R(zb, 16 * a0, 16 * a1), A.is_lt))
         chain(ra)
         chain(rv)
         mm([(P(c, 1, k, 128 - k, 16), R(fl, k, CA, 16), R("blk", 0, 128, 16), True, True) for k in range(16)])
@@ -487,9 +660,11 @@ def rank_program(g, core, T, topo):
             act(K("ov"), P(c, 1), F.Sign, R("thr", 0, 1))
         else:
             ts(K("ov"), P(c, 1), R("thr", 0, 1), A.add, 0.0, A.is_gt)
+        if JE:
+            return
         PH[0] = "end%d" % c
         o = P(c, 2)
-        msum(o, [(R("ial"), R(zb, 15, CA, 16)), (R("eye"), K("e15"))])
+        msum(o, [(R("eye"), S3(gb, 0, LC, 16, 17) if D3 else K("e15")), (R("ial"), R(zb, 15, CA, 16))])
         act(K("ab"), o, F.Abs)
         act(K("h"), o, F.Sign)
         act(K("ln"), K("ab"), F.Ln, None, 2.0 ** (8 * AGE))
@@ -529,9 +704,48 @@ def rank_program(g, core, T, topo):
         else:
             cp(ind(R("er"), K("vl")), K("nw"))
 
+    def end(t):
+        PH[0] = "end1"
+        lo, hi = P(1, 2, 0, 256), P(1, 2, 256, 256)
+        for c in range(NCH):
+            msum(P(1, 2, c * LC), [(R("eye"), R("e15_%d" % c)), (R("ial"), R("zb%d" % c, 15, CA, 16))])
+        act(R("jab"), lo, F.Abs)
+        act(R("jh"), lo, F.Sign)
+        act(R("jln"), R("jab"), F.Ln, None, 2.0 ** (8 * AGE))
+        aff("yi", R("jyi"), R("jln"), LA / LN2, R("m1c", 3, 4))
+        ts(R("jy7"), R("jyi"), 7, A.bitwise_and)
+        sv = "jo%d" % t
+        aff("y13", lo, R("jy7"), None, 13.0)
+        tt(R(sv), R("jh"), lo, A.mult)
+        if t < VI - 1:
+            remote("s%d_0" % t, R("js%d" % (t + 1)), R(sv))
+        for c in range(NCH):
+            msum(P(1, 2, 256 + c * LC), [(R(sv, c * LC, (c + 1) * LC), R("blk")), (R("jh", c * LC, (c + 1) * LC), R("b125"))])
+        tt(R("jum"), hi, R("msk"), A.mult)
+        o = P(1, 2, 0, 2 * NJ)
+        mm([(u[2], u[0], u[1], True, True) for u in pick(o, "jum", NCH)])
+        aff("ui", R("jui"), o, -1.0, 120.0)
+        ts(R("juj"), R("jui"), 15, A.bitwise_and)
+        tt(R("juk"), R("juj"), R("jvb"), A.add)
+        aff("vl", R("jvl"), R("juk"))
+        act(R("jeo"), ind(R("er"), R("jvl")), F.Copy)
+        msum(lo, [(R("neg"), R(sv)), (R("i125"), R("jh")), (R("eye"), R("jeo"))])
+        aff("eh", R("jeh"), lo, 0.5, 195.5)
+        aff("ne", R("jnw"), R("jeh"), None, -192.0)
+        if t < VI - 1:
+            ts(R("jcl"), R("jeh"), 196.0, A.max, 203.0, A.min)
+            aff("sg", R("jsg"), R("jeh"), 0.125, 167.0625)
+            msum(hi, [(R("n16"), R("jeh")), (R("e16"), R("jcl")), (R("neg"), R("jsg"))])
+            aff("ng", R("jng"), hi, None, 192.0)
+        else:
+            for c in range(NCH):
+                cp(ind(R("er"), R("jvl", c * NJ, (c + 1) * NJ)), R("jnw", c * LC, (c + 1) * LC))
+
     def table(t, c, tab, new):
         PH[0] = "tab"
-        if t < VI - 1:
+        if t < VI - 1 and JE:
+            cp(ind(R(tab), R("jvl", c * NJ, (c + 1) * NJ)), R("j" + new, c * LC, (c + 1) * LC))
+        elif t < VI - 1:
             cp(ind(R(tab), R("vl_%d" % c)), R("%s_%d" % (new, c)))
 
     def cand(t, c):
@@ -545,18 +759,27 @@ def rank_program(g, core, T, topo):
         ts(K("XL"), K("st"), 1.0, A.is_equal)
         o = P(c, 0)
         msum(o, [(K("XL"), R("eye"))])
-        act(K("X"), o, F.Copy, accum=R(ac, 0, 1) if t < VI - 1 else None)
-        tt(K("xs"), S_, o, A.mult)
-        mm([(P(c, 1, LC), K("X"), R("blkk"), True, True), (P(c, 1, 2 * LC), K("xs"), R("blk"), True, True)])
-        tt(K("xm"), P(c, 1, LC, 2 * LC), R("msk"), A.mult)
-        o = P(c, 0, LC, 2 * NJ)
-        msum(o, [(R("eye"), R("xbase"))] + pick(o, "xm_%d" % c, 2))
-        aff("xl", K("xl"), o)
+        xs = K("xm", LC, 2 * LC) if WK else K("xs")
+        tt(xs, S_, o, A.mult)
+        if WK:
+            ts(K("xm", 0, LC), o, R("kcol", 0, 1), A.mult)
+            aff("X", K("X"), o)
+            o = P(c, 1, LC, 2 * NJ)
+            msum(o, [(R("eye"), R("xbase"))] + [(R("wk", 128 * r, 128 * r + 128), K("xm", r, 2 * LC, 16)) for r in range(16)])
+        else:
+            aff("X", K("X"), o)
+            mm([(P(c, 1, LC), K("X"), R("blkk"), True, True), (P(c, 1, 2 * LC), K("xs"), R("blk"), True, True)])
+            tt(K("xm"), P(c, 1, LC, 2 * LC), R("msk"), A.mult)
+            o = P(c, 0, LC, 2 * NJ)
+            msum(o, [(R("eye"), R("xbase"))] + pick(o, "xm_%d" % c, 2))
+        aff("xl", K("xl"), o, None, 1024.0)
         sx, kap = P(c, 3, 2 * LC), P(c, 3, 3 * LC)
-        msum(sx, [(R("blk"), K("xs"))])
+        msum(sx, [(R("blk"), xs)])
         aff("sx", K("sx"), sx, None, 2048.0)
         aff("kap", kap, sx, R("kap", 0, 1), R("kap", 4 + t, 5 + t))
-        act(K("zx"), ind(R("zb%d" % c), K("xl", 0, NJ)), F.Copy)
+        if QL:
+            msum(sx, [(R("eye"), S_)])
+        aff("zx", K("zx"), ind(R("zb%d" % c, 0, CA), K("xl", 0, NJ)))
         if YV:
             tt(K("nx"), ind(R("nt"), K("xl", NJ, 2 * NJ)), K("zx"), A.subtract)
             if ENG["w8"] == "a":
@@ -572,7 +795,10 @@ def rank_program(g, core, T, topo):
             act(K("f1"), o, F.Sign)
         o = P(c, 0, 2 * LC)
         msum(o, [(R("mth"), K("X")), (R("nblk"), K("w8"))])
-        act(K("T"), o, F.Sign)
+        if ENG["T"] == "a":
+            act(K("T"), o, F.Sign)
+        else:
+            ts(K("T"), o, 0.0, A.is_gt, 2.0, A.mult)
         D = P(c, 3)
         msum(D, [(R("eye"), K("X")), (R("mt"), K("T"))])
         relu("D", D, D, R("m2c", 0, 1))
@@ -592,6 +818,52 @@ def rank_program(g, core, T, topo):
         def prod(n, wd, mask):
             tt(K(n, 0, LC), R(wd[0], wd[1], wd[1] + LC), mask, A.mult)
             tt(K(n, LC, 2 * LC), R(wd[0], wd[1] + LC, wd[1] + 2 * LC), mask, A.mult)
+
+        def change(f):
+            a0, a1 = f * LC, (f + 1) * LC
+            old, reg = R(w, a0, a1), [P(c, 3 - f, q * LC) for q in range(4)]
+            PH[0] = ("net%d", "why%d")[f] % c
+            if f:
+                msum(reg[2], [(R("eye"), old)])
+            tt(K("a2", a0, a1), reg[2], K("keep"), A.mult)
+            tt(K("m0", a0, a1), reg[2], K("k0"), A.mult)
+            msum(reg[1], [(R("tri"), K("X"))])
+            tt(K("a1", a0, a1), old, reg[1], A.mult)
+            msum(reg[0], [(R("eye"), old), (R("shd"), K("a1", a0, a1))] + [(R("eye"), K("iqe"))] * f)
+            terms = [(R("eye"), K("a2", a0, a1))]
+            for s in range(4):
+                cur = reg[3 - s % 2]
+                if s == 3:
+                    terms.append((R("i2048"), K("fm")) if f else (R("eye"), K("fi")))
+                terms.append((R("sh%d" % (1 << s)), K("m%d" % s, a0, a1)))
+                msum(cur, terms)
+                if s < 3:
+                    tt(K("m%d" % (s + 1), a0, a1), cur, K("k%d" % (s + 1)), A.mult)
+                if (WB, WQ)[f] >> (s + 1) & 1:
+                    aff("wb", K("wb%d" % s, a0, a1), cur)
+                    terms = [(R("eye"), K("wb%d" % s, a0, a1))]
+            return reg
+
+        if QL:
+            aff("cf", K("cf"), K("ci"), None, -2048.0)
+            tt(K("ne"), Q_, sdp, A.not_equal)
+            tt(K("keep"), K("ne"), D, A.is_gt)
+            tt(K("iqe"), K("X"), sdp, A.mult)
+            mm([(P(c, 1, LC), R("mr"), K("keep"), True, True), (P(c, 1, 2 * LC), R("tri"), K("keep"), True, True),
+                (P(c, 1, 3 * LC), R("blk"), K("keep"), True, True)])
+            relu("c0", K("c0"), P(c, 1, LC), R("m2c", 2, 3))
+            aff("ci", K("cn"), P(c, 1, 2 * LC), -1.0, R("m2c", 1, 2))
+            ts(K("fm"), P(c, 1, 3 * LC), R("kcol", 0, 1), A.is_le)
+            ts(K("k0"), K("c0"), 1, A.bitwise_and)
+            for s in range(1, 4):
+                ts(K("k%d" % s), K("cn"), s, A.arith_shift_right, 1, A.bitwise_and)
+            if FIP:
+                act(P(c, 1, LC), K("ci"), F.Copy, -2048.0)
+                tt(K("fi"), K("fm"), P(c, 1, LC), A.mult)
+            else:
+                tt(K("fi"), K("fm"), K("cf"), A.mult)
+            regs = [change(0), change(1)]
+            return score(t, c, [regs[0][2], regs[1][2]], [regs[0][0], regs[1][0]])
         wp = P(c, 2, 0, 2 * LC)
         aff("cf", K("cf"), K("ci"), None, -2048.0)
         msum(wp, [(R("eye"), W_)])
@@ -625,16 +897,27 @@ def rank_program(g, core, T, topo):
             cur = (P(c, 2, 2 * LC, 2 * LC), P(c, 3, 2 * LC, 2 * LC), wp, P(c, 3, 2 * LC, 2 * LC))[s]
             move = (R("sh%d" % (1 << s)), K("m%d" % s))
             if s == 3:
-                if WB:
+                if WB == 1:
                     terms = [(R("eye"), K("wb")), terms[-1]]
                 terms += [(R("eye"), K("fi"), P(c, 3, 2 * LC)), (R("i2048"), K("fm"), P(c, 3, 3 * LC))]
             terms.append(move)
             msum(cur, terms)
             if s < 3:
                 prod("m%d" % (s + 1), cur, K("k%d" % (s + 1)))
-            if s == 1 and WB:
+            if s == 1 and WB == 1:
                 aff("wb", K("wb"), cur)
-        rw = cur
+            if WB > 1 and WB >> (s + 1) & 1:
+                aff("wb", K("wb%d" % s), cur)
+                terms = [(R("eye"), K("wb%d" % s))]
+        if MP and t < VI - 1:
+            act(K("a2"), iw, F.Copy)
+            act(K("wb2"), cur, F.Copy)
+        score(t, c, [P(c, 3, 2 * LC), P(c, 3, 3 * LC)], [P(c, 3), P(c, 3, LC)])
+
+    def score(t, c, rw, iw):
+        def K(n, *a):
+            return R("%s_%d" % (n, c), *a)
+        ac = "ac%d_%d" % (t, c)
         PH[0] = "score%d" % c
         hb, cg = "hb%d" % c, "cg%d" % c
         rr, V = P(c, 0), P(c, 1)
@@ -657,22 +940,62 @@ def rank_program(g, core, T, topo):
         scan(K("fw"), R("r1"), V, A.max)
         scan(rev(K("mx")), R("r1"), rev(K("fw")), A.max)
         tt(K("M"), V, K("mx"), A.is_equal)
-        act(K("ins"), K("mx"), F.Sign, accum=R(ac, 1, 2) if t < VI - 1 else None)
+        if ENG["ins"] == "a":
+            act(K("ins"), K("mx"), F.Sign, accum=R(ac, 1, 2) if t < VI - 1 else None)
+        else:
+            ts(K("ins"), K("mx"), 0.0, A.is_gt)
+            if t < VI - 1:
+                act(K("fw", 0, 8), K("mx", 0, LC, 16), F.Sign, accum=R(ac, 1, 2))
         o = P(c, 0, LC)
         msum(o, [(K("M"), R("eye"))])
         tt(K("mc"), o, K("cf"), A.mult)
         PH[0] = "fin%d" % c
         o = P(c, 1, LC)
-        msum(o, [(R("blk"), K("X")), (K("ins"), R("neg"))])
-        aff("ret", K("ret"), o)
-        aff("nret", K("nret"), o, -1.0, 1.0)
+        msum(o, [(K("ins"), R("eye"))])
+        wo, wn = "wo%d_%d" % (t, c), "w%d_%d" % (t + 1, c)
+        if MP and t < VI - 1:
+            for f in range(2):
+                tt(K("m1", f * LC, (f + 1) * LC), K("wb2", f * LC, (f + 1) * LC), o, A.mult)
+                tt(K("m0", f * LC, (f + 1) * LC), K("a2", f * LC, (f + 1) * LC), o, A.mult)
+            o = P(c, 0, 2 * LC)
+            msum(o, [(R("blk"), K("mc"))])
+            tt(K("iv"), K("X"), o, A.mult)
+            fp = P(c, 2)
+            msum(fp, [(R("eye"), K("wb2", 0, LC)), (R("neg"), K("m1", 0, LC)), (R("eye"), K("m0", 0, LC)), (R("eye"), K("iv"))])
+            aff("off", R("oo%d_%d" % (t, c)), fp, None, 2048.0)
+            remote("p%d_%d" % (t, c), R("of%d_%d" % (t + 1, c)), R("oo%d_%d" % (t, c)))
+            msum(P(c, 2, LC), [(R("eye"), K("wb2", LC, 2 * LC)), (R("neg"), K("m1", LC, 2 * LC)), (R("eye"), K("m0", LC, 2 * LC))])
+            aff("wo", R(wo, LC, 2 * LC), P(c, 2, LC))
+            remote("q%d_%d" % (t, c), R(wn, LC, 2 * LC), R(wo, LC, 2 * LC))
+            return
+        aff("ret", K("ret"), o, -1.0, 1.0)
+        aff("nret", K("nret"), o)
         o = P(c, 0, 2 * LC)
         msum(o, [(R("blk"), K("mc"))])
-        prod("m1", rw, K("ret"))
-        prod("m0", iw, K("nret"))
+        for f in range(2):
+            PH[0] = ("why%d" if f and QL and t < VI - 1 else "fin%d") % c
+            tt(K("m1", f * LC, (f + 1) * LC), rw[f], K("ret"), A.mult)
+            tt(K("m0", f * LC, (f + 1) * LC), iw[f], K("nret"), A.mult)
+        PH[0] = "fin%d" % c
         tt(K("iv"), K("X"), o, A.mult)
-        wo, wn = "wo%d_%d" % (t, c), "w%d_%d" % (t + 1, c)
-        if SPLIT or t == VI - 1:
+        if QL and t < VI - 1:
+            fp = P(c, 1, 2 * LC)
+            msum(fp, [(R("eye"), K(nm, 0, LC)) for nm in ("m1", "m0", "iv")])
+            aff("off", R("oo%d_%d" % (t, c)), fp, None, 2048.0)
+            remote("p%d_%d" % (t, c), R("of%d_%d" % (t + 1, c)), R("oo%d_%d" % (t, c)))
+            PH[0] = "why%d" % c
+            msum(P(c, 2, LC), [(R("eye"), K(nm, LC, 2 * LC)) for nm in ("m1", "m0")])
+            aff("wo", R(wo, LC, 2 * LC), P(c, 2, LC))
+            remote("q%d_%d" % (t, c), R(wn, LC, 2 * LC), R(wo, LC, 2 * LC))
+        elif SPLIT == 2 and t < VI - 1:
+            fp = P(c, 1, 2 * LC)
+            msum(fp, [(R("eye"), K(nm, 0, LC)) for nm in ("m1", "m0", "iv")])
+            aff("off", R("oo%d_%d" % (t, c)), fp, None, 2048.0)
+            remote("p%d_%d" % (t, c), R("of%d_%d" % (t + 1, c)), R("oo%d_%d" % (t, c)))
+            msum(P(c, 1, 3 * LC), [(R("eye"), K(nm, LC, 2 * LC)) for nm in ("m1", "m0")])
+            aff("wo", R(wo), P(c, 1, 2 * LC, 2 * LC))
+            remote("q%d_%d" % (t, c), R(wn), R(wo))
+        elif SPLIT or t == VI - 1:
             for h, tag, y in ((1, "q", "yw"), (0, "p", "ys")):
                 a0, a1 = h * LC, (h + 1) * LC
                 fp = P(c, 1, (2 + h) * LC)
@@ -707,8 +1030,8 @@ def rank_program(g, core, T, topo):
         PH[0] = "count"
         o = P(0, 3, 3 * LC, 1)
         for c in range(NCH):
-            ts(R("acb", 2 * c, 2 * c + 2), R("ac%d_%d" % (t, c), 0, 2), 1.0, A.mult)
-        msum(o, [(R(("all1", "all16")[q % 2]), R("acb", q, q + 1)) for q in range(2 * NCH)])
+            ts(R("acb", c, c + 1), R("ac%d_%d" % (t, c), 1, 2), 1.0 / 16 if ENG["ins"] == "a" else 1.0, A.mult)
+        msum(o, [(R("all1"), R("acb", q, q + 1)) for q in range(NCH)])
         cp(R("rci", 0, 1), o)
         ts(R("rci", 4, 5), R("rci", 0, 1), 1, A.bitwise_and)
         ts(R("thr", 0, 1), R("rci", 4, 5), -1.0, A.mult, -1.5, A.add)
@@ -716,6 +1039,8 @@ def rank_program(g, core, T, topo):
     for t in range(VI):
         for c in range(NCH):
             run(t, c)
+        if JE:
+            end(t)
         for c in range(NCH):
             table(t, c, "gt", "ng")
         for c in range(NCH):
@@ -734,7 +1059,7 @@ def rank_program(g, core, T, topo):
     def gap(i, j):
         if i in ops[j]["soft"]:
             return 0.0
-        return ops[i]["lat"] + (HOP if ops[j]["q"] != ops[i]["q"] else 0.04)
+        return ops[i]["lat"] + (HOP if ops[j]["q"] != ops[i]["q"] else SELF)
     succ = [[] for _ in range(n)]
     for i, o in enumerate(ops):
         for d in o["deps"]:
@@ -746,48 +1071,9 @@ def rank_program(g, core, T, topo):
         for j in succ[i]:
             m = max(m, tail[j] + gap(i, j))
         tail[i] = m + o["cost"] + (SLACK if o["kind"] == "r" else 0.0)
-    prio = [tail[i] + BIAS.get(ops[i]["ph"], 0.0) + BIAS.get(ops[i]["nm"], 0.0) for i in range(n)]
-    pred = [sorted(o["deps"]) for o in ops]
-
-    def place(prio, before, after, back):
-        left = [len(b) for b in before]
-        ready = [o["lat"] if back else 0.0 for o in ops]
-        start = [0.0] * n
-        busy = {q: [] for q in "vatgs"}
-        avail = [i for i in range(n) if left[i] == 0]
-        while avail:
-            i = max(avail, key=lambda k: (prio[k], -k))
-            avail.remove(i)
-            o = ops[i]
-            st = ready[i]
-            if o["q"] != "x":
-                row = busy[o["q"]]
-                lo, hi = 0, len(row)
-                while lo < hi:
-                    mid = (lo + hi) // 2
-                    if row[mid][1] <= st:
-                        lo = mid + 1
-                    else:
-                        hi = mid
-                while lo < len(row) and row[lo][0] < st + o["cost"]:
-                    st = max(st, row[lo][1])
-                    lo += 1
-                row.insert(lo, (st, st + o["cost"]))
-            start[i] = st
-            for j in after[i]:
-                ready[j] = max(ready[j], st + o["cost"] + (gap(j, i) if back else gap(i, j)))
-                left[j] -= 1
-                if left[j] == 0:
-                    avail.append(j)
-        return start, max(start[i] + ops[i]["cost"] + ops[i]["lat"] for i in range(n))
-
-    start, span = place(prio, pred, succ, False)
-    for _ in range(PASSES):
-        late, _x = place([start[i] + ops[i]["cost"] for i in range(n)], succ, pred, True)
-        again, span2 = place([late[i] + ops[i]["cost"] for i in range(n)], pred, succ, False)
-        if span2 >= span:
-            break
-        start, span = again, span2
+    if not PLACED:
+        PLACED.append(arrange(ops, tail, gap))
+    start, span = PLACED[0]
     order = sorted(range(n), key=lambda i: (start[i], i))
 
     cnt = {"qv": 0, "qa": 0, "qt": 0, "qg": 0}

import numpy as np
import math
import comms_topo
from concourse.mybir import AluOpType as A, ActivationFunctionType as F

NCH, W, L, VI = 2, 4096, 16, 4
LC = 256 // NCH
CA = LC * L
NJ = LC // 16
NP = 2
NPC = 2
NG = 2
NF = 2
NC = 2
LN2 = math.log(2.0)
AGE = 7
LA = 80.0 / AGE
NDMA = 20
ROUNDS = 12000
SEED = 2
PM = 0.05
TEMP = 1.0
D3 = 0
JE = 1
QL = 0
WQ = 6
MP = 0
WK = 0
VFIX = 0.015
AFIX = 0.03
SELF = 0.1
TFIX = 0.008
MMC = 128
FIP = 0
WB = 6
ULA = 0
YV = 1
SPLIT = 2
RL2 = 4.0
RHOLD = 1.0
RLAT = 3.0
HOP = 0.19
ERS = (0, 512, 1536, 2560, 4096)
GP = ()
AQ = "s"
LEAD = 8.5
SLACK = 3.0
ENG = {'back': 'a', 'zx': 'a', 'X': 'v', 'T': 'v', 'ins': 'a', 'off': 'a', 'e15': 'a', 'slot': 'v', 'yi': 'a', 'ui': 'a', 'vl': 'a', 'ne': 'a', 'xl': 'a', 'sh': 'v', 'c16': 'a', 'cf': 'a', 'wb': 'a', 'wo': 'a', 'sx': 'a', 'ci': 'a', 'ret': 'v', 'nret': 'v', 'w8': 'v', 'ov': 'v', 'y13': 'a', 'kap': 'a', 'D': 'v', 'c0': 'a', 'ng': 'a', 'eh': 'a', 'sg': 'a'}
NTV = 4

SCRATCH = {}
SEMAPHORES = ["qv", "qa", "qt", "qg"] + ["d%d" % i for i in range(NDMA)]
for _t in range(VI - 1):
    for _c in range(NCH):
        SEMAPHORES += ["ap%d_%d" % (_t, _c), "as%d_%d" % (_t, _c), "lp%d_%d" % (_t, _c), "ls%d_%d" % (_t, _c)]
        if SPLIT:
            SEMAPHORES += ["aq%d_%d" % (_t, _c), "lq%d_%d" % (_t, _c)]
LOG = {}
_SHORT = {"bfloat16": "bf", "float16": "hf", "float32": "ff", "int32": "nn", "uint16": "uu"}


def _buf(name, cols, dtype, where="sbuf"):
    if where == "psum":
        SCRATCH[name] = (where, [128, cols], dtype)
        LOG[name] = (where, cols, dtype, name, 0)
        return
    t = "pk" + _SHORT[dtype]
    o = SCRATCH[t][1][1] if t in SCRATCH else 0
    SCRATCH[t] = ("sbuf", [128, o + -(-cols // 64) * 64], dtype)
    LOG[name] = (where, cols, dtype, t, o)


for _n in ("er", "gt", "nt", "tq", "tcl", "tsg"):
    _buf(_n, W, "bfloat16")
for _n in ("ip", "kp"):
    _buf(_n, 8, "int32")
_buf("kc", 256, "int32")
for _n in ("i48", "eye", "blk", "tri", "shd", "sh1", "sh2", "sh4", "sh8", "neg", "e16", "n16", "ial", "i125", "b125",
           "i2048", "mt", "mth", "nblk", "hblk", "blk32", "blkk", "r1", "r2", "tmp", "mr", "m16"):
    _buf(_n, 128, "bfloat16")
_buf("msk", 256, "bfloat16")
_buf("wk", 2048, "bfloat16")
SL = 16
_buf("al", SL * LC // NP, "bfloat16")
_buf("a16", 128, "bfloat16")
_buf("cb", 128, "float16")
for _n in ("all1", "all16", "acb"):
    _buf(_n, 128, "bfloat16")
for _n in ("kcol", "kap", "thr", "m1c", "m2c"):
    _buf(_n, 8, "float32")
_buf("rci", 8, "int32")
_buf("xbase", 2 * NJ, "float16")
_buf("xbi", NJ, "int32")
for _n in ("stl", "bal"):
    _buf(_n, 16, "uint16")
for _n in ("lb", "lc", "kq"):
    _buf(_n, 16, "int32")
for _n in ("an", "at"):
    _buf(_n, 512, "float16")
for _n in ("in00", "in01", "in10", "in11", "out00", "out01", "out10", "out11"):
    _buf(_n, 128, "bfloat16")
_buf("bari", 256, "int32")
for _n in ("barb", "sti", "sth", "stc", "stn"):
    _buf(_n, 256, "bfloat16")
for _n in ("jh", "jum", "jeo", "jeh", "jnw", "jcl", "jsg", "jng", "jo0", "jo1", "jo2", "jo3", "js0", "js1", "js2", "js3"):
    _buf(_n, 256, "bfloat16")
for _n in ("jab", "jln"):
    _buf(_n, 256, "float32")
for _n in ("jyi", "jy7"):
    _buf(_n, 256, "int32")
for _n in ("jui", "juj", "juk", "jvb"):
    _buf(_n, 16, "int32")
_buf("jvl", 16, "uint16")
_buf("actk", 256, "int32")
_buf("whyk", 256, "int32")
_buf("ysk", 256, "float32")
_buf("ywk", 256, "float32")
for _c in range(NCH):
    for _t in range(VI):
        _buf("w%d_%d" % (_t, _c), 2 * LC, "float16")
        _buf("wo%d_%d" % (_t, _c), 2 * LC, "float16")
        _buf("s%d_%d" % (_t, _c), LC, "bfloat16")
        _buf("so%d_%d" % (_t, _c), LC, "bfloat16")
        _buf("ac%d_%d" % (_t, _c), 8, "float32")
        _buf("of%d_%d" % (_t, _c), LC, "uint16")
        _buf("oo%d_%d" % (_t, _c), LC, "uint16")
    for _n in ("gb%d" % _c, "zb%d" % _c):
        if D3 and _n[0] == "g":
            SCRATCH[_n] = ("sbuf", [128, LC, 17], "bfloat16")
            LOG[_n] = ("sbuf", 17 * LC, "bfloat16", _n, 0)
        else:
            _buf(_n, CA + 16, "bfloat16")
    for _n in ("fl", "cg", "hb"):
        _buf("%s%d" % (_n, _c), CA, "bfloat16")
    for _n in ("e15", "h", "q", "um", "ov", "st", "XL", "X", "zx", "nx", "w8", "f1", "T", "M", "ins", "ret", "nret", "ne", "keep", "fm",
               "eo", "eh", "nw", "cl", "sg", "ng"):
        _buf("%s_%d" % (_n, _c), LC, "bfloat16")
    for _n in ("xs", "ds", "cf", "mc", "iqe", "fi", "fw", "mx", "iv"):
        _buf("%s_%d" % (_n, _c), LC, "float16")
    for _n in ("a1", "a2", "m0", "m1", "m2", "m3", "wb", "xm", "wb0", "wb1", "wb2"):
        _buf("%s_%d" % (_n, _c), 2 * LC, "float16")
    for _n in ("yi", "y7", "pr", "sh", "sm", "ci", "cn", "c0", "k0", "k1", "k2", "k3"):
        _buf("%s_%d" % (_n, _c), LC, "int32")
    for _n in ("ab", "ln", "sx"):
        _buf("%s_%d" % (_n, _c), LC, "float32")
    for _n in ("off", "c16"):
        _buf("%s_%d" % (_n, _c), LC, "uint16")
    _buf("xl_%d" % _c, 2 * NJ, "uint16")
    _buf("vl_%d" % _c, NJ, "uint16")
    for _n in ("ui", "uj", "uk", "vb"):
        _buf("%s_%d" % (_n, _c), NJ, "int32")
    for _n in ("ub", "uf", "vc"):
        _buf("%s_%d" % (_n, _c), NJ, "bfloat16")
for _i in range(8):
    _buf("p%d" % _i, 512, "float32", "psum")


def overlap(a, b):
    if a[0] != b[0] or a[1] >= b[2] or b[1] >= a[2]:
        return False
    if a[3] == b[3] and a[3] > 1 and (a[1] - b[1]) % a[3]:
        return False
    if a[4] is not None and b[4] is not None and a[4] != b[4]:
        return False
    return True


PLACED = []


def arrange(ops, tail, gap):
    n = len(ops)
    qs, cost, lat = [o["q"] for o in ops], [o["cost"] for o in ops], [o["lat"] for o in ops]
    before, above, same, seen, last = [], [0] * n, [], {}, None
    for j, o in enumerate(ops):
        near, far = [], 0
        for i in sorted(o["deps"], reverse=True):
            if not (far >> i & 1 and lat[i] == 0):
                near.append((i, gap(i, j)))
                far |= above[i]
        above[j] = far | sum(1 << i for i in o["deps"])
        before.append(near)
        if o["ph"] == "run0" and last != "run0":
            seen = {}
        last = o["ph"]
        seen[last, o["nm"]] = seen.get((last, o["nm"]), 0) + 1
        same.append((last, o["nm"], seen[last, o["nm"]]))

    def place(shift, was=None):
        prio = [0.0] * n
        for j in range(n):
            p = tail[j] + shift.get(same[j], 0.0)
            for i, _ in before[j]:
                if prio[i] <= p:
                    p = prio[i] - 1e-6
            prio[j] = p
        end = [0.0] * n
        busy = {q: ([], []) for q in "vatgs"}
        for _, j in sorted(zip(prio, range(n)), reverse=True):
            st, c = 0.0, cost[j]
            for i, d in before[j]:
                if end[i] + d > st:
                    st = end[i] + d
            if qs[j] == "x":
                if was and same[j][0][:3] == "fin" and st > was[j] + 1.5:
                    return 1e9, end, prio
            else:
                a, b = busy[qs[j]]
                lo = m = len(a)
                while lo and b[lo - 1] > st:
                    lo -= 1
                while lo < m and a[lo] < st + c:
                    st = b[lo] if b[lo] > st else st
                    lo += 1
                a.insert(lo, st)
                b.insert(lo, st + c)
            end[j] = st + c
        return max(end[j] + lat[j] for j in range(n)), end, prio

    def held(end):
        ahead, cur, out = {}, {}, []
        for j in sorted(range(n), key=lambda k: end[k]):
            ahead[j] = cur.get(qs[j])
            cur[qs[j]] = j
        j = max(range(n), key=lambda k: end[k] + lat[k])
        while j is not None:
            ready, i = max([(end[i] + d, i) for i, d in before[j]] + [(0.0, None)], key=lambda u: u[0])
            if end[j] - cost[j] - ready > 1e-6 and ahead[j] is not None:
                i = ahead[j]
                out.append((j, i))
            j = i
        return out

    part = {}
    for e in sorted(set(same)):
        part.setdefault(e[0], []).append(e)
    seed = [SEED]

    def rnd():
        seed[0] = (seed[0] * 1103515245 + 12345) % 2147483648
        return seed[0] / 2147483648.0

    shift = {}
    span, end, prio = place(shift)
    best, pairs = (span, end), held(end)
    for r in range(ROUNDS):
        new = dict(shift)
        for _ in range(1 + (rnd() < 0.33)):
            j, i = pairs[int(rnd() * len(pairs))]
            d, k = prio[i] - prio[j], rnd()
            if k < PM:
                u, v = same[j if rnd() < 0.5 else i][0], 2.0 * (rnd() - 0.5)
                for e in part[u]:
                    new[e] = new.get(e, 0.0) + v
            elif d < 0 or k < PM + 0.12:
                u = same[j if rnd() < 0.5 else i]
                new[u] = new.get(u, 0.0) + 3.0 * (rnd() - 0.5)
            elif k < 0.6:
                row, top = [j], prio[i] + 0.5 * rnd()
                for u in row:
                    new[same[u]] = top - tail[u] + 0.01 * len(row)
                    row += [e for e, _ in before[u] if prio[e] < top and e not in row and len(row) < 12]
            else:
                new[same[i]] = prio[j] - tail[i] - 0.5 * rnd()
        span2, end2, prio2 = place(new, end)
        if span2 <= span + TEMP * (1.0 - r / ROUNDS) * rnd():
            shift, span, end, prio = new, span2, end2, prio2
            pairs = held(end)
            if span < best[0]:
                best = (span, end)
    return [best[1][j] - cost[j] for j in range(n)], best[0]


def rank_program(g, core, T, topo):
    rank = T.rank_of(core)
    if rank is None:
        return
    nxt = T.cores[(rank + 1) % len(T.cores)]
    ops = []
    acc = {}
    Q = {"v": g.vector, "a": g.scalar, "t": g.tensor, "g": g, "s": g.sync}
    QS = {"v": "qv", "a": "qa", "t": "qt", "g": "qg"}
    dn = [0]
    moved = [0.0]
    PH = ["set"]
    PS = set("p%d" % i for i in range(8))

    def R(name, a=None, b=None, st=1, p=None):
        n = LOG[name][1] if name in LOG else T[name].shape[1]
        return (name, 0 if a is None else a, n if b is None else b, st, p)

    def rev(r):
        return (r[0], r[1], r[2], -1, None)

    def S3(name, l0, l1, k0, k1):
        return (name, 17 * l0, 17 * l1, 0, None, (k0, k1))

    def ap(r):
        if r[3] == 0:
            k0, k1 = r[5]
            return T[r[0]][:, r[1] // 17:r[2] // 17, k0] if k1 == k0 + 1 else T[r[0]][:, r[1] // 17:r[2] // 17, k0:k1]
        t, o = (LOG[r[0]][3], LOG[r[0]][4]) if r[0] in LOG else (r[0], 0)
        if r[4] is not None:
            return T[t][r[4][0]:r[4][1]:r[4][2], o + r[1]:o + r[2]]
        if r[3] > 1:
            return T[t][:, o + r[1]:o + r[2]:r[3]]
        if r[3] < 0:
            return T[t][:, o + r[2] - 1:o + r[1] - 1:-1]
        return T[t][:, o + r[1]:o + r[2]]

    def ind(win, off):
        return ("IND", win, off)

    def x(r):
        if isinstance(r, tuple):
            if r[0] == "IND":
                return ap(r[1]).indirect(ap(r[2]))
            return ap(r)
        return r

    def n_of(r):
        if r[3] == 0:
            return (r[2] - r[1]) // 17 * (r[5][1] - r[5][0])
        return -(-(r[2] - r[1]) // abs(r[3]))

    def add(q, fns, reads, writes, cost, kind="c", lat=0.0, sem=None, inc=0, extra=(), soft=()):
        i = len(ops)
        rd = []
        for r in reads:
            if isinstance(r, tuple):
                rd += [r[1], r[2]] if r[0] == "IND" else [r]
        wr = []
        for r in writes:
            if r[0] == "IND":
                wr.append(r[1])
                rd.append(r[2])
            else:
                wr.append(r)
        deps = set(extra)
        for lst, isw in ((rd, False), (wr, True)):
            for r in lst:
                ps = r[0] in PS
                for (j, r2, w2) in acc.get(r[0], ()):
                    if ps and ops[j]["q"] != q:
                        deps.add(j)
                    elif (isw or w2) and overlap(r, r2):
                        deps.add(j)
        for lst, isw in ((rd, False), (wr, True)):
            for r in lst:
                cur = acc.setdefault(r[0], [])
                if isw and r[3] == 1 and r[4] is None and r[0] not in PS:
                    cur[:] = [e for e in cur if not (e[1][1] >= r[1] and e[1][2] <= r[2])]
                cur.append((i, r, isw))
        deps |= set(soft)
        nm = rd[-1][0] if q == "t" or not wr or wr[0][0] in PS else wr[0][0]
        ops.append({"ph": PH[0], "nm": q + "".join(ch for ch in nm if ch.isalpha()) + PH[0][-1], "q": q,
                    "ind": any(isinstance(r, tuple) and r[0] == "IND" for r in list(reads) + list(writes)), "fns": fns, "deps": deps, "cost": cost, "kind": kind,
                    "lat": lat, "sem": sem, "inc": inc, "soft": set(soft)})
        return i

    def chain(row):
        for a, b in zip(row, row[1:]):
            if a not in ops[b]["deps"]:
                ops[b]["deps"].add(a)
                ops[b]["soft"].add(a)

    def two(*rs):
        return all(isinstance(r, tuple) and r[0] in LOG and LOG[r[0]][2] in ("bfloat16", "float16", "uint16") and r[0] not in PS for r in rs)

    CY = 0.00083

    def vc(n, rate):
        return VFIX + max(64, n * rate) * CY

    def tt(out, a, b, op):
        rate = 1.6 if a[0] == "IND" else (1.0 if a[0] in PS or b[0] in PS else 2.0)
        return add("v", [lambda: g.vector.tensor_tensor(x(out), x(a), x(b), op)], [a, b], [out], vc(n_of(out), rate))

    def ts(out, a, s1, op0, s2=None, op1=None):
        rate = 0.5 if two(out, a) else 1.0
        if op1 is None:
            f = lambda: g.vector.tensor_scalar(x(out), x(a), x(s1), None, op0)
        else:
            f = lambda: g.vector.tensor_scalar(x(out), x(a), x(s1), x(s2), op0, op1)
        return add("v", [f], [a, s1, s2], [out], vc(n_of(out), rate))

    def cp(out, a):
        rate = 4.0 if out[0] == "IND" else 1.8 if a[0] == "IND" else (0.5 if two(out, a) else 1.0)
        return add("v", [lambda: g.vector.tensor_copy(x(out), x(a))], [a], [out], vc(n_of(out if a[0] == "IND" else a), rate))

    def turn(out, a):
        return add("v", [lambda: g.vector.transpose(x(out), x(a))], [a], [out], vc(n_of(a), 1.0))

    def fill(out, v):
        add("v", [lambda: g.vector.memset(x(out), v)], [], [out], vc(n_of(out), 0.5 if two(out) else 1.0))

    def scan(out, d0, d1, op1):
        return add("v", [lambda: g.vector.tensor_tensor_scan(x(out), x(d0), x(d1), 0.0, A.mult, op1)], [d0, d1], [out],
                   vc(n_of(out), 0.5 if two(out, d0, d1) else 1.0))

    def act(out, a, func, bias=None, scale=None, accum=None):
        kw = {}
        if func == F.Copy and (bias is not None or scale is not None or accum is not None):
            func = F.Identity
        if bias is not None:
            kw["bias"] = bias
        if scale is not None:
            kw["scale"] = scale
        if accum is not None:
            kw["accum_out"] = accum
        rate = 1.6 if a[0] == "IND" else 1.0
        first = 1.3 if func == F.Ln and PH[0] == "set" else 0.0
        return add("a", [lambda: g.scalar.activation(x(out), x(a), func, **{k: x(v) for k, v in kw.items()})], [a, bias, scale],
                   [out] + ([accum] if accum is not None else []), AFIX + first + max(64, n_of(out) * rate) * CY)

    def aff(nm, out, a, scale=None, bias=None):
        if ENG[nm] == "a":
            return act(out, a, F.Copy, bias, scale)
        if scale is None:
            return cp(out, a) if bias is None else ts(out, a, bias, A.add)
        return ts(out, a, scale, A.mult) if bias is None else ts(out, a, scale, A.mult, bias, A.add)

    def relu(nm, out, a, bias=None):
        if ENG[nm] == "a":
            return act(out, a, F.Relu, bias)
        return ts(out, a, 0.0, A.max) if bias is None else ts(out, a, bias, A.add, 0.0, A.max)

    group = {}

    def mm(items):
        rows, cols = [[]], 0
        for it in items:
            n = max(64, n_of(it[2])) * (4 if LOG[it[2][0]][2] == "float32" else 1)
            if cols + n > MMC and rows[-1] and PH[0] != "gt":
                rows.append([])
                cols = 0
            rows[-1].append(it)
            cols += n
        for row in rows:
            fns, rd, wr, cost = [], [], [], TFIX * len(row)
            for (o, l, r, s, e) in row:
                fns.append(lambda o=o, l=l, r=r, s=s, e=e: g.tensor.matmul(x(o), x(l), x(r), s, e))
                rd += [l, r]
                wr.append(o)
                cost += max(64, n_of(r)) * CY * (4 if LOG[r[0]][2] == "float32" else 1)
            bank = row[0][0][0]
            i = add("t", fns, list(dict.fromkeys(rd)), list(dict.fromkeys(wr)), cost, soft=[] if row[0][3] else group[bank])
            if bank in group:
                chain([group[bank][-1], i])
            group[bank] = [i] if row[0][3] else group[bank] + [i]
        return i

    def msum(o, terms):
        return mm([(t[2] if len(t) > 2 else o, t[0], t[1], q == 0, q == len(terms) - 1) for q, t in enumerate(terms)])

    def dma(q, out, a):
        s = "d%d" % dn[0]
        dn[0] += 1
        moved[0] += n_of(out if out[0] in LOG else a) * 0.0008 - (0.3 if q == "s" else 0.0)
        return add(q, [lambda: Q[q].dma_start(x(out), x(a))], [a], [out], 0.6, "d", 2.0 + moved[0], s, 16)

    def remote(tag, out, a):
        m, ne = 0, 8
        for e in topo.engines(core, nxt)[:ne]:
            m |= 1 << e
        rid, pid = topo.addr(nxt)[0], topo.addr(nxt)[1]
        ra, la = T.sem["a" + tag], T.sem["l" + tag]
        i = add("g", [lambda: g.remote_dma(ap(out), ap(a), ra, la, pid, rid, m)], [a], [], RHOLD, "r", RLAT if tag[0] == "p" else RL2, "l" + tag, ne)
        return add("x", [], [], [out], 0.0, "x", 0.0, "a" + tag, ne, (i,))

    def P(c, i, a=0, n=LC, st=1):
        return R("p%d" % (4 * c + i), a, a + n, st)

    BC = {}
    for q, (nm, v) in enumerate((("need", 736.0), ("least", 13.0 / 16))):
        BC[nm] = R("m1c", q, q + 1)
        fill(BC[nm], v)
    act(R("m1c", 2, 3), BC["least"], F.Ln, None, 2.0 ** (8 * AGE))
    ts(R("m1c", 3, 4), R("m1c", 2, 3), -LA / LN2, A.mult, -0.21, A.add)
    for j, (c0, c1) in enumerate(zip(ERS, ERS[1:])):
        dma("s", R("er", c0, c1), R("eff", c0, c1))
        if c1 == W:
            dma(AQ, R("actk"), R("act"))
            dma(AQ, R("sti"), R("st0"))
    chain([i for i, o in enumerate(ops) if o["q"] == "a"])
    for j in range(2):
        dma("s", R("tq", 2048 * j, 2048 * j + 2048), R("req", 2048 * j, 2048 * j + 2048))
    dma("s", R("whyk"), R("why"))
    fill(R("bari"), 1)
    dma("s", R("bari", None, None, 1, (0, 128, 16)), R("bar"))
    chain([i for i, o in enumerate(ops) if o["q"] == "s"])

    def iota(out, pattern, base, cm):
        add("g", [lambda: g.iota(x(out), pattern, base, cm)], [], [out], 0.13 + 2 * n_of(out) * CY)
    def keep(out, a, value, op, other):
        add("g", [lambda: g.affine_select(x(out), x(a), value[0], op, other, value[1], value[2])], [a], [out], 0.17 + 2 * n_of(out) * CY)

    def c_p(d):
        return ([[1, 128]], -d, -1)

    def row(k):
        return ([[-16, 8], [0, 16]], -k, 1)
    fill(R("all1"), 1.0)
    keep(R("eye"), R("all1"), c_p(0), A.is_equal, 0.0)
    iota(R("ip"), [[0, 8]], 0, 1)
    iota(R("kc"), [[0, 16], [1, 16]], 0, 0)
    keep(R("tmp"), R("all1"), row(0), A.is_ge, 0.0)
    keep(R("blk"), R("tmp"), ([[16, 8], [0, 16]], 15, -1), A.is_ge, 0.0)
    iota(R("xbi"), [[16 * SL, NJ]], 0, 0)
    iota(R("lb"), [[64, 2], [128, 2], [4, 4]], 0, 0)
    iota(R("lc"), [[4, 2], [8, 2], [64, 4]], 0, 0)
    for g2 in range(2):
        for h in range(2):
            keep(R("in%d%d" % (g2, h)), R("all1"), ([[-32, 4], [200, 2], [-2, 16]], -h - 200 * g2, 1), A.is_equal, 0.0)
            keep(R("out%d%d" % (g2, h)), R("all1"), ([[-32, 4], [-1, 16], [200, 2]], -16 * g2 - 200 * h, 1), A.is_equal, 0.0)
    for nm, f in (("e16", 1.0 / 16), ("n16", -1.0 / 16)):
        ts(R(nm), R("eye"), f, A.mult)
    for nm, f in (("neg", -1.0), ("ial", 2.0 ** -AGE), ("i125", 12.5), ("i2048", 2048.0),
                  ("m16", -16.0), ("i48", 48.0)):
        act(R(nm), R("eye"), F.Copy, None, f)
    ts(R("kp"), R("ip"), 15, A.bitwise_and)
    ts(R("kcol", 0, 1), R("kp", 0, 1), 1.0, A.mult)
    keep(R("tri"), R("blk"), c_p(0), A.is_ge, 0.0)
    for nm, de in (("sh1", -1), ("shd", 1), ("sh2", -2), ("sh4", -4), ("sh8", -8)):
        keep(R(nm), R("blk"), c_p(de), A.is_equal, 0.0)
        keep(R(nm), R(nm), c_p(0), A.not_equal, -1.0)
    keep(R("mt"), R("sh1"), row(0), A.not_equal, 0.5)
    keep(R("mt"), R("mt"), ([[-16, 8], [128, 16]], 0, 1), A.not_equal, -0.5)
    fill(R("al"), 2.0 ** -AGE)
    fill(R("al", 0, SL * LC // NP, SL), 0.0)
    fill(R("a16"), 2.0 ** -AGE)
    fill(R("a16", 0, 128, 16), 0.0)
    scan(rev(R("mth")), R("a16"), rev(R("i48")), A.add)
    keep(R("mth"), R("mth"), ([[-1, 128]], 0, 1), A.is_ge, 48.0)
    keep(R("mth"), R("mth"), row(0), A.is_ge, 0.0)
    for nm, f in (("nblk", -1.0), ("hblk", 0.5), ("b125", -12.5), ("blk32", -33.0), ("blkk", R("kcol", 0, 1))):
        ts(R(nm), R("blk"), f, A.mult)
    ts(R("msk"), R("kc"), R("kcol", 0, 1), A.is_equal)
    keep(R("r1"), R("all1"), ([[0, 8], [1, 16]], -1, 0), A.is_ge, 0.0)
    ts(R("r2"), R("r1"), 2.0, A.mult)
    ts(R("cb"), R("kc", 0, 128), -1.0 / 32, A.mult, 25.5, A.add)
    keep(R("cb"), R("cb"), row(1), A.is_equal, 0.0)
    keep(R("cb"), R("cb"), row(0), A.not_equal, -1.0)
    for r in range(16 * WK):
        keep(R("wk", 128 * r, 128 * r + 128), R("blk"), ([[0, 8], [1, 16]], -r, 0), A.is_equal, 0.0)
    keep(R("mr"), R("nblk"), c_p(0), A.is_ge, 0.0)
    keep(R("mr"), R("mr"), c_p(0), A.not_equal, 63.0)
    ts(R("kap", 0, 1), R("kcol", 0, 1), 241.0, A.mult, 101.0, A.add)
    for t in range(VI):
        ts(R("kap", 4 + t, 5 + t), R("kap", 0, 1), 2048.0, A.mult, float(97 * t), A.add)
    ts(R("m2c", 0, 1), R("kcol", 0, 1), 15.0, A.is_equal, -0.5, A.add)
    if ENG["T"] == "v":
        ts(R("m2c", 0, 1), R("m2c", 0, 1), 2.0, A.mult)
    ts(R("m2c", 1, 2), R("kcol", 0, 1), 1.0, A.add)
    ts(R("m2c", 2, 3), R("kcol", 0, 1), -63.0, A.add)
    fill(R("thr", 0, 1), -1.5)
    ts(R("kcol", 2, 3), R("kcol", 0, 1), float(SL), A.mult, -1024.0, A.add)
    ts(R("xbase", 0, NJ), R("xbi"), R("kcol", 2, 3), A.add)
    fill(R("xbase", NJ, 2 * NJ), 1024.0)
    ts(R("kq", 0, 1), R("kp", 0, 1), 3, A.bitwise_and)
    ts(R("kq", 4, 5), R("kp", 0, 1), 2, A.arith_shift_right)
    cp(R("kcol", 4, 5), R("kq", 0, 1))
    cp(R("kcol", 5, 6), R("kq", 4, 5))
    ts(R("kcol", 6, 7), R("kcol", 4, 5), 16.0, A.mult, R("kcol", 5, 6), A.add)
    ts(R("kcol", 7, 8), R("kcol", 5, 6), 16.0, A.mult, R("kcol", 4, 5), A.add)
    ts(R("stl"), R("lb"), R("kcol", 6, 7), A.add)
    ts(R("bal"), R("lc"), R("kcol", 7, 8), A.add)
    for c in range(0 if JE else NCH):
        ts(R(("vc_%d" if ULA else "vb_%d") % c), R("lb", c * NJ, (c + 1) * NJ), R("kcol", 6, 7), A.add, 16.0, A.mult)
    act(R("barb"), ind(R("bari"), R("bal")), F.Copy)
    ts(R("an", 0, 256), R("actk"), -2048.0, A.add)
    ts(R("whyk"), R("whyk"), 8191, A.bitwise_and)
    ts(R("an", 256, 512), R("whyk"), 4096.0, A.min, -2048.0, A.add)

    def plans(f):
        PH[0] = "set"
        for c in range(NCH):
            a0 = 256 * f + LC * c
            for c4 in range(4):
                turn(R("at", a0 + c4, a0 + LC, 4), R("an", 256 * f + 4 * c + c4, 256 * f + 256, 8))
            for h in range(2):
                msum(P(0, c + 2 * f, 64 * h, 64), [(R("in%d%d" % (g2, h)), R("at", a0 + 64 * g2, a0 + 64 * g2 + 64)) for g2 in range(2)])
            act(R("w0_%d" % c, f * LC, (f + 1) * LC), P(0, c + 2 * f), F.Copy)
    ts(R("sth"), R("sti"), 8.0, A.is_lt, 25.0, A.mult)
    ts(R("stn"), R("sti"), -1.0, A.mult, -5.0, A.add)
    tt(R("stc"), R("stn"), R("sth"), A.add)
    if JE:
        act(R("js0"), ind(R("stc"), R("stl")), F.Copy)
        ts(R("jvb"), R("lb"), R("kcol", 6, 7), A.add, 16.0, A.mult)
    for c in range(0 if JE else NCH):
        act(R("s0_%d" % c), ind(R("stc"), R("stl", c * NJ, (c + 1) * NJ)), F.Copy)

    PH[0] = "gt"
    for j in range(8):
        c0, c1 = 512 * j, 512 * j + 512
        b = R("p%d" % j)
        if j in GP:
            act(b, R("er", c0, c1), F.Copy, None, 1.0 / 16)
            ts(R("tcl", c0, c1), b, 4.0 / 16, A.max, 11.0 / 16, A.min)
            tt(R("tsg", c0, c1), R("tcl", c0, c1), b, A.subtract)
            act(b, R("tsg", c0, c1), F.Sign)
            tt(R("gt", c0, c1), R("tsg", c0, c1), b, A.add)
        else:
            ts(R("tcl", c0, c1), R("er", c0, c1), 4.0, A.max, 11.0, A.min)
            msum(b, [(R("n16"), R("er", c0, c1)), (R("e16"), R("tcl", c0, c1))])
            act(R("tsg", c0, c1), b, F.Sign)
            tt(R("gt", c0, c1), R("tsg", c0, c1), b, A.add)
        if j == 7:
            plans(0)
            PH[0] = "gt"
    plans(1)
    PH[0] = "nt"
    for j in range(4):
        c0, c1 = 1024 * j, 1024 * j + 1024
        if j < NTV:
            ts(R("nt", c0, c1), R("tq", c0, c1), 12.0, A.is_lt, 32.0, A.mult)
        else:
            act(R("nt", c0, c1), R("tq", c0, c1), F.Relu, BC["need"], -64.0)

    def pick(o, xm, n):
        return [(R(xm, q * LC, (q + 1) * LC), R("blk", 0, 128, 16), R(o[0], o[1] + q * NJ, o[1] + (q + 1) * NJ)) for q in range(n)]

    def cut(a, b, n):
        return [(a + (b - a) * i // n, a + (b - a) * (i + 1) // n) for i in range(n)]

    def run(t, c):
        def K(n, *a):
            return R("%s_%d" % (n, c), *a)
        PH[0] = "run%d" % c
        gb, zb, fl = "gb%d" % c, "zb%d" % c, "fl%d" % c
        w, s = "w%d_%d" % (t, c), "s%d_%d" % (t, c)
        of = "of%d_%d" % (t, c)
        if SPLIT < 2 or t == 0:
            aff("off", R(of), R(w, 0, LC), None, 2048.0)
        elif QL or MP:
            aff("back", R(w, 0, LC), R(of), None, -2048.0)
        ra, rv = [], []
        for p in range(NP):
            l0, l1 = p * LC // NP, (p + 1) * LC // NP
            e0, e1 = 16 * l0, 16 * l1
            if D3:
                aff("slot", S3(gb, l0, l1, 0, 1), R(s, l0, l1), 1.0 / 16)
                for (a0, a1) in cut(l0, l1, NG):
                    ra.append(act(S3(gb, a0, a1, 1, 17), ind(R("gt"), R(of, a0, a1)), F.Copy))
                rv.append(scan(R(zb, e0, e1), R("al"), S3(gb, l0, l1, 0, 16), A.add))
                for (a0, a1) in cut(l0, l1, NF):
                    rv.append(tt(R(fl, 16 * a0, 16 * a1), ind(R("nt"), R(of, a0, a1)), R(zb, 16 * a0, 16 * a1), A.is_lt))
                continue
            for (a0, a1) in cut(l0, l1, NG):
                ra.append(act(R(gb, 16 * a0 + 1, 16 * a1 + 1), ind(R("gt"), R(of, a0, a1)), F.Copy))
            aff("e15", K("e15", l0, l1), R(gb, e0 + 16, e1 + 1, 16))
            aff("slot", R(gb, e0, e1, 16), R("js%d" % t, c * LC + l0, c * LC + l1) if JE else R(s, l0, l1), 1.0 / 16)
            rv.append(scan(R(zb, e0, e1), R("al"), R(gb, e0, e1), A.add))
            for (a0, a1) in cut(l0, l1, NF):
                rv.append(tt(R(fl, 16 * a0, 16 * a1), ind(R("nt"), R(of, a0, a1)), R(zb, 16 * a0, 16 * a1), A.is_lt))
        chain(ra)
        chain(rv)
        mm([(P(c, 1, k, 128 - k, 16), R(fl, k, CA, 16), R("blk", 0, 128, 16), True, True) for k in range(16)])
        if ENG["ov"] == "a":
            act(K("ov"), P(c, 1), F.Sign, R("thr", 0, 1))
        else:
            ts(K("ov"), P(c, 1), R("thr", 0, 1), A.add, 0.0, A.is_gt)
        if JE:
            return
        PH[0] = "end%d" % c
        o = P(c, 2)
        msum(o, [(R("eye"), S3(gb, 0, LC, 16, 17) if D3 else K("e15")), (R("ial"), R(zb, 15, CA, 16))])
        act(K("ab"), o, F.Abs)
        act(K("h"), o, F.Sign)
        act(K("ln"), K("ab"), F.Ln, None, 2.0 ** (8 * AGE))
        aff("yi", K("yi"), K("ln"), LA / LN2, R("m1c", 3, 4))
        ts(K("y7"), K("yi"), 7, A.bitwise_and)
        sv = R("so%d_%d" % (t, c))
        aff("y13", o, K("y7"), None, 13.0)
        tt(sv, K("h"), o, A.mult)
        if t < VI - 1:
            remote("s%d_%d" % (t, c), R("s%d_%d" % (t + 1, c)), sv)
        o = P(c, 2, 2 * LC)
        msum(o, [(sv, R("blk")), (K("h"), R("b125"))])
        tt(K("um"), o, R("msk", 0, LC), A.mult)
        o = P(c, 2, 3 * LC, NJ)
        msum(o, pick(o, "um_%d" % c, 1))
        if ULA:
            act(K("ub"), o, F.Copy)
            act(K("uf"), o, F.Copy, 192.0 + 112.5 / 16, -1.0 / 16)
            msum(o, [(R("eye"), K("vc")), (R("neg"), K("ub")), (R("m16"), K("uf"))])
            aff("vl", K("vl"), o, None, 3192.0)
        else:
            aff("ui", K("ui"), o, -1.0, 120.0)
            ts(K("uj"), K("ui"), 15, A.bitwise_and)
            tt(K("uk"), K("uj"), K("vb"), A.add)
            aff("vl", K("vl"), K("uk"))
        act(K("eo"), ind(R("er"), K("vl")), F.Copy)
        o = P(c, 2)
        msum(o, [(R("neg"), sv), (R("i125"), K("h")), (R("eye"), K("eo"))])
        aff("eh", K("eh"), o, 0.5, 195.5)
        aff("ne", K("nw"), K("eh"), None, -192.0)
        if t < VI - 1:
            ts(K("cl"), K("eh"), 196.0, A.max, 203.0, A.min)
            aff("sg", K("sg"), K("eh"), 0.125, 167.0625)
            o = P(c, 2, LC)
            msum(o, [(R("n16"), K("eh")), (R("e16"), K("cl")), (R("neg"), K("sg"))])
            aff("ng", K("ng"), o, None, 192.0)
        else:
            cp(ind(R("er"), K("vl")), K("nw"))

    def end(t):
        PH[0] = "end1"
        lo, hi = P(1, 2, 0, 256), P(1, 2, 256, 256)
        for c in range(NCH):
            msum(P(1, 2, c * LC), [(R("eye"), R("e15_%d" % c)), (R("ial"), R("zb%d" % c, 15, CA, 16))])
        act(R("jab"), lo, F.Abs)
        act(R("jh"), lo, F.Sign)
        act(R("jln"), R("jab"), F.Ln, None, 2.0 ** (8 * AGE))
        aff("yi", R("jyi"), R("jln"), LA / LN2, R("m1c", 3, 4))
        ts(R("jy7"), R("jyi"), 7, A.bitwise_and)
        sv = "jo%d" % t
        aff("y13", lo, R("jy7"), None, 13.0)
        tt(R(sv), R("jh"), lo, A.mult)
        if t < VI - 1:
            remote("s%d_0" % t, R("js%d" % (t + 1)), R(sv))
        for c in range(NCH):
            msum(P(1, 2, 256 + c * LC), [(R(sv, c * LC, (c + 1) * LC), R("blk")), (R("jh", c * LC, (c + 1) * LC), R("b125"))])
        tt(R("jum"), hi, R("msk"), A.mult)
        o = P(1, 2, 0, 2 * NJ)
        mm([(u[2], u[0], u[1], True, True) for u in pick(o, "jum", NCH)])
        aff("ui", R("jui"), o, -1.0, 120.0)
        ts(R("juj"), R("jui"), 15, A.bitwise_and)
        tt(R("juk"), R("juj"), R("jvb"), A.add)
        aff("vl", R("jvl"), R("juk"))
        act(R("jeo"), ind(R("er"), R("jvl")), F.Copy)
        msum(lo, [(R("neg"), R(sv)), (R("i125"), R("jh")), (R("eye"), R("jeo"))])
        aff("eh", R("jeh"), lo, 0.5, 195.5)
        aff("ne", R("jnw"), R("jeh"), None, -192.0)
        if t < VI - 1:
            ts(R("jcl"), R("jeh"), 196.0, A.max, 203.0, A.min)
            aff("sg", R("jsg"), R("jeh"), 0.125, 167.0625)
            msum(hi, [(R("n16"), R("jeh")), (R("e16"), R("jcl")), (R("neg"), R("jsg"))])
            aff("ng", R("jng"), hi, None, 192.0)
        else:
            for c in range(NCH):
                cp(ind(R("er"), R("jvl", c * NJ, (c + 1) * NJ)), R("jnw", c * LC, (c + 1) * LC))

    def table(t, c, tab, new):
        PH[0] = "tab"
        if t < VI - 1 and JE:
            cp(ind(R(tab), R("jvl", c * NJ, (c + 1) * NJ)), R("j" + new, c * LC, (c + 1) * LC))
        elif t < VI - 1:
            cp(ind(R(tab), R("vl_%d" % c)), R("%s_%d" % (new, c)))

    def cand(t, c):
        def K(n, *a):
            return R("%s_%d" % (n, c), *a)
        PH[0] = "head%d" % c
        w = "w%d_%d" % (t, c)
        W_, S_, Q_ = R(w), R(w, 0, LC), R(w, LC, 2 * LC)
        ac = "ac%d_%d" % (t, c)
        scan(K("st"), R("r2"), K("ov"), A.max)
        ts(K("XL"), K("st"), 1.0, A.is_equal)
        o = P(c, 0)
        msum(o, [(K("XL"), R("eye"))])
        xs = K("xm", LC, 2 * LC) if WK else K("xs")
        tt(xs, S_, o, A.mult)
        if WK:
            ts(K("xm", 0, LC), o, R("kcol", 0, 1), A.mult)
            aff("X", K("X"), o)
            o = P(c, 1, LC, 2 * NJ)
            msum(o, [(R("eye"), R("xbase"))] + [(R("wk", 128 * r, 128 * r + 128), K("xm", r, 2 * LC, 16)) for r in range(16)])
        else:
            aff("X", K("X"), o)
            mm([(P(c, 1, LC), K("X"), R("blkk"), True, True), (P(c, 1, 2 * LC), K("xs"), R("blk"), True, True)])
            tt(K("xm"), P(c, 1, LC, 2 * LC), R("msk"), A.mult)
            o = P(c, 0, LC, 2 * NJ)
            msum(o, [(R("eye"), R("xbase"))] + pick(o, "xm_%d" % c, 2))
        aff("xl", K("xl"), o, None, 1024.0)
        sx, kap = P(c, 3, 2 * LC), P(c, 3, 3 * LC)
        msum(sx, [(R("blk"), xs)])
        aff("sx", K("sx"), sx, None, 2048.0)
        aff("kap", kap, sx, R("kap", 0, 1), R("kap", 4 + t, 5 + t))
        if QL:
            msum(sx, [(R("eye"), S_)])
        aff("zx", K("zx"), ind(R("zb%d" % c, 0, CA), K("xl", 0, NJ)))
        if YV:
            tt(K("nx"), ind(R("nt"), K("xl", NJ, 2 * NJ)), K("zx"), A.subtract)
            if ENG["w8"] == "a":
                act(K("w8"), K("nx"), F.Relu, None, -1.0)
            else:
                ts(K("w8"), K("nx"), -1.0, A.mult, 0.0, A.max)
            act(K("f1"), K("nx"), F.Sign, None, -1.0)
        else:
            act(K("nx"), ind(R("nt"), K("xl", NJ, 2 * NJ)), F.Copy)
            o = P(c, 1)
            msum(o, [(R("eye"), K("zx")), (R("neg"), K("nx"))])
            relu("w8", K("w8"), o)
            act(K("f1"), o, F.Sign)
        o = P(c, 0, 2 * LC)
        msum(o, [(R("mth"), K("X")), (R("nblk"), K("w8"))])
        if ENG["T"] == "a":
            act(K("T"), o, F.Sign)
        else:
            ts(K("T"), o, 0.0, A.is_gt, 2.0, A.mult)
        D = P(c, 3)
        msum(D, [(R("eye"), K("X")), (R("mt"), K("T"))])
        relu("D", D, D, R("m2c", 0, 1))
        tt(K("ds"), S_, D, A.mult)
        sda = sdp = P(c, 3, LC)
        msum(sda, [(R("blk"), K("ds"))])
        tt(K("pr"), sda, K("sx"), A.mult)
        if ENG["sh"] == "a":
            act(K("sh"), K("pr"), F.Copy, -31.0 / 64, 1.0 / 32)
        else:
            ts(K("sh"), K("pr"), 5, A.arith_shift_right)
        tt(K("sm"), K("sh"), kap, A.add)
        ts(K("ci"), K("sm"), 4095, A.bitwise_and)
        aff("c16", K("c16"), K("ci"))
        PH[0] = "net%d" % c

        def prod(n, wd, mask):
            tt(K(n, 0, LC), R(wd[0], wd[1], wd[1] + LC), mask, A.mult)
            tt(K(n, LC, 2 * LC), R(wd[0], wd[1] + LC, wd[1] + 2 * LC), mask, A.mult)

        def change(f):
            a0, a1 = f * LC, (f + 1) * LC
            old, reg = R(w, a0, a1), [P(c, 3 - f, q * LC) for q in range(4)]
            PH[0] = ("net%d", "why%d")[f] % c
            if f:
                msum(reg[2], [(R("eye"), old)])
            tt(K("a2", a0, a1), reg[2], K("keep"), A.mult)
            tt(K("m0", a0, a1), reg[2], K("k0"), A.mult)
            msum(reg[1], [(R("tri"), K("X"))])
            tt(K("a1", a0, a1), old, reg[1], A.mult)
            msum(reg[0], [(R("eye"), old), (R("shd"), K("a1", a0, a1))] + [(R("eye"), K("iqe"))] * f)
            terms = [(R("eye"), K("a2", a0, a1))]
            for s in range(4):
                cur = reg[3 - s % 2]
                if s == 3:
                    terms.append((R("i2048"), K("fm")) if f else (R("eye"), K("fi")))
                terms.append((R("sh%d" % (1 << s)), K("m%d" % s, a0, a1)))
                msum(cur, terms)
                if s < 3:
                    tt(K("m%d" % (s + 1), a0, a1), cur, K("k%d" % (s + 1)), A.mult)
                if (WB, WQ)[f] >> (s + 1) & 1:
                    aff("wb", K("wb%d" % s, a0, a1), cur)
                    terms = [(R("eye"), K("wb%d" % s, a0, a1))]
            return reg

        if QL:
            aff("cf", K("cf"), K("ci"), None, -2048.0)
            tt(K("ne"), Q_, sdp, A.not_equal)
            tt(K("keep"), K("ne"), D, A.is_gt)
            tt(K("iqe"), K("X"), sdp, A.mult)
            mm([(P(c, 1, LC), R("mr"), K("keep"), True, True), (P(c, 1, 2 * LC), R("tri"), K("keep"), True, True),
                (P(c, 1, 3 * LC), R("blk"), K("keep"), True, True)])
            relu("c0", K("c0"), P(c, 1, LC), R("m2c", 2, 3))
            aff("ci", K("cn"), P(c, 1, 2 * LC), -1.0, R("m2c", 1, 2))
            ts(K("fm"), P(c, 1, 3 * LC), R("kcol", 0, 1), A.is_le)
            ts(K("k0"), K("c0"), 1, A.bitwise_and)
            for s in range(1, 4):
                ts(K("k%d" % s), K("cn"), s, A.arith_shift_right, 1, A.bitwise_and)
            if FIP:
                act(P(c, 1, LC), K("ci"), F.Copy, -2048.0)
                tt(K("fi"), K("fm"), P(c, 1, LC), A.mult)
            else:
                tt(K("fi"), K("fm"), K("cf"), A.mult)
            regs = [change(0), change(1)]
            return score(t, c, [regs[0][2], regs[1][2]], [regs[0][0], regs[1][0]])
        wp = P(c, 2, 0, 2 * LC)
        aff("cf", K("cf"), K("ci"), None, -2048.0)
        msum(wp, [(R("eye"), W_)])
        tt(K("ne"), Q_, sdp, A.not_equal)
        tt(K("keep"), K("ne"), D, A.is_gt)
        tt(K("iqe"), K("X"), sdp, A.mult)
        mm([(P(c, 1, LC), R("mr"), K("keep"), True, True), (P(c, 1, 2 * LC), R("tri"), K("keep"), True, True),
            (P(c, 1, 3 * LC), R("blk"), K("keep"), True, True)])
        relu("c0", K("c0"), P(c, 1, LC), R("m2c", 2, 3))
        aff("ci", K("cn"), P(c, 1, 2 * LC), -1.0, R("m2c", 1, 2))
        ts(K("fm"), P(c, 1, 3 * LC), R("kcol", 0, 1), A.is_le)
        prod("a2", wp, K("keep"))
        ts(K("k0"), K("c0"), 1, A.bitwise_and)
        prod("m0", wp, K("k0"))
        for s in range(1, 4):
            ts(K("k%d" % s), K("cn"), s, A.arith_shift_right, 1, A.bitwise_and)
        PH[0] = "pre%d" % c
        msum(sda, [(R("tri"), K("X"))])
        tt(K("a1", 0, LC), S_, sda, A.mult)
        tt(K("a1", LC, 2 * LC), Q_, sda, A.mult)
        iw = P(c, 3, 0, 2 * LC)
        msum(iw, [(R("eye"), W_), (R("shd"), K("a1")), (R("eye"), K("iqe"), P(c, 3, LC))])
        PH[0] = "net%d" % c
        if FIP:
            act(P(c, 1, LC), K("ci"), F.Copy, -2048.0)
            tt(K("fi"), K("fm"), P(c, 1, LC), A.mult)
        else:
            tt(K("fi"), K("fm"), K("cf"), A.mult)
        terms = [(R("eye"), K("a2"))]
        for s in range(4):
            cur = (P(c, 2, 2 * LC, 2 * LC), P(c, 3, 2 * LC, 2 * LC), wp, P(c, 3, 2 * LC, 2 * LC))[s]
            move = (R("sh%d" % (1 << s)), K("m%d" % s))
            if s == 3:
                if WB == 1:
                    terms = [(R("eye"), K("wb")), terms[-1]]
                terms += [(R("eye"), K("fi"), P(c, 3, 2 * LC)), (R("i2048"), K("fm"), P(c, 3, 3 * LC))]
            terms.append(move)
            msum(cur, terms)
            if s < 3:
                prod("m%d" % (s + 1), cur, K("k%d" % (s + 1)))
            if s == 1 and WB == 1:
                aff("wb", K("wb"), cur)
            if WB > 1 and WB >> (s + 1) & 1:
                aff("wb", K("wb%d" % s), cur)
                terms = [(R("eye"), K("wb%d" % s))]
        if MP and t < VI - 1:
            act(K("a2"), iw, F.Copy)
            act(K("wb2"), cur, F.Copy)
        score(t, c, [P(c, 3, 2 * LC), P(c, 3, 3 * LC)], [P(c, 3), P(c, 3, LC)])

    def score(t, c, rw, iw):
        def K(n, *a):
            return R("%s_%d" % (n, c), *a)
        ac = "ac%d_%d" % (t, c)
        PH[0] = "score%d" % c
        hb, cg = "hb%d" % c, "cg%d" % c
        rr, V = P(c, 0), P(c, 1)
        msum(rr, [(R("n16"), K("nx")), (R("eye"), K("f1"))])
        mm([(V, R("barb", c * LC, (c + 1) * LC), R("cb"), True, False), (V, K("X"), R("blk32"), False, False),
            (V, K("f1"), R("hblk"), False, False)])
        ra, rv = [], []
        for p in range(NPC):
            l0, l1 = p * LC // NPC, (p + 1) * LC // NPC
            for (a0, a1) in cut(l0, l1, NC):
                if t < VI - 1:
                    ra.append(act(R(cg, 16 * a0, 16 * a1), ind(R("er"), K("c16", a0, a1)), F.Copy, -1.875, 0.25))
                else:
                    ra.append(act(R(cg, 16 * a0, 16 * a1), ind(R("gt"), K("c16", a0, a1)), F.Copy, None, -2.0))
            for m in range(16):
                rv.append(tt(R(hb, m * LC + l0, m * LC + l1), R(cg, 16 * l0 + m, 16 * l1, 16), P(c, 0, l0, l1 - l0), A.is_gt))
        chain(ra)
        chain(rv)
        mm([(P(c, 1, m, 128 - m, 16), R(hb, m * LC, (m + 1) * LC), R("blk", 0, 128, 16), False, m == 15) for m in range(16)])
        scan(K("fw"), R("r1"), V, A.max)
        scan(rev(K("mx")), R("r1"), rev(K("fw")), A.max)
        tt(K("M"), V, K("mx"), A.is_equal)
        if ENG["ins"] == "a":
            act(K("ins"), K("mx"), F.Sign, accum=R(ac, 1, 2) if t < VI - 1 else None)
        else:
            ts(K("ins"), K("mx"), 0.0, A.is_gt)
            if t < VI - 1:
                act(K("fw", 0, 8), K("mx", 0, LC, 16), F.Sign, accum=R(ac, 1, 2))
        o = P(c, 0, LC)
        msum(o, [(K("M"), R("eye"))])
        tt(K("mc"), o, K("cf"), A.mult)
        PH[0] = "fin%d" % c
        o = P(c, 1, LC)
        msum(o, [(K("ins"), R("eye"))])
        wo, wn = "wo%d_%d" % (t, c), "w%d_%d" % (t + 1, c)
        if MP and t < VI - 1:
            for f in range(2):
                tt(K("m1", f * LC, (f + 1) * LC), K("wb2", f * LC, (f + 1) * LC), o, A.mult)
                tt(K("m0", f * LC, (f + 1) * LC), K("a2", f * LC, (f + 1) * LC), o, A.mult)
            o = P(c, 0, 2 * LC)
            msum(o, [(R("blk"), K("mc"))])
            tt(K("iv"), K("X"), o, A.mult)
            fp = P(c, 2)
            msum(fp, [(R("eye"), K("wb2", 0, LC)), (R("neg"), K("m1", 0, LC)), (R("eye"), K("m0", 0, LC)), (R("eye"), K("iv"))])
            aff("off", R("oo%d_%d" % (t, c)), fp, None, 2048.0)
            remote("p%d_%d" % (t, c), R("of%d_%d" % (t + 1, c)), R("oo%d_%d" % (t, c)))
            msum(P(c, 2, LC), [(R("eye"), K("wb2", LC, 2 * LC)), (R("neg"), K("m1", LC, 2 * LC)), (R("eye"), K("m0", LC, 2 * LC))])
            aff("wo", R(wo, LC, 2 * LC), P(c, 2, LC))
            remote("q%d_%d" % (t, c), R(wn, LC, 2 * LC), R(wo, LC, 2 * LC))
            return
        aff("ret", K("ret"), o, -1.0, 1.0)
        aff("nret", K("nret"), o)
        o = P(c, 0, 2 * LC)
        msum(o, [(R("blk"), K("mc"))])
        for f in range(2):
            PH[0] = ("why%d" if f and QL and t < VI - 1 else "fin%d") % c
            tt(K("m1", f * LC, (f + 1) * LC), rw[f], K("ret"), A.mult)
            tt(K("m0", f * LC, (f + 1) * LC), iw[f], K("nret"), A.mult)
        PH[0] = "fin%d" % c
        tt(K("iv"), K("X"), o, A.mult)
        if QL and t < VI - 1:
            fp = P(c, 1, 2 * LC)
            msum(fp, [(R("eye"), K(nm, 0, LC)) for nm in ("m1", "m0", "iv")])
            aff("off", R("oo%d_%d" % (t, c)), fp, None, 2048.0)
            remote("p%d_%d" % (t, c), R("of%d_%d" % (t + 1, c)), R("oo%d_%d" % (t, c)))
            PH[0] = "why%d" % c
            msum(P(c, 2, LC), [(R("eye"), K(nm, LC, 2 * LC)) for nm in ("m1", "m0")])
            aff("wo", R(wo, LC, 2 * LC), P(c, 2, LC))
            remote("q%d_%d" % (t, c), R(wn, LC, 2 * LC), R(wo, LC, 2 * LC))
        elif SPLIT == 2 and t < VI - 1:
            fp = P(c, 1, 2 * LC)
            msum(fp, [(R("eye"), K(nm, 0, LC)) for nm in ("m1", "m0", "iv")])
            aff("off", R("oo%d_%d" % (t, c)), fp, None, 2048.0)
            remote("p%d_%d" % (t, c), R("of%d_%d" % (t + 1, c)), R("oo%d_%d" % (t, c)))
            msum(P(c, 1, 3 * LC), [(R("eye"), K(nm, LC, 2 * LC)) for nm in ("m1", "m0")])
            aff("wo", R(wo), P(c, 1, 2 * LC, 2 * LC))
            remote("q%d_%d" % (t, c), R(wn), R(wo))
        elif SPLIT or t == VI - 1:
            for h, tag, y in ((1, "q", "yw"), (0, "p", "ys")):
                a0, a1 = h * LC, (h + 1) * LC
                fp = P(c, 1, (2 + h) * LC)
                parts = [("m1", a0), ("m0", a0)] + ([] if h else [("iv", 0)])
                if t < VI - 1:
                    msum(fp, [(R("eye"), K(nm, b0, b0 + LC)) for nm, b0 in parts])
                    aff("wo", R(wo, a0, a1), fp)
                    remote("%s%d_%d" % (tag, t, c), R(wn, a0, a1), R(wo, a0, a1))
                    continue
                for g2 in range(2):
                    msum(P(c, 1, (2 + h) * LC + 64 * g2, 64), [(R("out%d%d" % (g2, u)), K(nm, b0 + 64 * u, b0 + 64 * u + 64))
                                                               for nm, b0 in parts for u in range(2)])
                yt = K("sx" if h else "ln")
                if h:
                    ts(K("ab"), fp, 2048.0, A.is_lt, 4097.0, A.mult)
                    tt(K("ab"), K("ab"), fp, A.add)
                    act(yt, K("ab"), F.Copy, -2049.0)
                else:
                    act(yt, fp, F.Copy, 2048.0)
                for c4 in range(4):
                    turn(R(y + "k", 4 * c + c4, 256, 8), R(yt[0], c4, LC, 4))
                if c == NCH - 1:
                    moved[0] = 0.3
                    dma("a" if h else "s", R(y), R(y + "k"))
        else:
            fp = P(c, 1, 2 * LC, 2 * LC)
            msum(fp, [(R("eye"), K("m1")), (R("eye"), K("m0")), (R("eye"), K("iv"), P(c, 1, 2 * LC))])
            aff("wo", R(wo), fp)
            remote("p%d_%d" % (t, c), R(wn), R(wo))

    def count(t):
        PH[0] = "count"
        o = P(0, 3, 3 * LC, 1)
        for c in range(NCH):
            ts(R("acb", c, c + 1), R("ac%d_%d" % (t, c), 1, 2), 1.0 / 16 if ENG["ins"] == "a" else 1.0, A.mult)
        msum(o, [(R("all1"), R("acb", q, q + 1)) for q in range(NCH)])
        cp(R("rci", 0, 1), o)
        ts(R("rci", 4, 5), R("rci", 0, 1), 1, A.bitwise_and)
        ts(R("thr", 0, 1), R("rci", 4, 5), -1.0, A.mult, -1.5, A.add)

    for t in range(VI):
        for c in range(NCH):
            run(t, c)
        if JE:
            end(t)
        for c in range(NCH):
            table(t, c, "gt", "ng")
        for c in range(NCH):
            cand(t, c)
        for c in range(NCH):
            table(t, c, "er", "nw")
        if t < VI - 1:
            count(t)
    moved[0] = 4.0
    for j in range(2):
        dma("s", R("ye", 2048 * j, 2048 * j + 2048), R("er", 2048 * j, 2048 * j + 2048))

    n = len(ops)
    tail = [0.0] * n

    def gap(i, j):
        if i in ops[j]["soft"]:
            return 0.0
        return ops[i]["lat"] + (HOP if ops[j]["q"] != ops[i]["q"] else SELF)
    succ = [[] for _ in range(n)]
    for i, o in enumerate(ops):
        for d in o["deps"]:
            succ[d].append(i)
    for i in range(n - 1, -1, -1):
        o = ops[i]
        m = LEAD if o["ph"] == "fin0" else 0.0
        m += o["lat"]
        for j in succ[i]:
            m = max(m, tail[j] + gap(i, j))
        tail[i] = m + o["cost"] + (SLACK if o["kind"] == "r" else 0.0)
    if not PLACED:
        PLACED.append(arrange(ops, tail, gap))
    start, span = PLACED[0]
    order = sorted(range(n), key=lambda i: (start[i], i))

    cnt = {"qv": 0, "qa": 0, "qt": 0, "qg": 0}
    known = {q: {} for q in "vatgs"}
    done = {}
    tot = {}

    def wait(q, sem, v):
        if known[q].get(sem, 0) < v:
            Q[q].wait_ge(T.sem[sem], v)
            known[q][sem] = v

    for i in order:
        o = ops[i]
        q = o["q"]
        if q == "x":
            done[i] = (o["sem"], o["inc"], {o["sem"]: o["inc"]})
            tot[o["sem"]] = o["inc"]
            continue
        for d in sorted(o["deps"] - o["soft"], reverse=True):
            sem, v, clk = done[d]
            if known[q].get(sem, 0) < v:
                wait(q, sem, v)
                for s2, v2 in clk.items():
                    if known[q].get(s2, 0) < v2:
                        known[q][s2] = v2
        for f in o["fns"]:
            r = f()
            if o["kind"] == "c":
                cnt[QS[q]] += 1
                r.then_inc(T.sem[QS[q]], 1)
            elif o["kind"] == "d":
                r.then_inc(T.sem[o["sem"]], 16)
        clk = dict(known[q])
        s, v = (QS[q], cnt[QS[q]]) if o["kind"] == "c" else (o["sem"], o["inc"])
        clk[s] = v
        done[i] = (s, v, clk)
        tot[s] = v
    for s, v in tot.items():
        wait("g", s, v)
